import numpy as np, ml_dtypes
CORES = [1,5,17,21,33,37,49,53]
N = 8
import mx_ref
BF = ml_dtypes.bfloat16
def cols(t, e):
    v = np.concatenate([t.reshape(128, -1, 4), np.zeros((128, 1, 4), BF)], axis=1)
    return np.ascontiguousarray(v[:, e]).reshape(128, -1)
def tile(rs):
    return np.stack(rs, axis=2).reshape(128, -1).astype(BF)
def pick(q, e):
    c = np.concatenate([q[0].reshape(128, -1, 4), np.zeros((128, 1, 4), np.uint8)], axis=1); s = np.concatenate([q[1], np.ones((16, 1), np.uint8)], axis=1)
    return (np.ascontiguousarray(c[:, e].reshape(128, -1)), np.ascontiguousarray(s[:, e]))
def join(*qs):
    return (np.concatenate([q[0] for q in qs], axis=1), np.concatenate([q[1] for q in qs], axis=1))
def put(q, e, v):
    c, s = q[0].reshape(128, -1, 4).copy(), q[1].copy(); c[:, e] = v[0].reshape(128, -1, 4); s[:, e] = v[1]
    return (c.reshape(128, -1), s)
def pk(c, s):
    return (np.ascontiguousarray(c), mx_ref.live(s))
def emit(q):
    return q[0], q[1]
def packed(v, rng):
    q = [mx_ref.quantize(np.ascontiguousarray(v[r])) for r in range(N)]
    return np.stack([a for a, b in q]), np.stack([mx_ref.plane(b, rng) for a, b in q])
def decode(q):
    o = []
    for b in range(4):
        e = np.zeros((128, 128, 4), np.float32); e[np.arange(128), np.arange(128), b] = 1
        o.append(mx_ref.matmul(mx_ref.quantize(e.reshape(128, 512).astype(BF)), q))
    return np.stack(o, axis=2).reshape(128, -1)
def f(rng, *shape):
    return mx_ref.flush((rng.standard_normal(shape, dtype=np.float32) * np.exp2(rng.integers(-2, 3, shape[:-1] + (1,)))).astype(BF))
def wide(rng, *shape, cols=0):
    v = rng.standard_normal(shape, dtype=np.float32) * np.exp2(rng.integers(-12, 13, shape)).astype(np.float32)
    if cols: v *= np.repeat(np.exp2(rng.integers(-cols, cols + 1, shape[:-2] + (1, shape[-1] // 4))) * (rng.random(shape[:-2] + (1, shape[-1] // 4)) > 0.0625), 4, axis=-1).astype(np.float32)
    return mx_ref.flush(v.astype(BF))
C, S, K, R = 256, 32, 4, 3
def home(j):
    return j % N * S + j // N
def choose(z):
    e = np.arange(C).reshape(S, N)
    return np.concatenate([e[np.argsort(-z[e[:, a]], kind="stable")[:K], a] for a in range(N)])
def big(v, k):
    v = v.astype(np.float32) * np.float32(k)
    v[np.abs(v) < np.float32(2.0 ** -16)] = 0
    return v.astype(BF)
def weights(rng, k, zero=0, still=slice(0)):
    w = big(f(rng, 128, 2048), k)
    w[:zero] = 0
    w = w.reshape(128, 4, 128, 4)
    w[:, :, still] = 0
    w = w.reshape(128, 2048)
    c, p = packed(np.stack([w] * N), rng)
    return {"wc": c, "ws": p}
def numbers_of(rng):
    return {"x": big(f(rng, N, 128, 4 * C), 1), "pr": big(f(rng, N, 128, 4 * S), 1), "pd": big(f(rng, N, 128, 4 * S), 1), "u": np.array(f(rng, N, 128, 512)), "v": np.array(f(rng, N, 128, 512))}
def signs(rng):
    g = np.stack([rng.permutation(N) % 2 * 2.0 - 1.0 for r in range(N)])
    return g[:, np.arange(C) % N].astype(np.float32)
def setup_inputs(rng):
    return {**numbers_of(rng), **weights(rng, 0.25)}
def setup_inputs_ties(rng):
    d = setup_inputs(rng)
    for r in range(N):
        k = np.stack([rng.permutation(S) % 3 for a in range(N)], axis=1).reshape(-1)
        d["x"][r] = cols(d["x"][r], np.where(k == 2, -1, k))
        for n in ("pr", "pd"): d[n][r] = cols(d[n][r], np.zeros(S, int))
    return d
def setup_inputs_near(rng):
    d = {**numbers_of(rng), **weights(rng, 0.25, 0, np.r_[0:16, 64:64 + 8 * R])}
    x = d["x"].reshape(N, 128, C, 4)
    d["u"][:, :, :4 * R] = 0
    d["v"][:, :, :4 * R] = 0
    for n, g in (("pr", -1), ("pd", 1)):
        p = d[n].reshape(N, 128, S, 4)
        p[:, 0, :, 0] = g
        d[n] = p.reshape(N, 128, 4 * S)
    x[:, :8] = 0
    x[:, 8, :, 0] = signs(rng).astype(BF)
    x[:, 64:64 + 8 * R] = 0
    for t in range(R):
        p = 64 + 8 * t
        d["v"][:, 0, 4 * t] = 1
        d["u"][:, 8, 4 * t] = 1
        d["u"][:, p:p + 2, 4 * t:4 * t + 4] = 1
        s = (np.arange(C) // N + t * (K + 1)) % S + K % 4
        v = (((s[:, None] >> np.arange(8)) & 1) * np.exp2(np.arange(8) - 23.0)).astype(np.float32).astype(BF)
        x[:, p] = v[None, :, :4]
        x[:, p + 1] = v[None, :, 4:]
    return {**d, "x": x.reshape(N, 128, 4 * C)}
def setup_inputs_huge(rng):
    d = numbers_of(rng)
    d["u"][:, :, :4 * R] = ((1.5 + 0.5 * rng.random((N, 128, 4 * R))) * 2.0 ** 29).astype(np.float32).astype(BF)
    g = signs(rng)
    top = (np.arange(C) // N // K)[None, :] == np.arange(N)[:, None]
    size = np.repeat(np.where(top == (g > 0), 1.5, 1.0625), 4, axis=1)[:, None, :]
    x = (size + 0.25 * rng.random((N, 128, 4 * C))) * np.repeat(np.where(g > 0, 2.0 ** 26, -2.0 ** 28), 4, axis=1)[:, None, :]
    return {**d, "x": x.astype(np.float32).astype(BF), "pr": big(d["pr"], 2.0 ** 22), "pd": big(d["pd"], 2.0 ** 22), "v": big(d["v"], 2.0 ** 25), **weights(rng, 2.0 ** -7)}
def setup_inputs_crowd(rng):
    d = {**numbers_of(rng), **weights(rng, 0.25, 64)}
    x = d["x"].reshape(N, 128, C, 4)
    d["u"][:, :, :4 * R] = 0
    d["u"][:, :8, :4 * R] = 1
    d["v"][:, :8, :4 * R] = 0
    for kind, lo, hi, n in (("pr", 0, S // 2, K // 2), ("pd", S // 2, S - 1, K - K // 2)):
        p = d[kind].reshape(N, 128, S, 4)
        for a in range(N):
            for i, s in enumerate(lo + rng.permutation(hi - lo)[:R * n]):
                v = rng.integers(4, 8, (56, 4)) * np.exp2(rng.integers(-2, 1, (56, 4))) * rng.choice([-1.0, 1.0], (56, 4))
                o = rng.permutation(N)
                for r in range(N):
                    j = s * N + a + (r if kind == "pd" else 0)
                    g = 1.0 if r == o[0] else -1.0 if r == o[1] else 2.0 ** -26
                    x[r, :8, j] = 256 * 2 ** (R - 1 - i // n)
                    x[r, 8:64, j] = (v * g).astype(np.float32).astype(BF)
                    x[r, 64:, j] = 0
                p[a, 8:64, s] = (v * 2.0 ** -25).astype(np.float32).astype(BF)
        d[kind] = p.reshape(N, 128, 4 * S)
    return {**d, "x": x.reshape(N, 128, 4 * C)}
def setup_inputs_spread(rng):
    d = setup_inputs(rng)
    d["x"] = big(wide(rng, N, 128, 4 * C, cols=6), 1)
    for n in ("pr", "pd"): d[n] = big(wide(rng, N, 128, 4 * S, cols=6), 1)
    return d
def check_inputs(d):
    b = []
    for k in ("x", "pr", "pd", "u", "v"):
        a = np.abs(d[k].astype(np.float32))
        if not (np.isfinite(a).all() and ((a == 0) | (a >= 2.0 ** -30) & (a <= 2.0 ** 30)).all()): b.append("a value of " + k)
    if (d["wc"] != d["wc"][:1]).any(): b.append("wc differs between ranks")
    s = [mx_ref.live(p) for p in d["ws"]]
    if any((p != s[0]).any() for p in s): b.append("ws differs between ranks")
    return b
def reference(x, pr, pd, u, v, wc, ws):
    w = pk(wc[0], ws[0])
    qu, qv = [mx_ref.quantize(u[r]) for r in range(N)], [mx_ref.quantize(v[r]) for r in range(N)]
    data = join(*[mx_ref.quantize(x[r]) for r in range(N)])
    par = join(*[mx_ref.quantize(pr[r]) for r in range(N)], *[mx_ref.quantize(pd[r]) for r in range(N)])
    mine = [C * r + np.arange(C) for r in range(N)]
    own = [np.concatenate([S * r + np.arange(S), C + S * r + np.arange(S)]) for r in range(N)]
    n = N * K
    for t in range(R):
        s = np.zeros(2 * C, np.float32)
        for r in range(N): s[own[r]] = mx_ref.matmul(qv[r], pick(par, own[r]))[t]
        took, rows, diags = [], [], []
        for r in range(N):
            j = np.arange(C)
            a = mx_ref.matmul(qu[r], pick(data, mine[r]))[t]
            z = (a - s[home(j)]) - s[C + home((j - r) % C)]
            e = choose(z + np.float32(0.0))
            took.append(C * r + e)
            rows.append(home(e))
            diags.append(C + home((e - r) % C))
        at = np.concatenate(took)
        old = pick(data, at)
        new = mx_ref.quantize(tile([np.maximum(mx_ref.matmul(pick(w, np.arange(128 * b, 128 * b + 128)), old), np.float32(0.0)) * np.float32(0.0625) for b in range(4)]))
        delta = decode(mx_ref.quantize((decode(new) - decode(old)).astype(BF))).reshape(128, -1, 4)
        p, anew = decode(par).reshape(128, -1, 4), np.zeros(2 * C, bool)
        for r in range(N):
            for h in (rows[r], diags[r]):
                p[:, h] = p[:, h] + delta[:, n * r:n * r + n]
                anew[h] = True
        e = np.flatnonzero(anew)
        par = put(par, e, pick(mx_ref.quantize(np.ascontiguousarray(p.reshape(128, -1).astype(BF))), e))
        data = put(data, at, new)
    y = np.zeros((N, 128, C + 2 * S), np.float32)
    oc, osc = np.zeros((N, 128, 4 * (C + 2 * S)), np.uint8), np.zeros((N, 16, C + 2 * S), np.uint8)
    for r in range(N):
        a, b = pick(data, mine[r]), pick(par, own[r])
        y[r] = np.concatenate([mx_ref.matmul(qu[r], a), mx_ref.matmul(qv[r], b)], axis=1)
        oc[r], osc[r] = emit(join(a, b))
    return {"y": y, "oc": oc, "osc": osc}

@@ -1,0 +1,726 @@
+from concourse.bass import DstId, RemoteDMATransfer
+from concourse.mybir import dt, AluOpType as A, ActivationFunctionType as F
+
+R = 3
+HALF = 4
+NHAND = 4
+TINY = 2.0 ** -110
+MID = 124
+OLD = 128
+LAP = 80
+FP8, U8, BF, F32, I32, U16 = "float8_e4m3fn_x4", "uint8", "bfloat16", "float32", "int32", "uint16"
+SCRATCH = {"ps": ("psum", [128, 4096], F32)}
+
+
+def _add(d, text, mx=False):
+    for item in text.split():
+        name, n = item.split(":")
+        if mx:
+            SCRATCH["c_" + name] = ("sbuf", [128, int(n)], FP8)
+            SCRATCH["z_" + name] = ("sbuf", [128, int(n)], U8)
+        else:
+            SCRATCH[name] = ("sbuf", [128, int(n)], d)
+
+
+_add(BF, "XB:1024 PT:512 UB:512 VB:512 ONE:520 EB:520 NB:520 ZB:512 HT0:1024 DT0:1024 HT1:512 DT1:512 NT:512 "
+         "INV0:256 INV1:256 INV2:256 INVT:256 VALS:32 KX0:64 KX1:64 KX2:64 WK0:32 WK1:32 WK2:32 KW:354 CT:848 "
+         "GG:192 HH:320 HHT:320 SH:320 MS:128")
+_add(FP8, "X:256 U:128 V:128 W:512 E:1024 D0:384 D1:384 D2:384 D3:256 FD:256 NX:416 DL:416 PB0:256 PB1:256 PB2:256 "
+          "PB3:256 DC0:32 DC1:32 DC2:32 SN0:64 SN1:64 SN2:64 LA0:144 LA1:144 LA2:144 AR:128", mx=True)
+_add(FP8, "c_HC0:32 c_HC1:32 c_HC2:32")
+_add(U8, "z_HZ0:32 z_HZ1:32 z_HZ2:32")
+_add(F32, "N0:16 N1:16 N2:16 SC0:1 SC1:1 SC2:1 FC:64 MAP:64 LM:64 SM:512 TMPF:320 "
+          "ACOL:8 RA:64 RB:128 TB:128 ST:64 RR:64 G1:64 G2:64 CC:64 XR:8 RG:64 RT:64 MM:64 SCN:128 DMP:64 DF:64 "
+          "DK:32 YB:320 UP:128")
+_add(I32, "PI:1 INTC:16 TMPI:256")
+ALIAS = {}
+for _buf, _text in (("SM", "OWN:0 C1:16 WD:32 WE:48 SQ:64 ALF:68 SX:72 SEG:96 MT:160 IOI:248 KTB:312 K4:376 OFR:440"),
+                    ("CT", "TBL:0 WT:144 MASK:272 SEGG:336 SEGH:528"),
+                    ("KW", "RGK:0 MK:32 SK:64 KB:96 KT:128 CN:160 VPB:352 VDB:353"),
+                    ("LW", "DLS:0 SEL:16 AL:32 L1U:40 L2U:42")):
+    for _item in _text.split(" "):
+        ALIAS[_item.split(":")[0]] = (_buf, int(_item.split(":")[1]))
+LISTS = {"nat": 0, "out": 16, "bl": 32, "sh": 40, "rg": 44, "ac": 48, "w2": 52, "r2": 54, "sn": 56, "ow": 60, "se": 62, "sl": 64, "pp": 66}
+_add(U16, "LST:70 LW:44")
+TILES = ("NT", "HT0", "HT1", "DT0", "DT1")
+SEMAPHORES = (["qg", "qv", "qs", "qt", "snt"] + [s + str(t) for s in ("sc", "dl", "ls", "hs") for t in range(R)]
+              + ["m%d" % i for i in range(48)])
+
+
+def pos(s, d):
+    return s if s < d else s - 1
+
+
+def bits(e):
+    return sum(1 << x for x in e)
+
+
+def _far(s, cores, topo):
+    return [o for o in range(len(cores)) if o != s and topo.chip(cores[s]) != topo.chip(cores[o])]
+
+
+def _near(src, dst, away, topo):
+    return [x for x in topo.engines(src, dst) if x not in away]
+
+
+def _helpers(s, cores, topo):
+    return [c for c in topo.cores_of(cores[s]) if topo.die(c) == topo.die(cores[s]) and c not in cores][:3]
+
+
+def _half(h, s):
+    return [o for o in range(HALF * h, HALF * h + HALF) if o != s]
+
+
+def _calls(s, cores, topo):
+    fs = _far(s, cores, topo)
+    n = len(topo.engines(cores[s], cores[fs[0]])) // 2
+    return [[o for o in range(len(cores)) if o != s and o not in fs[n:]], fs[n:]]
+
+
+def _mask(s, d, dests, src, cores, topo):
+    fs = _far(s, cores, topo)
+    away = topo.engines(src, cores[fs[0]])
+    if d not in fs:
+        return _near(src, cores[d], away, topo)[:2]
+    fs = [o for o in dests if o in fs]
+    n = 2 if len(fs) > 2 else 4
+    i = n * fs.index(d)
+    return away[i:i + n]
+
+
+def _list_mask(s, d, cores, topo):
+    dests = [c for c in _calls(s, cores, topo) if d in c][0]
+    return _mask(s, d, dests, cores[s], cores, topo)
+
+
+def _hand_mask(s, d, src, cores, topo):
+    return _mask(s, d, _half(d // HALF, s), src, cores, topo)[:2]
+
+
+def _to(core, topo):
+    rid, pid = topo.addr(core)[:2]
+    return DstId(rid=rid, pnc=pid)
+
+
+def hand_on(g, core, s, cores, T, topo):
+    k = _helpers(s, cores, topo).index(core)
+    h = k if k < 2 else 1 - s // HALF
+    dests = _half(h, s)
+    for t in range(R):
+        g.wait_ge(T.sem["hs%d" % t], NHAND if k < 2 else 2 * NHAND)
+        tf = []
+        for o in dests:
+            p, i = pos(s, o), o - HALF * h
+            if k < 2:
+                src = T["c_HC%d" % t][:, 8 * i:8 * i + 8].bitcast(dt.uint8)
+                land = T["c_LA%d" % t][:, 16 + 8 * p:24 + 8 * p].bitcast(dt.uint8)
+            else:
+                src, land = T["z_HZ%d" % t][:, 8 * i:8 * i + 8], T["z_LA%d" % t][:, 16 + 8 * p:24 + 8 * p]
+            tf.append(RemoteDMATransfer(dst_ids=[_to(cores[o], topo)], dma_engine_mask=bits(_hand_mask(s, o, core, cores, topo)),
+                                        remote_sem=T.sem["dl%d" % t], srcs=[src], dsts=[land]))
+        g.remote_dma_fused(tf, local_sem=T.sem.snt)
+    g.wait_ge(T.sem.snt, 2 * len(dests) * R)
+
+
+def rank_program(g, core, T, topo):
+    cores = [int(c) for c in T.cores]
+    n_ranks = len(cores)
+    me = T.rank_of(core)
+    if me is None:
+        for s in range(n_ranks):
+            if core in _helpers(s, cores, topo):
+                hand_on(g, core, s, cores, T, topo)
+        return
+    r = me
+    Q = {"g": g, "v": g.vector, "s": g.scalar, "t": g.tensor, "y": g.sync}
+    csem = {"g": "qg", "v": "qv", "s": "qs", "t": "qt"}
+    total, known, hist = {}, {q: {} for q in Q}, {}
+    ndma = [0]
+
+    def w(name, c0, c1, step=1, p0=0, p1=128):
+        if name in ALIAS:
+            name, c0, c1 = ALIAS[name][0], c0 + ALIAS[name][1], c1 + ALIAS[name][1]
+        t = T[name]
+        if p0 == 0 and p1 == 128:
+            a = t[:, c0:c1] if step == 1 else t[:, c0:c1:step]
+        else:
+            a = t[p0:p1, c0:c1] if step == 1 else t[p0:p1, c0:c1:step]
+        if step == 4 and name in TILES:
+            b = c0 % 4
+            return (a, [(name, c0 - b, c1, 32 * b, 32 * b + 32)])
+        return (a, [(name, c0, c1, p0, p1)])
+
+    def ind(v, o):
+        return (v[0].indirect(o[0]), v[1] + o[1])
+
+    def lst(name, n, off=0):
+        a = LISTS[name] + off
+        return w("LST", a, a + n)
+
+    def norm(reg):
+        name, c0, c1, p0, p1 = reg
+        if name == "ps":
+            return (name, c0 // 512 * 512, (c1 + 511) // 512 * 512, 0, 128)
+        return reg
+
+    def waits(q, reads, writes):
+        need = {}
+        def want(h):
+            sem, n, clock = h[7], h[8], h[9]
+            if known[q].get(sem, 0) >= n:
+                return
+            if sem not in need or need[sem][0] < n:
+                need[sem] = (n, clock)
+        for reg in reads:
+            name, c0, c1, p0, p1 = norm(reg)
+            for h in hist.get(name, ()):
+                if h[0] < c1 and c0 < h[1] and h[2] < p1 and p0 < h[3] and (h[4] or (name == "ps" and h[5] != q)):
+                    want(h)
+        for reg in writes:
+            name, c0, c1, p0, p1 = norm(reg)
+            for h in hist.get(name, ()):
+                if h[0] < c1 and c0 < h[1] and h[2] < p1 and p0 < h[3]:
+                    if name == "ps" and h[5] == q:
+                        continue
+                    want(h)
+        for sem in sorted(need):
+            n, clock = need[sem]
+            if any(s2 != sem and c2.get(sem, 0) >= n for s2, (n2, c2) in need.items()):
+                continue
+            Q[q].wait_ge(T.sem[sem], n)
+        for sem in need:
+            n, clock = need[sem]
+            for k, v in clock.items():
+                if known[q].get(k, 0) < v:
+                    known[q][k] = v
+            known[q][sem] = max(known[q].get(sem, 0), n)
+
+    def record(q, reads, writes, sem, n, clock, dma):
+        for reg in writes:
+            reg = norm(reg)
+            name, c0, c1, p0, p1 = reg
+            hs = [h for h in hist.get(name, ()) if not (c0 <= h[0] and h[1] <= c1 and p0 <= h[2] and h[3] <= p1)]
+            hs.append((c0, c1, p0, p1, True, q, dma, sem, n, clock))
+            hist[name] = hs
+        for reg in reads:
+            reg = norm(reg)
+            name, c0, c1, p0, p1 = reg
+            hs = [h for h in hist.get(name, ()) if not (not h[4] and not dma and not h[6] and h[5] == q and (c0, c1, p0, p1) == tuple(h[:4]))]
+            hs.append((c0, c1, p0, p1, False, q, dma, sem, n, clock))
+            hist[name] = hs
+
+    def run(q, call, reads, writes, dma=False):
+        rr = [x for v in reads for x in v[1]]
+        ww = [x for v in writes for x in v[1]]
+        waits(q, rr, ww)
+        if dma:
+            sem, inc = "m%d" % ndma[0], 16
+            ndma[0] += 1
+        else:
+            sem, inc = csem[q], 1
+        total[sem] = total.get(sem, 0) + inc
+        call().then_inc(T.sem[sem], inc)
+        clock = dict(known[q])
+        clock[sem] = total[sem]
+        record(q, rr, ww, sem, total[sem], clock, dma)
+
+    def arrive(views, sem, n):
+        total[sem] = n
+        record("x", [], [x for v in views for x in v[1]], sem, n, {sem: n}, True)
+
+    def S(x):
+        return x[0] if isinstance(x, tuple) else x
+
+    def deps(*xs):
+        return [x for x in xs if isinstance(x, tuple)]
+
+    def cp(q, out, a):
+        if q == "v":
+            run("v", lambda: g.vector.tensor_copy(out[0], a[0]), [a], [out])
+        else:
+            run("s", lambda: g.scalar.activation(out[0], a[0], F.Copy), [a], [out])
+
+    def sa(out, a, scale=1.0, bias=0.0):
+        run("s", lambda: g.scalar.activation(out[0], a[0], F.Identity, bias=S(bias), scale=S(scale)), [a] + deps(scale, bias), [out])
+
+    def tt(out, a, b, op):
+        run("v", lambda: g.vector.tensor_tensor(out[0], a[0], b[0], op), [a, b], [out])
+
+    def ts(out, a, s1, op0, s2=None, op1=None):
+        if op1 is None:
+            run("v", lambda: g.vector.tensor_scalar(out[0], a[0], S(s1), None, op0), [a] + deps(s1), [out])
+        else:
+            run("v", lambda: g.vector.tensor_scalar(out[0], a[0], S(s1), S(s2), op0, op1), [a] + deps(s1, s2), [out])
+
+    def tr(out, a):
+        run("v", lambda: g.vector.transpose(out[0], a[0]), [a], [out])
+
+    def scan(out, a, b):
+        run("v", lambda: g.vector.tensor_tensor_scan(out[0], a[0], b[0], 0.0, A.mult, A.add), [a, b], [out])
+
+    def fill(out, c):
+        run("v", lambda: g.vector.memset(out[0], c), [], [out])
+
+    def iota(out, pattern, base=0, ch=0, small=True):
+        if small:
+            run("g", lambda: g.iota(out[0], pattern, base, ch, allow_small_or_imprecise_dtypes=True), [], [out])
+        else:
+            run("g", lambda: g.iota(out[0], pattern, base, ch), [], [out])
+
+    def quant(name, c0, src):
+        n = (src[1][0][2] - src[1][0][1]) // 4
+        c, z = w("c_" + name, c0, c0 + n), w("z_" + name, c0, c0 + n)
+        run("v", lambda: g.vector.quantize_mx(c[0], z[0], src[0]), [src], [c, z])
+
+    def pick(dst, d0, n, src, width, off, a0=0):
+        b, k = off
+        o = w(b, k, k + n // 16)
+        co, ci = w("c_" + dst, d0, d0 + n), w("c_" + src, a0, a0 + width)
+        run("v", lambda: g.vector.tensor_copy(co[0].bitcast(dt.uint32), ci[0].bitcast(dt.uint32).indirect(o[0])), [ci, o], [co])
+        zo, zi = w("z_" + dst, d0, d0 + n), w("z_" + src, a0, a0 + width)
+        run("s", lambda: g.scalar.activation(zo[0], zi[0].indirect(o[0]), F.Copy), [zi, o], [zo])
+
+    def mm(bank, n, lhs, l0, rhs, r0, start=True, stop=True):
+        out = w("ps", 512 * bank, 512 * bank + n)
+        a, az = w("c_" + lhs, l0, l0 + 128), w("z_" + lhs, l0, l0 + 128)
+        b, bz = w("c_" + rhs, r0, r0 + n), w("z_" + rhs, r0, r0 + n)
+        run("t", lambda: g.tensor.matmul_mx(out[0], a[0], az[0], b[0], bz[0], start, stop), [a, az, b, bz], [out])
+
+    def bank(b, n, c0=0):
+        return w("ps", 512 * b + c0, 512 * b + c0 + n)
+
+    def load(q, out, a):
+        run(q, lambda: Q[q].dma_start(out[0], a), [], [out], dma=True)
+
+    def store(q, a, src):
+        run(q, lambda: Q[q].dma_start(a, src[0]), [src], [], dma=True)
+
+    others = [o for o in range(n_ranks) if o != me]
+    afar = _far(me, cores, topo)
+    away = topo.engines(core, cores[afar[0]])
+    helpers = _helpers(me, cores, topo)
+    mine = _half(me // HALF, me)
+
+    def fused(reads, transfers):
+        waits("g", [x for v in reads for x in v[1]], [])
+        g.remote_dma_fused([RemoteDMATransfer(dst_ids=[_to(c, topo) for c in ds], dma_engine_mask=bits(e), remote_sem=sem, srcs=[src], dsts=[land] * len(ds))
+                            for ds, e, sem, src, land in transfers], local_sem=T.sem.snt)
+        total["snt"] = total.get("snt", 0) + sum(len(x[1]) for x in transfers)
+
+    def send_scores(t):
+        src, land, sem = w("SC%d" % t, 0, 1), T["N%d" % t][:, me:me + 1], T.sem["sc%d" % t]
+        fused([src], [([cores[o] for o in afar], away, sem, src[0], land)]
+              + [([cores[o]], _near(core, cores[o], away, topo)[:2], sem, src[0], land) for o in others if o not in afar])
+
+    def score_count():
+        return sum(len(away) if s in afar else 2 for s in others)
+
+    def delta_count(s):
+        direct = s // HALF == me // HALF
+        scales = _mask(s, me, _half(s // HALF, s), cores[s], cores, topo) if direct else _hand_mask(s, me, _helpers(s, cores, topo)[2], cores, topo)
+        codes = _hand_mask(s, me, _helpers(s, cores, topo)[me // HALF], cores, topo)
+        return len(codes) + len(scales)
+
+    QB = me % 4
+    DB = QB + 1 if QB < 3 else 2
+    CLASH = r % 4 == 0
+
+    load("s", w("VB", 0, 512), T.v[:, :])
+    for b in range(4):
+        load("ys"[b % 2], w("PT", 128 * b, 128 * b + 128), (T.pr if b == QB else T.pd)[:, :])
+    load("y", w("XB", 0, 1024), T.x[:, :])
+    load("s", w("UB", 0, 512), T.u[:, :])
+    cw = w("c_W", 0, 512)
+    load("y", (cw[0].bitcast(dt.uint8), cw[1]), T.wc[:, :])
+    load("s", w("z_W", 0, 512), T.ws[:, :])
+
+    TMP = [0]
+    def ftmp(n):
+        a = TMP[0]
+        TMP[0] += n
+        return w("TMPF", a, a + n)
+    kt, ioi, mp = w("KTB", 0, 64), w("IOI", 0, 64), w("MAP", 0, 64)
+    fnat, fbl, frg, fsh, fsn, fout, fr2, fc1, f1, fa, fb, fh, fkp, ktf, fm = [ftmp(n) for n in (16, 4, 4, 4, 4, 16, 2, 16, 64, 2, 2, 2, 32, 32, 64)]
+    iota(w("PI", 0, 1), [[0, 1]], 0, 1, small=False)
+    fill(w("ONE", 0, 520), 1.0)
+    sa(w("ZB", 0, 512), w("ONE", 0, 512), 0.0)
+    sa(w("HT1", 128, 512), w("ONE", 0, 384), 0.0)
+    sa(w("DT1", 128, 512), w("ONE", 0, 384), 0.0)
+
+    def col(j):
+        return w("FC", j, j + 1)
+    P16, P31, KK, QQ, B2, B3, Q0, Q1, M, ODD, B0, B1, K1, P8, K2 = range(15)
+    for j, (sh, an) in enumerate(((0, 15), (0, 31), (2, 3), (5, 3), (2, 1), (3, 1), (5, 1), (6, 1), (0, 3), (4, 1), (0, 1), (1, 1), (1, 7), (0, 7), (2, 7))):
+        o, i = w("INTC", j, j + 1), w("PI", 0, 1)
+        if sh:
+            ts(o, i, sh, A.arith_shift_right, an, A.bitwise_and)
+        else:
+            ts(o, i, an, A.bitwise_and)
+    C8P, CX, CSN, C16, CW2, CNX, CND, C32K, COUT, KR, SHF, PC, PC3, VP, VD, OP, C1P, MK1, SU, Y0, Y2 = range(16, 37)
+    fill(w("SEG", 0, 64), 1.0)
+    cp("v", w("FC", 0, 15), w("INTC", 0, 15))
+    fill(w("SEG", 32, 33), 0.0)
+    for h in range(2):
+        fill(lst("ac", 2, 2 * h), h)
+    eb, one = w("EB", 0, 520), w("ONE", 0, 520)
+    run("g", lambda: g.affine_select(eb[0], one[0], [[-1, 520]], A.is_equal, 0.0, 4, 4), [one], [eb])
+    iota(fnat, [[1, 8], [128, 2]])
+    iota(fbl, [[4, 2], [0, 2]])
+    iota(fsh, [[0, 2], [16, 2]])
+
+    quant("V", 0, w("VB", 0, 512))
+    quant("PB0", OLD, w("PT", 0, 512))
+
+    def scores(t):
+        sc, n = "SC%d" % t, "N%d" % t
+        mm(0, 128, "PB%d" % t, OLD, "V", 0)
+        cp("s", w(sc, 0, 1), w("ps", t, t + 1))
+        send_scores(t)
+        run("y", lambda: g.sync.dma_start(T[n][:, me:me + 1], T[sc][:, 0:1]), [w(sc, 0, 1)], [w(n, me, me + 1)], dma=True)
+        arrive([w(n, a, b) for a, b in ((0, me), (me + 1, 8)) if b > a], "sc%d" % t, score_count())
+
+    scores(0)
+    iota(frg, [[1, 2], [0, 2]])
+    iota(fsn, [[2, 4]])
+    iota(ioi, [[0, 2], [1, 32]])
+    iota(w("MT", 0, 64), [[0, 16], [1, 4]])
+    iota(fr2, [[4, 2]])
+    iota(mp, [[128, 2], [1, 32]])
+    iota(kt, [[4, 2], [0, 32]])
+    iota(w("VALS", 0, 32), [[0, 8], [1, 4]])
+    own16, c1, sq = w("OWN", 0, 16), w("C1", 0, 16), w("SQ", 0, 4)
+    iota(own16, [[16, 16]])
+    iota(sq, [[16, 4]])
+    iota(fc1, [[4, 8], [0, 2]])
+    iota(fkp, [[8, 32]], -MID)
+    iota(fm, [[16, 2], [0, 2], [1, 16]])
+    iota(w("WT", 0, 128), [[16, 4], [0, 2], [1, 16]])
+    iota(fout, [[2, 16]])
+
+    ts(col(C8P), col(P16), 8.0, A.mult)
+    tt(col(CNX), col(B2), col(Q0), A.not_equal)
+    tt(col(CND), col(B3), col(Q1), A.not_equal)
+    ts(lst("nat", 16), fnat, col(C8P), A.add)
+    sa(w("NB", 0, 520), eb, -1.0)
+    quant("X", 0, w("XB", 0, 1024))
+    pick("D0", 0, 256, "X", 256, ("LST", LISTS["nat"]))
+    quant("U", 0, w("UB", 0, 512))
+    for b in range(2):
+        mm(b, 256, "W", 128 * b, "D0", 0)
+    for h in range(2):
+        mm(4 + h, 128, "D0", 128 * h, "U", 0)
+    for b in range(2, 4):
+        mm(b, 256, "W", 128 * b, "D0", 0)
+    for b in range(4):
+        quant("E", 512 + 128 * b, w("NB", 4 - b, 516 - b))
+
+    def relu(tile, b, cols, bk):
+        o, i = w(tile, b, 4 * cols, 4), bank(bk, cols)
+        run("s", lambda: g.scalar.activation(o[0], i[0], F.Relu, scale=0.0625), [i], [o])
+
+    relu("HT0", 0, 256, 0)
+    relu("HT0", 1, 256, 1)
+    cp("s", w("ACOL", 0, 2), w("ps", 2048, 3072, 512))
+    relu("HT0", 2, 256, 2)
+    relu("HT0", 3, 256, 3)
+    sa(col(C32K), col(KK), 32.0)
+    sa(col(C16), col(ODD), 16.0)
+    sa(kt, kt, 1.0, col(KK))
+    sa(mp, mp, 1.0, col(C32K))
+    sa(w("DMP", 0, 64), mp, 0.0, -1.0)
+    sa(f1, kt, 32.0)
+    cp("s", w("DMP", 31, 64, 32), w("MAP", 31, 64, 32))
+    for b in range(4):
+        mm(4 + b, 256, "E", 512 + 128 * b, "D0", 0, True, False)
+    bi, shi, sni = w("TMPI", 12, 16), w("TMPI", 0, 4), w("TMPI", 4, 8)
+    t0, b0, b1, hh = [w("TMPI", a, a + 2) for a in (144, 146, 148, 150)]
+    kti, k0 = w("TMPI", 80, 112), ktf[1][0][1]
+    ts(col(KR), col(Q1), float(r), A.mult, col(KK), A.add)
+    ts(bi, fbl, col(QQ), A.add, float(8 - r), A.add)
+    ts(shi, fsh, col(P16), A.add)
+    ts(t0, fr2, col(KR), A.add)
+    ts(col(CX), col(CND), 2.0, A.mult, col(CNX), A.add)
+    ts(col(CSN), col(B2), float(r), A.mult, col(B3), A.add)
+    ts(bi, bi, 7, A.bitwise_and)
+    for h in range(2):
+        n = min(max(r - 4 * h, 0), 4)
+        if n:
+            v = w("TMPI", 2 * h, 2 * h + 2, 1, 0, 32 * n)
+            ts(v, v, 31.0, A.add)
+    ts(t0, t0, 7, A.bitwise_and)
+    ts(col(CX), col(CX), 2.0, A.mult)
+    ts(sni, fsn, col(CSN), A.add)
+    ts(lst("bl", 4, 4), bi, 8.0 if CLASH else 0.0, A.add)
+    ts(shi, shi, 31, A.bitwise_and)
+    ts(b0, t0, 1, A.bitwise_and)
+    ts(lst("rg", 4), frg, col(CX), A.add)
+    ts(sni, sni, 7, A.bitwise_and)
+    cp("v", lst("sh", 2), w("TMPI", 0, 2))
+    ts(lst("sh", 2, 2), w("TMPI", 2, 4), 32.0, A.add)
+    ts(lst("bl", 4), fbl, col(QQ), A.add)
+    ts(lst("sn", 4), sni, 4.0, A.mult, col(M), A.add)
+    ts(w("LM", 0, 64), ioi, col(P31), A.is_lt, TINY, A.mult)
+    for b in range(4):
+        quant("E", 128 * b, w("EB", 4 - b, 516 - b))
+
+    def arow():
+        cp("v", w("RA", 0, 64), ind(w("ACOL", 0, 2), lst("ac", 4)))
+
+    arow()
+    quant("NX", 0, w("HT0", 0, 1024))
+    for b in range(4):
+        mm(4 + b, 256, "E", 128 * b, "NX", 0, False, True)
+    for b in range(4):
+        cp("s", w("DT0", b, 1024, 4), bank(4 + b, 256))
+
+    def differences(name, c, src):
+        tt(w(name, c, c + 63), w(src, 0, 63), w(src, 1, 64), A.subtract)
+        cp("s", w(name, c + 31, c + 64, 32), w(src, 31, 64, 32))
+
+    x1 = w("TMPI", 16, 80)
+    gaps = [
+        lambda: ts(col(SHF), col(K2), float(8 - r), A.is_ge, 31.0, A.mult),
+        lambda: ts(b1, t0, 1, A.arith_shift_right, 1, A.bitwise_and),
+        lambda: ts(col(SHF), col(SHF), col(Q1), A.mult),
+        lambda: ts(fa, b0, col(Q0), A.not_equal, 2.0, A.mult),
+        lambda: ts(kti, w("IOI", 0, 32), col(SHF), A.add),
+        lambda: ts(fb, b1, col(Q1), A.not_equal, 4.0, A.mult),
+        lambda: ts(hh, t0, 2, A.arith_shift_right, 1, A.bitwise_and),
+        lambda: ts(kti, kti, 31, A.bitwise_and),
+        lambda: tt(fa, fa, fb, A.add),
+        lambda: ts(fh, hh, 1.0, A.mult),
+        lambda: ts(ktf, kti, 8.0, A.mult, float(r - MID), A.add),
+        lambda: ts(x1, ioi, col(C16), A.add),
+        lambda: tt(fa, fa, fh, A.add),
+        lambda: tt(w("DK", 0, 31), w("TMPF", k0, k0 + 31), w("TMPF", k0 + 1, k0 + 32), A.subtract),
+        lambda: cp("v", w("DK", 31, 32), w("TMPF", k0 + 31, k0 + 32)),
+        lambda: cp("v", lst("r2", 2), fa)]
+    after = [
+        lambda: ts(x1, x1, 31, A.bitwise_and),
+        lambda: tt(col(CNX), col(B0), col(ODD), A.not_equal),
+        lambda: ts(sq, sq, col(P16), A.add, 32.0 * QB, A.add),
+        lambda: tt(w("OFR", 0, 64), f1, x1, A.add),
+        lambda: ts(col(CW2), col(CNX), 16.0, A.mult),
+        lambda: ts(col(Y0), col(B2), 4.0 * ((2 * r) % 8 - r), A.mult, col(M), A.add),
+        lambda: differences("DF", 0, "OFR"),
+        lambda: ts(lst("w2", 1), col(K1), 32.0, A.mult, col(CW2), A.add),
+        lambda: ts(w("SQ", 2, 4), w("SQ", 2, 4), 32.0 * (DB - QB - 1) if DB < QB else 0.0, A.add),
+        lambda: ts(lst("ow", 1), col(Y0), 4.0 * r, A.add),
+        lambda: ts(own16, own16, col(P16), A.add),
+        lambda: quant("D0", 256, w("ZB", 0, 512)),
+        lambda: cp("v", lst("pp", 4), sq),
+        lambda: tt(c1, fc1, own16, A.subtract)]
+    owner = [
+        lambda: ts(col(VP), col(Q1), 32.0, A.mult, float(LAP), A.add),
+        lambda: ts(col(VD), col(K2), 7.0, A.is_equal, -72.0, A.mult),
+        lambda: ts(c1, c1, 256.0, A.add),
+        lambda: ts(col(SU), col(K2), 8.0, A.mult, 16.0, A.add),
+        lambda: ts(col(OP), col(Q1), 32.0 * (DB - QB), A.mult, OLD + 32.0 * QB, A.add),
+        lambda: tt(w("VPB", 0, 1), col(VP), col(P31), A.add),
+        lambda: tt(col(VD), col(VD), col(M), A.add),
+        lambda: ts(col(C1P), col(Q1), 64.0, A.mult, -1.0, A.add),
+        lambda: tt(col(OP), col(OP), col(P31), A.add),
+        lambda: tt(col(VD), col(VD), col(SU), A.add),
+        lambda: ts(col(SU), col(Q1), 4.0, A.mult),
+        lambda: ts(col(PC), col(P31), 8.0, A.mult, -MID - 0.5, A.add),
+        lambda: tt(col(C1P), col(C1P), col(OP), A.subtract),
+        lambda: tt(w("VDB", 0, 1), col(VD), col(SU), A.add),
+        lambda: ts(col(PC3), col(P31), 8.0, A.mult, 7.5 - MID, A.add),
+        lambda: fill(w("TBL", 0, LAP), 1.0),
+        lambda: fill(w("TBL", LAP, 144), 0.0),
+        lambda: ts(w("MASK", 0, 64), fm, col(P31), A.is_equal),
+        lambda: ts(col(Y2), col(K1), float(QB), A.is_equal, -2.0, A.mult),
+        lambda: cp("v", lst("sl", 1), col(M)),
+        lambda: pick("LA0", LAP, 64, "PB0", 128, ("LST", LISTS["pp"]), OLD),
+        lambda: ts(lst("se", 1), col(Y2), col(B0), A.add, 2.0, A.add)]
+
+    def gap(n=1):
+        for i in range(n):
+            if gaps:
+                gaps.pop(0)()
+
+    def choose(t):
+        n = "N%d" % t
+        if CLASH:
+            for h, q in enumerate("vs" if t else "vv"):
+                cp(q, w(n, 8, 16, 1, 64 * h, 64 * h + 64), w(n, 0, 8, 1, 64 - 64 * h, 128 - 64 * h))
+        rb, tb = w("RB", 0, 128), w("TB", 0, 128)
+        tt(w("RB", 0, 64), ind(w(n, 0, 8), lst("bl", 4)), w("RA", 0, 64), A.subtract)
+        cp("s" if t else "v", w("RB", 64, 128), ind(w(n, 0, 16 if CLASH else 8), lst("bl", 4, 4)))
+        gap(2)
+        tr(tb, rb)
+        gap(2)
+        st, rr, g1, g2, cc = [w(x, 0, 64) for x in ("ST", "RR", "G1", "G2", "CC")]
+        tt(st, ind(w("TB", 64, 128), lst("sh", 4)), w("TB", 0, 64), A.add)
+        gap(2)
+        tr(rr, st)
+        gap(2)
+        tt(g1, st, rr, A.subtract)
+        gap(2)
+        tt(g2, g1, w("LM", 0, 64), A.is_lt)
+        gap(2)
+        scan(cc, w("SEG", 0, 64), g2)
+        gap(2)
+        for q in range(4):
+            cp("vs"[q % 2], w("XR", 2, 4, 1, 32 * q, 32 * q + 32), w("CC", 31, 64, 32, 32 * (q ^ 1), 32 * (q ^ 1) + 32))
+        cp("v", w("XR", 0, 2), w("CC", 31, 64, 32))
+        cp("v", w("XR", 4, 8, 1, 0, 64), w("XR", 0, 4, 1, 64, 128))
+        cp("s", w("XR", 4, 8, 1, 64, 128), w("XR", 0, 4, 1, 0, 64))
+        gap(len(gaps))
+        rg, m, xr = w("RG", 0, 64), w("MM", 0, 64), w("XR", 0, 8)
+        wk = "WK%d" % t
+        tt(rg, ind(xr, lst("rg", 4)), w("MT", 0, 64), A.not_equal)
+        tt(w("RGK", 0, 32), ind(xr, lst("r2", 2)), w("MT", 0, 32), A.not_equal)
+        tr(m, rg)
+        tr(w("MK", 0, 32), w("RGK", 0, 32))
+        scan(w("SCN", 0, 64), m, w("DMP", 0, 64))
+        scan(w("SK", 0, 32), w("MK", 0, 32), w("DK", 0, 32))
+        cp("v", w("L1U", 0, 2), w("SCN", 31, 64, 32))
+        ts(w("KB", 0, 32), w("ONE", 0, 32), w("SK", 31, 32), A.mult)
+        if t == 0:
+            quant("DL", 0, w("DT0", 0, 1024))
+        dc, sn, la, kx = "DC%d" % t, "SN%d" % t, "LA%d" % t, "KX%d" % t
+        pick(dc, 0, 32, "DL", 256 + 32 * t, ("L1U", 0))
+        tr(w(wk, 0, 32), w("KB", 0, 32))
+        if t:
+            scan(w("SCN", 64, 128), m, w("DF", 0, 64))
+        pick(sn, 0, 64, dc, 32, ("LST", LISTS["sn"]))
+        hs, close = T.sem["hs%d" % t], _near(core, helpers[0], away, topo)
+        fused([w("c_" + sn, 0, 64)], [([helpers[h]], close[NHAND * h:NHAND * h + NHAND], hs, T["c_" + sn][:, 32 * h:32 * h + 32].bitcast(dt.uint8),
+                                       T["c_HC%d" % t][:, 0:32].bitcast(dt.uint8)) for h in range(2)])
+        a = 32 * (1 - me // HALF)
+        fused([w("z_" + sn, 0, 64)], [([helpers[2]], close[:2 * NHAND], hs, T["z_" + sn][:, a:a + 32], T["z_HZ%d" % t][:, 0:32])])
+        for part in _calls(me, cores, topo):
+            fused([w(wk, 0, 32)], [([cores[o]], _list_mask(me, o, cores, topo), T.sem["ls%d" % t], T[wk][:, 4 * o:4 * o + 4],
+                                    T[kx][:, 32 + 4 * pos(me, o):36 + 4 * pos(me, o)]) for o in part])
+        fused([w("z_" + sn, 0, 64)], [([cores[o]], _mask(me, o, mine, core, cores, topo), T.sem["dl%d" % t], T["z_" + sn][:, 8 * o:8 * o + 8],
+                                       T["z_" + la][:, 16 + 8 * pos(me, o):24 + 8 * pos(me, o)]) for o in mine])
+        run("y", lambda: g.sync.dma_start(T[kx][:, 60:64], T[wk][:, 4 * me:4 * me + 4]), [w(wk, 4 * me, 4 * me + 4)], [w(kx, 60, 64)], dma=True)
+        arrive([w(kx, 32, 60)], "ls%d" % t, sum(len(_list_mask(s, me, cores, topo)) for s in others))
+        arrive([w("c_" + la, 16, 72), w("z_" + la, 16, 72)], "dl%d" % t, sum(delta_count(s) for s in others))
+        inv, vals, l2 = w("INV%d" % t, 0, 256), w("VALS", 0, 32), w("L2U", 0, 2)
+        sa(inv, w("EB", 0, 256), 0.0, 8.0)
+        if t == 0:
+            for k in range(R):
+                sa(w("KX%d" % k, 0, 32), fkp, 1.0, -0.5)
+            sa(w("SEGG", 0, 192), w("ONE", 0, 192), 0.0, 1.0)
+            sa(w("SEGH", 0, 320), w("ONE", 0, 320), 0.0, 1.0)
+            sa(col(COUT), col(P8), 32.0, col(B3))
+            sa(w("K4", 0, 64), kt, 4.0, 256.0)
+            sa(w("SEGG", 0, 192, 64), w("ONE", 0, 3), 0.0)
+            sa(w("SEGH", 0, 320, 32), w("ONE", 0, 10), 0.0)
+            for f in after:
+                f()
+            scan(w("SCN", 64, 128), m, w("DF", 0, 64))
+        cp("v", l2, w("SCN", 95, 128, 32))
+        run("v", lambda: g.vector.tensor_copy(inv[0].indirect(l2[0]), vals[0]), [vals, l2], [inv])
+        pick(la, 0, 16, dc, 32, ("LST", LISTS["ow"]))
+        tr(w("INVT", 0, 256), inv)
+
+    def advance(t):
+        d, dn, it = "D%d" % t, "D%d" % (t + 1), w("INVT", 0, 256)
+        pick(d, 256, 32, "NX", 256 + 32 * t, ("L1U", 0))
+        if t < R - 1:
+            for b in range(4):
+                mm(b, 128, "W", 128 * b, d, 256)
+        wd, we, dls = w("WD", 0, 16), w("WE", 0, 16), w("DLS", 0, 16)
+        rg, rt, mask, u = w("RG", 0, 64), w("RT", 0, 64), w("UP", 0, 64), w("UP", 64, 128)
+        row = [lambda: cp("v", wd, ind(it, lst("w2", 1))), lambda: ts(we, wd, 8.0, A.not_equal), lambda: tt(wd, wd, c1, A.add),
+               lambda: tt(wd, wd, we, A.mult), lambda: tt(wd, wd, own16, A.add), lambda: cp("v", dls, wd)]
+        moved = [lambda: cp("v", rg, ind(w("XR", 0, 8), lst("rg", 4))), lambda: tr(rt, rg), lambda: ts(mask, rt, 4.0, A.is_lt),
+                 lambda: tt(u, rt, w("K4", 0, 64), A.add), lambda: tt(u, u, mp, A.subtract), lambda: tt(u, u, mask, A.mult)]
+        for i in range(6):
+            row[i]()
+            if t < R - 1:
+                moved[i]()
+            if t == 0:
+                for f in owner[4 * i:4 * i + 4]:
+                    f()
+        if t < R - 1:
+            for b in range(4):
+                relu("HT1", b, 32, b)
+            tt(mp, mp, u, A.add)
+            quant("NX", 256 + 32 * t, w("HT1", 0, 512))
+        pick(dn, 0, 256, d, 288, ("DLS", 0))
+        if t < R - 1:
+            differences("DMP", 0, "MAP")
+            for h in range(2):
+                mm(4 + h, 128, dn, 128 * h, "U", 0)
+            cp("s", w("ACOL", 0, 2), w("ps", 2048 + t + 1, 3072, 512))
+            if t == 0:
+                sa(w("K4", 0, 64), w("K4", 0, 64), 1.0, 32.0)
+        else:
+            ts(lst("out", 16), fout, col(COUT), A.add)
+            pick("FD", 0, 256, dn, 256, ("LST", LISTS["out"]))
+            mm(4, 256, "U", 0, "FD", 0)
+            cp("s", w("YB", 0, 256), w("ps", 2048, 2304))
+            fd = w("c_FD", 0, 256)
+            store("y", T.oc[:, 0:1024], (fd[0].bitcast(dt.uint8), fd[1]))
+            store("y", T.y[:, 0:256], w("YB", 0, 256))
+            for k in range(4):
+                store("y", T.osc[4 * k:4 * k + 4, 0:256], w("z_FD", 0, 256, 1, 32 * k, 32 * k + 4))
+
+    def patch(t):
+        la, kx, pb, pn, last = "LA%d" % t, "KX%d" % t, "PB%d" % t, "PB%d" % (t + 1), t == R - 1
+        tr(w("KT", 0, 32), w(kx, 32, 64))
+        ts(w("GG", 0, 64), w(kx, 0, 64), col(PC), A.is_lt)
+        ts(w("GG", 128, 192), w(kx, 0, 64), col(PC3), A.is_lt)
+        ts(w("GG", 64, 128), w(kx, 0, 64), w("KT", 0, 1), A.is_lt)
+        scan(w("CN", 0, 192), w("SEGG", 0, 192), w("GG", 0, 192))
+        pp, pd, p3 = w("CN", 63, 64), w("CN", 127, 128), w("CN", 191, 192)
+        ts(w("HH", 0, 128), w("WT", 0, 128), pp, A.is_equal, w("VPB", 0, 1), A.mult)
+        ts(w("HH", 128, 256), w("WT", 0, 128), pd, A.is_equal, w("VDB", 0, 1), A.mult)
+        ts(col(MK1), p3, pp, A.subtract, 1.0, A.is_gt)
+        tr(w("HHT", 0, 256), w("HH", 0, 256))
+        ts(col(SU), p3, col(C1P), A.add, col(MK1), A.mult)
+        scan(w("SH", 0, 256), w("SEGH", 0, 256), w("HHT", 0, 256))
+        ts(col(SU), col(SU), col(OP), A.add)
+        tt(w("ALF", 0, 4), w("SH", 31, 128, 32), w("SH", 159, 256, 32), A.add)
+        ts(w("HH", 256, 320), w("MASK", 0, 64), col(SU), A.mult)
+        for k in range(2):
+            for h in range(2):
+                cp("v", w("AL", 4 * k, 4 * k + 4, 1, 64 * h, 64 * h + 64), w("ALF", 0, 4, 1, 64 * k, 64 * k + 64))
+        ms, tb, al = w("MS", 0, 128), w("TBL", 0, 144), w("AL", 0, 8)
+        pick("AR", 0, 128, la, 144, ("AL", 0))
+        run("s", lambda: g.scalar.activation(ms[0], tb[0].indirect(al[0]), F.Copy), [tb, al], [ms])
+        for b in range(4):
+            mm(b, 128, "E", 128 * b, "AR", 0)
+        tr(w("HHT", 256, 320), w("HH", 256, 320))
+        scan(w("SH", 256, 320), w("SEGH", 256, 320), w("HHT", 256, 320))
+        for k in range(2):
+            for h in range(2):
+                cp("s", w("SX", 2 * k, 2 * k + 2, 1, 64 * h, 64 * h + 64), w("SH", 287, 320, 32, 64 * k, 64 * k + 64))
+        for b in range(4):
+            scan(w("NT", b, 512, 4), ms, bank(b, 128))
+            if b == 2:
+                cp("v", w("SEL", 0, 16), ind(w("SX", 0, 4), lst("sl" if last else "se", 1)))
+        quant(pb, 0, w("NT", 0, 512))
+        pick(pn, OLD, 128, pb, 256, ("SEL", 0))
+        if not last:
+            scores(t + 1)
+            pick("LA%d" % (t + 1), LAP, 64, pn, 128, ("LST", LISTS["pp"]), OLD)
+            for b in range(4):
+                mm(4 + b, 128, "E", 512 + 128 * b, "D%d" % t, 256, True, False)
+                mm(4 + b, 128, "E", 128 * b, "NX", 256 + 32 * t, False, True)
+            for b in range(4):
+                cp("vs"[b % 2], w("DT1", b, 128, 4), bank(4 + b, 32))
+            quant("DL", 256 + 32 * t, w("DT1", 0, 512))
+            arow()
+            if t == 0:
+                quant("D1", 256, w("ZB", 0, 512))
+        else:
+            mm(0, 128, "V", 0, pn, OLD)
+            cc = w("c_" + pn, OLD, OLD + 64)
+            store("y", T.oc[:, 1024:1280], (cc[0].bitcast(dt.uint8), cc[1]))
+            for k in range(4):
+                store("ys"[k % 2], T.osc[4 * k:4 * k + 4, 256:320], w("z_" + pn, OLD, OLD + 64, 1, 32 * k, 32 * k + 4))
+            cp("v", w("YB", 256, 320), bank(0, 64))
+            store("s", T.y[:, 256:320], w("YB", 256, 320))
+
+    for t in range(R):
+        choose(t)
+        advance(t)
+        patch(t)
+    for sem in sorted(total):
+        if known["g"].get(sem, 0) < total[sem]:
+            g.wait_ge(T.sem[sem], total[sem])

@@ -22,19 +22,20 @@ def _add(d, text, mx=False):
             SCRATCH[name] = ("sbuf", [128, int(n)], d)
 
 
-_add(BF, "XB:1024 PT:512 UB:512 VB:512 ONE:520 EB:520 NB:520 ZB:512 HT0:1024 DT0:1024 HT1:512 DT1:512 NT:512 "
+_add(BF, "XB:1024 PT:512 UB:512 VB:512 UV:512 ONE:520 EB:520 NB:520 ZB:512 HT0:1024 DT0:1024 HT1:512 DT1:512 NT:512 "
          "INV0:256 INV1:256 INV2:256 INVT:256 VALS:32 KX0:64 KX1:64 KX2:64 WK0:32 WK1:32 WK2:32 KW:354 CT:848 "
          "GG:192 HH:320 HHT:320 SH:320 MS:128")
-_add(FP8, "X:256 U:128 V:128 W:512 E:1024 D0:384 D1:384 D2:384 D3:256 FD:256 NX:416 DL:416 PB0:256 PB1:256 PB2:256 "
+_add(FP8, "X:256 U:128 V:128 S:128 W:512 E:1024 D0:384 D1:384 D2:384 D3:256 FD:256 NX:416 DL:416 PB0:256 PB1:256 PB2:256 "
           "PB3:256 DC0:32 DC1:32 DC2:32 SN0:64 SN1:64 SN2:64 LA0:144 LA1:144 LA2:144 AR:128", mx=True)
 _add(FP8, "c_HC0:32 c_HC1:32 c_HC2:32")
 _add(U8, "z_HZ0:32 z_HZ1:32 z_HZ2:32")
-_add(F32, "N0:16 N1:16 N2:16 SC0:1 SC1:1 SC2:1 FC:64 MAP:64 LM:64 SM:512 TMPF:320 "
-          "ACOL:8 RA:64 RB:128 TB:128 ST:64 RR:64 G1:64 G2:64 CC:64 XR:8 RG:64 RT:64 MM:64 SCN:128 DMP:64 DF:64 "
-          "DK:32 YB:320 UP:128")
+_add(F32, "N0:16 N1:16 N2:16 SC0:1 SC1:1 SC2:1 FC:64 MAP:64 SM:832 TMPF:320 "
+          "ACOL:8 RA:64 RB:128 TB:128 ST:64 RR:64 XR:8 RG:64 RT:64 MM:64 SCN:128 DMP:64 DF:64 "
+          "YB:320 UP:128")
 _add(I32, "PI:1 INTC:16 TMPI:256")
 ALIAS = {}
-for _buf, _text in (("SM", "OWN:0 C1:16 WD:32 WE:48 SQ:64 ALF:68 SX:72 SEG:96 MT:160 IOI:248 KTB:312 K4:376 OFR:440"),
+for _buf, _text in (("SM", "OWN:0 C1:16 WD:32 WE:48 SQ:64 ALF:68 SX:72 SEG:96 MT:160 IOI:248 KTB:312 K4:376 OFR:440 "
+                           "LM:512 G1:576 G2:640 CC:704 DK:768"),
                     ("CT", "TBL:0 WT:144 MASK:272 SEGG:336 SEGH:528"),
                     ("KW", "RGK:0 MK:32 SK:64 KB:96 KT:128 CN:160 VPB:352 VDB:353"),
                     ("LW", "DLS:0 SEL:16 AL:32 L1U:40 L2U:42")):
@@ -74,14 +75,14 @@ def _half(h, s):
 def _calls(s, cores, topo):
     fs = _far(s, cores, topo)
     n = len(topo.engines(cores[s], cores[fs[0]])) // 2
-    return [[o for o in range(len(cores)) if o != s and o not in fs[n:]], fs[n:]]
+    return [fs[:n], [o for o in range(len(cores)) if o != s and o not in fs[:n]]]
 
 
-def _mask(s, d, dests, src, cores, topo):
+def _mask(s, d, dests, src, cores, topo, near=2):
     fs = _far(s, cores, topo)
     away = topo.engines(src, cores[fs[0]])
     if d not in fs:
-        return _near(src, cores[d], away, topo)[:2]
+        return _near(src, cores[d], away, topo)[:near]
     fs = [o for o in dests if o in fs]
     n = 2 if len(fs) > 2 else 4
     i = n * fs.index(d)
@@ -90,7 +91,7 @@ def _mask(s, d, dests, src, cores, topo):
 
 def _list_mask(s, d, cores, topo):
     dests = [c for c in _calls(s, cores, topo) if d in c][0]
-    return _mask(s, d, dests, cores[s], cores, topo)
+    return _mask(s, d, dests, cores[s], cores, topo, 8)
 
 
 def _hand_mask(s, d, src, cores, topo):
@@ -325,14 +326,16 @@ def rank_program(g, core, T, topo):
     DB = QB + 1 if QB < 3 else 2
     CLASH = r % 4 == 0
 
-    load("s", w("VB", 0, 512), T.v[:, :])
-    for b in range(4):
-        load("ys"[b % 2], w("PT", 128 * b, 128 * b + 128), (T.pr if b == QB else T.pd)[:, :])
+    load("s", w("PT", 128 * DB, 128 * DB + 128), T.pd[:, :])
+    load("y", w("PT", 128 * QB, 128 * QB + 128), T.pr[:, :])
+    load("s", w("UV", 16, 32), T.v[:, 0:16])
+    load("y", w("UV", 0, 16), T.u[:, 0:16])
     load("y", w("XB", 0, 1024), T.x[:, :])
-    load("s", w("UB", 0, 512), T.u[:, :])
+    load("s", w("z_W", 0, 512), T.ws[:, :])
     cw = w("c_W", 0, 512)
     load("y", (cw[0].bitcast(dt.uint8), cw[1]), T.wc[:, :])
-    load("s", w("z_W", 0, 512), T.ws[:, :])
+    load("y", w("UB", 0, 512), T.u[:, :])
+    load("y", w("VB", 0, 512), T.v[:, :])
 
     TMP = [0]
     def ftmp(n):
@@ -343,9 +346,10 @@ def rank_program(g, core, T, topo):
     fnat, fbl, frg, fsh, fsn, fout, fr2, fc1, f1, fa, fb, fh, fkp, ktf, fm = [ftmp(n) for n in (16, 4, 4, 4, 4, 16, 2, 16, 64, 2, 2, 2, 32, 32, 64)]
     iota(w("PI", 0, 1), [[0, 1]], 0, 1, small=False)
     fill(w("ONE", 0, 520), 1.0)
+    iota(fnat, [[1, 8], [128, 2]])
+    iota(fbl, [[4, 2], [0, 2]])
+    sa(w("UV", 32, 512), w("ONE", 0, 480), 0.0)
     sa(w("ZB", 0, 512), w("ONE", 0, 512), 0.0)
-    sa(w("HT1", 128, 512), w("ONE", 0, 384), 0.0)
-    sa(w("DT1", 128, 512), w("ONE", 0, 384), 0.0)
 
     def col(j):
         return w("FC", j, j + 1)
@@ -356,7 +360,7 @@ def rank_program(g, core, T, topo):
             ts(o, i, sh, A.arith_shift_right, an, A.bitwise_and)
         else:
             ts(o, i, an, A.bitwise_and)
-    C8P, CX, CSN, C16, CW2, CNX, CND, C32K, COUT, KR, SHF, PC, PC3, VP, VD, OP, C1P, MK1, SU, Y0, Y2 = range(16, 37)
+    C8P, CX, CSN, C16, CW2, CNX, CND, KK4, COUT, KR, SHF, PC, PC3, VP, VD, OP, C1P, MK1, SU, Y0, Y2 = range(16, 37)
     fill(w("SEG", 0, 64), 1.0)
     cp("v", w("FC", 0, 15), w("INTC", 0, 15))
     fill(w("SEG", 32, 33), 0.0)
@@ -364,74 +368,49 @@ def rank_program(g, core, T, topo):
         fill(lst("ac", 2, 2 * h), h)
     eb, one = w("EB", 0, 520), w("ONE", 0, 520)
     run("g", lambda: g.affine_select(eb[0], one[0], [[-1, 520]], A.is_equal, 0.0, 4, 4), [one], [eb])
-    iota(fnat, [[1, 8], [128, 2]])
-    iota(fbl, [[4, 2], [0, 2]])
     iota(fsh, [[0, 2], [16, 2]])
+    iota(frg, [[1, 2], [0, 2]])
+    iota(fsn, [[2, 4]])
+    iota(fr2, [[4, 2]])
+    iota(w("MT", 0, 64), [[0, 16], [1, 4]])
+    scan(ioi, w("SEG", 0, 64), w("ONE", 0, 64))
+    ts(col(C8P), col(P16), 8.0, A.mult)
+    ts(col(KK4), col(KK), 4.0, A.add)
+    ts(ioi, ioi, -1.0, A.add)
+    tt(col(CNX), col(B2), col(Q0), A.not_equal)
+    tt(col(CND), col(B3), col(Q1), A.not_equal)
+    ts(lst("nat", 16), fnat, col(C8P), A.add)
+    for h in range(2):
+        sa(w("KTB", 32 * h, 32 * h + 32), w("ONE", 0, 32), 0.0, col(KK4 if h else KK))
+    sa(f1, kt, 32.0)
+    sa(col(C16), col(ODD), 16.0)
+    sa(w("NB", 0, 520), eb, -1.0)
 
-    quant("V", 0, w("VB", 0, 512))
+    for b in range(4):
+        if b not in (QB, DB):
+            cp("v", w("PT", 128 * b, 128 * b + 128), w("PT", 128 * DB, 128 * DB + 128))
+    quant("S", 0, w("UV", 0, 512))
     quant("PB0", OLD, w("PT", 0, 512))
 
     def scores(t):
         sc, n = "SC%d" % t, "N%d" % t
-        mm(0, 128, "PB%d" % t, OLD, "V", 0)
-        cp("s", w(sc, 0, 1), w("ps", t, t + 1))
+        mm(0, 128, "PB%d" % t, OLD, "S", 0)
+        cp("s", w(sc, 0, 1), w("ps", 4 + t, 5 + t))
         send_scores(t)
         run("y", lambda: g.sync.dma_start(T[n][:, me:me + 1], T[sc][:, 0:1]), [w(sc, 0, 1)], [w(n, me, me + 1)], dma=True)
         arrive([w(n, a, b) for a, b in ((0, me), (me + 1, 8)) if b > a], "sc%d" % t, score_count())
 
     scores(0)
-    iota(frg, [[1, 2], [0, 2]])
-    iota(fsn, [[2, 4]])
-    iota(ioi, [[0, 2], [1, 32]])
-    iota(w("MT", 0, 64), [[0, 16], [1, 4]])
-    iota(fr2, [[4, 2]])
-    iota(mp, [[128, 2], [1, 32]])
-    iota(kt, [[4, 2], [0, 32]])
-    iota(w("VALS", 0, 32), [[0, 8], [1, 4]])
     own16, c1, sq = w("OWN", 0, 16), w("C1", 0, 16), w("SQ", 0, 4)
-    iota(own16, [[16, 16]])
     iota(sq, [[16, 4]])
+    iota(own16, [[16, 16]])
     iota(fc1, [[4, 8], [0, 2]])
+    iota(w("VALS", 0, 32), [[0, 8], [1, 4]])
     iota(fkp, [[8, 32]], -MID)
     iota(fm, [[16, 2], [0, 2], [1, 16]])
     iota(w("WT", 0, 128), [[16, 4], [0, 2], [1, 16]])
     iota(fout, [[2, 16]])
 
-    ts(col(C8P), col(P16), 8.0, A.mult)
-    tt(col(CNX), col(B2), col(Q0), A.not_equal)
-    tt(col(CND), col(B3), col(Q1), A.not_equal)
-    ts(lst("nat", 16), fnat, col(C8P), A.add)
-    sa(w("NB", 0, 520), eb, -1.0)
-    quant("X", 0, w("XB", 0, 1024))
-    pick("D0", 0, 256, "X", 256, ("LST", LISTS["nat"]))
-    quant("U", 0, w("UB", 0, 512))
-    for b in range(2):
-        mm(b, 256, "W", 128 * b, "D0", 0)
-    for h in range(2):
-        mm(4 + h, 128, "D0", 128 * h, "U", 0)
-    for b in range(2, 4):
-        mm(b, 256, "W", 128 * b, "D0", 0)
-    for b in range(4):
-        quant("E", 512 + 128 * b, w("NB", 4 - b, 516 - b))
-
-    def relu(tile, b, cols, bk):
-        o, i = w(tile, b, 4 * cols, 4), bank(bk, cols)
-        run("s", lambda: g.scalar.activation(o[0], i[0], F.Relu, scale=0.0625), [i], [o])
-
-    relu("HT0", 0, 256, 0)
-    relu("HT0", 1, 256, 1)
-    cp("s", w("ACOL", 0, 2), w("ps", 2048, 3072, 512))
-    relu("HT0", 2, 256, 2)
-    relu("HT0", 3, 256, 3)
-    sa(col(C32K), col(KK), 32.0)
-    sa(col(C16), col(ODD), 16.0)
-    sa(kt, kt, 1.0, col(KK))
-    sa(mp, mp, 1.0, col(C32K))
-    sa(w("DMP", 0, 64), mp, 0.0, -1.0)
-    sa(f1, kt, 32.0)
-    cp("s", w("DMP", 31, 64, 32), w("MAP", 31, 64, 32))
-    for b in range(4):
-        mm(4 + b, 256, "E", 512 + 128 * b, "D0", 0, True, False)
     bi, shi, sni = w("TMPI", 12, 16), w("TMPI", 0, 4), w("TMPI", 4, 8)
     t0, b0, b1, hh = [w("TMPI", a, a + 2) for a in (144, 146, 148, 150)]
     kti, k0 = w("TMPI", 80, 112), ktf[1][0][1]
@@ -451,8 +430,30 @@ def rank_program(g, core, T, topo):
     ts(col(CX), col(CX), 2.0, A.mult)
     ts(sni, fsn, col(CSN), A.add)
     ts(lst("bl", 4, 4), bi, 8.0 if CLASH else 0.0, A.add)
+
+    quant("X", 0, w("XB", 0, 1024))
     ts(shi, shi, 31, A.bitwise_and)
     ts(b0, t0, 1, A.bitwise_and)
+    pick("D0", 0, 256, "X", 256, ("LST", LISTS["nat"]))
+    tt(mp, ioi, f1, A.add)
+    for h in range(2):
+        mm(4 + h, 128, "D0", 128 * h, "S", 0)
+    for b in range(4):
+        mm(b, 256, "W", 128 * b, "D0", 0)
+    for b in range(4):
+        quant("E", 512 + 128 * b, w("NB", 4 - b, 516 - b))
+
+    def relu(tile, b, cols, bk):
+        o, i = w(tile, b, 4 * cols, 4), bank(bk, cols)
+        run("s", lambda: g.scalar.activation(o[0], i[0], F.Relu, scale=0.0625), [i], [o])
+
+    cp("s", w("ACOL", 0, 2), w("ps", 2048, 3072, 512))
+    sa(w("DMP", 0, 64), mp, 0.0, -1.0)
+    cp("s", w("DMP", 31, 64, 32), w("MAP", 31, 64, 32))
+    for b in range(4):
+        relu("HT0", b, 256, b)
+    for b in range(4):
+        mm(4 + b, 256, "E", 512 + 128 * b, "D0", 0, True, False)
     ts(lst("rg", 4), frg, col(CX), A.add)
     ts(sni, sni, 7, A.bitwise_and)
     cp("v", lst("sh", 2), w("TMPI", 0, 2))
@@ -465,13 +466,6 @@ def rank_program(g, core, T, topo):
 
     def arow():
         cp("v", w("RA", 0, 64), ind(w("ACOL", 0, 2), lst("ac", 4)))
-
-    arow()
-    quant("NX", 0, w("HT0", 0, 1024))
-    for b in range(4):
-        mm(4 + b, 256, "E", 128 * b, "NX", 0, False, True)
-    for b in range(4):
-        cp("s", w("DT0", b, 1024, 4), bank(4 + b, 256))
 
     def differences(name, c, src):
         tt(w(name, c, c + 63), w(src, 0, 63), w(src, 1, 64), A.subtract)
@@ -539,6 +533,16 @@ def rank_program(g, core, T, topo):
             if gaps:
                 gaps.pop(0)()
 
+    arow()
+    gap(8)
+    quant("NX", 0, w("HT0", 0, 1024))
+    gap(8)
+    for b in range(4):
+        mm(4 + b, 256, "E", 128 * b, "NX", 0, False, True)
+    for b in range(4):
+        cp("s", w("DT0", b, 1024, 4), bank(4 + b, 256))
+    gaps.extend(after)
+
     def choose(t):
         n = "N%d" % t
         if CLASH:
@@ -577,22 +581,27 @@ def rank_program(g, core, T, topo):
         scan(w("SK", 0, 32), w("MK", 0, 32), w("DK", 0, 32))
         cp("v", w("L1U", 0, 2), w("SCN", 31, 64, 32))
         ts(w("KB", 0, 32), w("ONE", 0, 32), w("SK", 31, 32), A.mult)
+        dc, sn, la, kx = "DC%d" % t, "SN%d" % t, "LA%d" % t, "KX%d" % t
         if t == 0:
             quant("DL", 0, w("DT0", 0, 1024))
-        dc, sn, la, kx = "DC%d" % t, "SN%d" % t, "LA%d" % t, "KX%d" % t
+            tr(w(wk, 0, 32), w("KB", 0, 32))
         pick(dc, 0, 32, "DL", 256 + 32 * t, ("L1U", 0))
-        tr(w(wk, 0, 32), w("KB", 0, 32))
         if t:
-            scan(w("SCN", 64, 128), m, w("DF", 0, 64))
+            tr(w(wk, 0, 32), w("KB", 0, 32))
+
+        def keys(part):
+            fused([w(wk, 0, 32)], [([cores[o]], _list_mask(me, o, cores, topo), T.sem["ls%d" % t], T[wk][:, 4 * o:4 * o + 4],
+                                    T[kx][:, 32 + 4 * pos(me, o):36 + 4 * pos(me, o)]) for o in part])
+        parts = _calls(me, cores, topo)
+        keys(parts[0])
+        scan(w("SCN", 64, 128), m, w("DF", 0, 64))
         pick(sn, 0, 64, dc, 32, ("LST", LISTS["sn"]))
         hs, close = T.sem["hs%d" % t], _near(core, helpers[0], away, topo)
         fused([w("c_" + sn, 0, 64)], [([helpers[h]], close[NHAND * h:NHAND * h + NHAND], hs, T["c_" + sn][:, 32 * h:32 * h + 32].bitcast(dt.uint8),
                                        T["c_HC%d" % t][:, 0:32].bitcast(dt.uint8)) for h in range(2)])
         a = 32 * (1 - me // HALF)
         fused([w("z_" + sn, 0, 64)], [([helpers[2]], close[:2 * NHAND], hs, T["z_" + sn][:, a:a + 32], T["z_HZ%d" % t][:, 0:32])])
-        for part in _calls(me, cores, topo):
-            fused([w(wk, 0, 32)], [([cores[o]], _list_mask(me, o, cores, topo), T.sem["ls%d" % t], T[wk][:, 4 * o:4 * o + 4],
-                                    T[kx][:, 32 + 4 * pos(me, o):36 + 4 * pos(me, o)]) for o in part])
+        keys(parts[1])
         fused([w("z_" + sn, 0, 64)], [([cores[o]], _mask(me, o, mine, core, cores, topo), T.sem["dl%d" % t], T["z_" + sn][:, 8 * o:8 * o + 8],
                                        T["z_" + la][:, 16 + 8 * pos(me, o):24 + 8 * pos(me, o)]) for o in mine])
         run("y", lambda: g.sync.dma_start(T[kx][:, 60:64], T[wk][:, 4 * me:4 * me + 4]), [w(wk, 4 * me, 4 * me + 4)], [w(kx, 60, 64)], dma=True)
@@ -601,17 +610,15 @@ def rank_program(g, core, T, topo):
         inv, vals, l2 = w("INV%d" % t, 0, 256), w("VALS", 0, 32), w("L2U", 0, 2)
         sa(inv, w("EB", 0, 256), 0.0, 8.0)
         if t == 0:
+            sa(w("K4", 0, 64), kt, 4.0, 256.0)
+            sa(w("HT1", 128, 512), w("ONE", 0, 384), 0.0)
             for k in range(R):
                 sa(w("KX%d" % k, 0, 32), fkp, 1.0, -0.5)
             sa(w("SEGG", 0, 192), w("ONE", 0, 192), 0.0, 1.0)
             sa(w("SEGH", 0, 320), w("ONE", 0, 320), 0.0, 1.0)
             sa(col(COUT), col(P8), 32.0, col(B3))
-            sa(w("K4", 0, 64), kt, 4.0, 256.0)
             sa(w("SEGG", 0, 192, 64), w("ONE", 0, 3), 0.0)
             sa(w("SEGH", 0, 320, 32), w("ONE", 0, 10), 0.0)
-            for f in after:
-                f()
-            scan(w("SCN", 64, 128), m, w("DF", 0, 64))
         cp("v", l2, w("SCN", 95, 128, 32))
         run("v", lambda: g.vector.tensor_copy(inv[0].indirect(l2[0]), vals[0]), [vals, l2], [inv])
         pick(la, 0, 16, dc, 32, ("LST", LISTS["ow"]))
@@ -641,15 +648,11 @@ def rank_program(g, core, T, topo):
                 relu("HT1", b, 32, b)
             tt(mp, mp, u, A.add)
             quant("NX", 256 + 32 * t, w("HT1", 0, 512))
-        pick(dn, 0, 256, d, 288, ("DLS", 0))
-        if t < R - 1:
-            differences("DMP", 0, "MAP")
-            for h in range(2):
-                mm(4 + h, 128, dn, 128 * h, "U", 0)
-            cp("s", w("ACOL", 0, 2), w("ps", 2048 + t + 1, 3072, 512))
             if t == 0:
                 sa(w("K4", 0, 64), w("K4", 0, 64), 1.0, 32.0)
+                sa(w("DT1", 128, 512), w("ONE", 0, 384), 0.0)
         else:
+            pick(dn, 0, 256, d, 288, ("DLS", 0))
             ts(lst("out", 16), fout, col(COUT), A.add)
             pick("FD", 0, 256, dn, 256, ("LST", LISTS["out"]))
             mm(4, 256, "U", 0, "FD", 0)
@@ -698,16 +701,25 @@ def rank_program(g, core, T, topo):
         pick(pn, OLD, 128, pb, 256, ("SEL", 0))
         if not last:
             scores(t + 1)
-            pick("LA%d" % (t + 1), LAP, 64, pn, 128, ("LST", LISTS["pp"]), OLD)
+            dn = "D%d" % (t + 1)
+            pick(dn, 0, 256, "D%d" % t, 288, ("DLS", 0))
             for b in range(4):
                 mm(4 + b, 128, "E", 512 + 128 * b, "D%d" % t, 256, True, False)
                 mm(4 + b, 128, "E", 128 * b, "NX", 256 + 32 * t, False, True)
+            for h in range(2):
+                mm(1 + h, 128, dn, 128 * h, "S", 0)
             for b in range(4):
                 cp("vs"[b % 2], w("DT1", b, 128, 4), bank(4 + b, 32))
+            cp("s", w("ACOL", 0, 2), w("ps", 512 + t + 1, 1536, 512))
+            differences("DMP", 0, "MAP")
             quant("DL", 256 + 32 * t, w("DT1", 0, 512))
             arow()
+            pick("LA%d" % (t + 1), LAP, 64, pn, 128, ("LST", LISTS["pp"]), OLD)
             if t == 0:
                 quant("D1", 256, w("ZB", 0, 512))
+            else:
+                quant("U", 0, w("UB", 0, 512))
+                quant("V", 0, w("VB", 0, 512))
         else:
             mm(0, 128, "V", 0, pn, OLD)
             cc = w("c_" + pn, OLD, OLD + 64)

@@ -1,13 +1,12 @@
 from concourse.bass import DstId, RemoteDMATransfer
-from concourse.mybir import dt, AluOpType as A, ActivationFunctionType as F
+from concourse.mybir import dt, AluOpType as A, ActivationFunctionType as F, AxisListType as AX
 
 R = 3
 HALF = 4
-NHAND = 4
-TINY = 2.0 ** -110
 MID = 124
 OLD = 128
 LAP = 80
+BIG = 2.0 ** 60
 FP8, U8, BF, F32, I32, U16 = "float8_e4m3fn_x4", "uint8", "bfloat16", "float32", "int32", "uint16"
 SCRATCH = {"ps": ("psum", [128, 4096], F32)}
 
@@ -22,30 +21,53 @@ def _add(d, text, mx=False):
             SCRATCH[name] = ("sbuf", [128, int(n)], d)
 
 
-_add(BF, "XB:1024 PT:512 UB:512 VB:512 UV:512 ONE:520 EB:520 NB:520 ZB:512 HT0:1024 DT0:1024 HT1:512 DT1:512 NT:512 "
-         "INV0:256 INV1:256 INV2:256 INVT:256 VALS:32 KX0:64 KX1:64 KX2:64 WK0:32 WK1:32 WK2:32 KW:354 CT:848 "
-         "GG:192 HH:320 HHT:320 SH:320 MS:128")
-_add(FP8, "X:256 U:128 V:128 S:128 W:512 E:1024 D0:384 D1:384 D2:384 D3:256 FD:256 NX:416 DL:416 PB0:256 PB1:256 PB2:256 "
-          "PB3:256 DC0:32 DC1:32 DC2:32 SN0:64 SN1:64 SN2:64 LA0:144 LA1:144 LA2:144 AR:128", mx=True)
+_add(BF, "XB:1024 PT:512 UB:512 VB:512 UV:512 ONE:520 EB:520 NB:520 HT:1024 DT:1024 NT:512 "
+         "KX0:64 KX1:64 KX2:64 WK0:32 WK1:32 WK2:32 KW:256 CT:1072 GG:192 HH:384 HHT:384 SH:384 MS:128 "
+         "EL:128 CC:256 RG:128 MM:128 XR:16")
+_add(FP8, "X:256 U:128 V:128 S:128 W:512 E:1024 XA:1024 FD:320 DL:768 PB0:256 PB1:256 PB2:256 "
+          "SN0:64 SN1:64 SN2:64 LA0:144 LA1:144 LA2:144 AR:128", mx=True)
 _add(FP8, "c_HC0:32 c_HC1:32 c_HC2:32")
 _add(U8, "z_HZ0:32 z_HZ1:32 z_HZ2:32")
-_add(F32, "N0:16 N1:16 N2:16 SC0:1 SC1:1 SC2:1 FC:64 MAP:64 SM:832 TMPF:320 "
-          "ACOL:8 RA:64 RB:128 TB:128 ST:64 RR:64 XR:8 RG:64 RT:64 MM:64 SCN:128 DMP:64 DF:64 "
-          "YB:320 UP:128")
-_add(I32, "PI:1 INTC:16 TMPI:256")
+_add(F32, "N0:32 N1:32 N2:32 SC0:1 SC1:1 SC2:1 FC:64 SM:224 TMPF:72 RA:64 RB:64 RR:64 ST:64 SCN:128 DMP:128 MP:128 MPT:128 YB:320")
+_add(I32, "PI:1 XI:8 INTC:16 TMPI:48")
 ALIAS = {}
-for _buf, _text in (("SM", "OWN:0 C1:16 WD:32 WE:48 SQ:64 ALF:68 SX:72 SEG:96 MT:160 IOI:248 KTB:312 K4:376 OFR:440 "
-                           "LM:512 G1:576 G2:640 CC:704 DK:768"),
-                    ("CT", "TBL:0 WT:144 MASK:272 SEGG:336 SEGH:528"),
-                    ("KW", "RGK:0 MK:32 SK:64 KB:96 KT:128 CN:160 VPB:352 VDB:353"),
-                    ("LW", "DLS:0 SEL:16 AL:32 L1U:40 L2U:42")):
+for _buf, _text in (("SM", "XL:0 ACOL:8 AV1:32 AV2:40 LV:48 VM:64 PV:80 U8:88 SX:96 FB:136 FT:168 FO:200 SQ:216"),
+                    ("CT", "TBL:0 WT:144 MASK:272 SEGH:400 MT:784 RST:912 EM:1040"),
+                    ("KW", "RGK:0 MK:32 SK:96 KT:160 DK:192"),
+                    ("LW", "OUT:0 SEL:16 AL:32 L:40")):
     for _item in _text.split(" "):
         ALIAS[_item.split(":")[0]] = (_buf, int(_item.split(":")[1]))
-LISTS = {"nat": 0, "out": 16, "bl": 32, "sh": 40, "rg": 44, "ac": 48, "w2": 52, "r2": 54, "sn": 56, "ow": 60, "se": 62, "sl": 64, "pp": 66}
-_add(U16, "LST:70 LW:44")
-TILES = ("NT", "HT0", "HT1", "DT0", "DT1")
+LISTS = {"nat": 0, "bl": 16, "ac": 24, "rg": 28, "r2": 36, "fo": 38, "ow": 40, "hh": 42, "se": 44, "sl": 46, "pp": 48}
+_add(U16, "LST:52 LW:44")
 SEMAPHORES = (["qg", "qv", "qs", "qt", "snt"] + [s + str(t) for s in ("sc", "dl", "ls", "hs") for t in range(R)]
               + ["m%d" % i for i in range(48)])
+
+
+def _blocks(o):
+    b = o // 2
+    lay = ["R" if q == b else "D" if q > b else "S" for q in range(4)]
+    if b == 0:
+        lay[3] = "S"
+    if b == 3:
+        lay[2] = "D"
+    return lay
+
+
+def _fetch(r):
+    need, col = [], {}
+    for k in range(8):
+        o, q, kind = (k - r) % 8, k // 2, "D" if k >= r else "S"
+        col[k] = o
+        if _blocks(o)[q] != kind:
+            need.append((k, [x for x in range(4) if _blocks(o)[x] == kind]))
+    ways = [[]]
+    for k, src in need:
+        ways = [x + [(64 * (k // 4), 64 - 64 * (k // 4), 64) if s == (k // 2 + 2) % 4 else (32 * (k // 2), 32 * s, 32)] for x in ways for s in src]
+    way = min(ways, key=lambda x: len(set(x)))
+    moves = sorted(set(way), key=lambda x: (-x[2], x))
+    for (k, src), mv in zip(need, way):
+        col[k] += 8 + 8 * moves.index(mv)
+    return moves, col
 
 
 def pos(s, d):
@@ -72,30 +94,34 @@ def _half(h, s):
     return [o for o in range(HALF * h, HALF * h + HALF) if o != s]
 
 
+def _share(kind, dests, engines):
+    n = max(x for x in (1, 2, 4, 8, 16) if x * len(dests) <= len(engines))
+    return [(kind, d, engines[n * i:n * i + n]) for i, d in enumerate(dests)]
+
+
 def _calls(s, cores, topo):
     fs = _far(s, cores, topo)
-    n = len(topo.engines(cores[s], cores[fs[0]])) // 2
-    return [fs[:n], [o for o in range(len(cores)) if o != s and o not in fs[:n]]]
+    near = [o for o in range(len(cores)) if o != s and o not in fs]
+    away = topo.engines(cores[s], cores[fs[0]])
+    close = _near(cores[s], cores[near[0]], away, topo)
+    n = len(away) // 2
+    return [_share("key", fs[:n], away), _share("code", [0, 1], close), _share("hand", [2], close),
+            _share("key", fs[n:], away) + _share("key", near, close),
+            _share("scale", [o for o in _half(s // HALF, s) if o in fs], away) + _share("scale", near, close[:2])]
 
 
-def _mask(s, d, dests, src, cores, topo, near=2):
-    fs = _far(s, cores, topo)
-    away = topo.engines(src, cores[fs[0]])
-    if d not in fs:
-        return _near(src, cores[d], away, topo)[:near]
-    fs = [o for o in dests if o in fs]
-    n = 2 if len(fs) > 2 else 4
-    i = n * fs.index(d)
-    return away[i:i + n]
-
-
-def _list_mask(s, d, cores, topo):
-    dests = [c for c in _calls(s, cores, topo) if d in c][0]
-    return _mask(s, d, dests, cores[s], cores, topo, 8)
+def _sent(s, kind, d, cores, topo):
+    return sum(len(e) for call in _calls(s, cores, topo) for k, o, e in call if (k, o) == (kind, d))
 
 
 def _hand_mask(s, d, src, cores, topo):
-    return _mask(s, d, _half(d // HALF, s), src, cores, topo)[:2]
+    fs = _far(s, cores, topo)
+    away = topo.engines(src, cores[fs[0]])
+    if d not in fs:
+        return _near(src, cores[d], away, topo)[:2]
+    fs = [o for o in _half(d // HALF, s) if o in fs]
+    i = len(away) // len(fs) * fs.index(d)
+    return away[i:i + 2]
 
 
 def _to(core, topo):
@@ -108,7 +134,7 @@ def hand_on(g, core, s, cores, T, topo):
     h = k if k < 2 else 1 - s // HALF
     dests = _half(h, s)
     for t in range(R):
-        g.wait_ge(T.sem["hs%d" % t], NHAND if k < 2 else 2 * NHAND)
+        g.wait_ge(T.sem["hs%d" % t], _sent(s, "code" if k < 2 else "hand", k, cores, topo))
         tf = []
         for o in dests:
             p, i = pos(s, o), o - HALF * h
@@ -146,10 +172,14 @@ def rank_program(g, core, T, topo):
             a = t[:, c0:c1] if step == 1 else t[:, c0:c1:step]
         else:
             a = t[p0:p1, c0:c1] if step == 1 else t[p0:p1, c0:c1:step]
-        if step == 4 and name in TILES:
-            b = c0 % 4
-            return (a, [(name, c0 - b, c1, 32 * b, 32 * b + 32)])
-        return (a, [(name, c0, c1, p0, p1)])
+        if name == "ps":
+            cols = sum(1 << b for b in range(c0 // 512, (c1 + 511) // 512))
+            return (a, [(name, cols, 0, 128)])
+        cols = ((1 << (c1 - c0)) - 1) << c0 if step == 1 else sum(1 << c for c in range(c0, c1, step))
+        return (a, [(name, cols, p0, p1)])
+
+    def part(v, a, b, p0=0, p1=128, step=1):
+        return w("TMPF", v[2] + a, v[2] + b, step, p0, p1)
 
     def ind(v, o):
         return (v[0].indirect(o[0]), v[1] + o[1])
@@ -158,30 +188,22 @@ def rank_program(g, core, T, topo):
         a = LISTS[name] + off
         return w("LST", a, a + n)
 
-    def norm(reg):
-        name, c0, c1, p0, p1 = reg
-        if name == "ps":
-            return (name, c0 // 512 * 512, (c1 + 511) // 512 * 512, 0, 128)
-        return reg
-
     def waits(q, reads, writes):
         need = {}
         def want(h):
-            sem, n, clock = h[7], h[8], h[9]
+            sem, n, clock = h[6], h[7], h[8]
             if known[q].get(sem, 0) >= n:
                 return
             if sem not in need or need[sem][0] < n:
                 need[sem] = (n, clock)
-        for reg in reads:
-            name, c0, c1, p0, p1 = norm(reg)
+        for name, cols, p0, p1 in reads:
             for h in hist.get(name, ()):
-                if h[0] < c1 and c0 < h[1] and h[2] < p1 and p0 < h[3] and (h[4] or (name == "ps" and h[5] != q)):
+                if h[0] & cols and h[1] < p1 and p0 < h[2] and (h[3] or (name == "ps" and h[4] != q)):
                     want(h)
-        for reg in writes:
-            name, c0, c1, p0, p1 = norm(reg)
+        for name, cols, p0, p1 in writes:
             for h in hist.get(name, ()):
-                if h[0] < c1 and c0 < h[1] and h[2] < p1 and p0 < h[3]:
-                    if name == "ps" and h[5] == q:
+                if h[0] & cols and h[1] < p1 and p0 < h[2]:
+                    if name == "ps" and h[4] == q:
                         continue
                     want(h)
         for sem in sorted(need):
@@ -197,17 +219,13 @@ def rank_program(g, core, T, topo):
             known[q][sem] = max(known[q].get(sem, 0), n)
 
     def record(q, reads, writes, sem, n, clock, dma):
-        for reg in writes:
-            reg = norm(reg)
-            name, c0, c1, p0, p1 = reg
-            hs = [h for h in hist.get(name, ()) if not (c0 <= h[0] and h[1] <= c1 and p0 <= h[2] and h[3] <= p1)]
-            hs.append((c0, c1, p0, p1, True, q, dma, sem, n, clock))
+        for name, cols, p0, p1 in writes:
+            hs = [h for h in hist.get(name, ()) if not (h[0] & ~cols == 0 and p0 <= h[1] and h[2] <= p1)]
+            hs.append((cols, p0, p1, True, q, dma, sem, n, clock))
             hist[name] = hs
-        for reg in reads:
-            reg = norm(reg)
-            name, c0, c1, p0, p1 = reg
-            hs = [h for h in hist.get(name, ()) if not (not h[4] and not dma and not h[6] and h[5] == q and (c0, c1, p0, p1) == tuple(h[:4]))]
-            hs.append((c0, c1, p0, p1, False, q, dma, sem, n, clock))
+        for name, cols, p0, p1 in reads:
+            hs = [h for h in hist.get(name, ()) if not (not h[3] and not dma and not h[5] and h[4] == q and (cols, p0, p1) == tuple(h[:3]))]
+            hs.append((cols, p0, p1, False, q, dma, sem, n, clock))
             hist[name] = hs
 
     def run(q, call, reads, writes, dma=False):
@@ -259,8 +277,14 @@ def rank_program(g, core, T, topo):
     def scan(out, a, b):
         run("v", lambda: g.vector.tensor_tensor_scan(out[0], a[0], b[0], 0.0, A.mult, A.add), [a, b], [out])
 
+    def rsum(out, a):
+        run("v", lambda: g.vector.tensor_reduce(out[0], a[0], AX.X, A.add), [a], [out])
+
     def fill(out, c):
         run("v", lambda: g.vector.memset(out[0], c), [], [out])
+
+    def sfill(name, a, b, c, step=1):
+        sa(w(name, a, b, step), w("ONE", 0, len(range(a, b, step))), 0.0, c)
 
     def iota(out, pattern, base=0, ch=0, small=True):
         if small:
@@ -268,10 +292,9 @@ def rank_program(g, core, T, topo):
         else:
             run("g", lambda: g.iota(out[0], pattern, base, ch), [], [out])
 
-    def quant(name, c0, src):
-        n = (src[1][0][2] - src[1][0][1]) // 4
-        c, z = w("c_" + name, c0, c0 + n), w("z_" + name, c0, c0 + n)
-        run("v", lambda: g.vector.quantize_mx(c[0], z[0], src[0]), [src], [c, z])
+    def quant(name, c0, src, n):
+        c, z, a = w("c_" + name, c0, c0 + n), w("z_" + name, c0, c0 + n), w(src[0], src[1], src[1] + 4 * n)
+        run("v", lambda: g.vector.quantize_mx(c[0], z[0], a[0]), [a], [c, z])
 
     def pick(dst, d0, n, src, width, off, a0=0):
         b, k = off
@@ -290,17 +313,22 @@ def rank_program(g, core, T, topo):
     def bank(b, n, c0=0):
         return w("ps", 512 * b + c0, 512 * b + c0 + n)
 
-    def load(q, out, a):
-        run(q, lambda: Q[q].dma_start(out[0], a), [], [out], dma=True)
+    def load(q, out, a, after=()):
+        run(q, lambda: Q[q].dma_start(out[0], a), list(after), [out], dma=True)
 
     def store(q, a, src):
         run(q, lambda: Q[q].dma_start(a, src[0]), [src], [], dma=True)
+
+    def weave(*chains):
+        for i in range(max(len(c) for c in chains)):
+            for c in chains:
+                if i < len(c) and c[i]:
+                    c[i]()
 
     others = [o for o in range(n_ranks) if o != me]
     afar = _far(me, cores, topo)
     away = topo.engines(core, cores[afar[0]])
     helpers = _helpers(me, cores, topo)
-    mine = _half(me // HALF, me)
 
     def fused(reads, transfers):
         waits("g", [x for v in reads for x in v[1]], [])
@@ -310,21 +338,20 @@ def rank_program(g, core, T, topo):
 
     def send_scores(t):
         src, land, sem = w("SC%d" % t, 0, 1), T["N%d" % t][:, me:me + 1], T.sem["sc%d" % t]
-        fused([src], [([cores[o] for o in afar], away, sem, src[0], land)]
-              + [([cores[o]], _near(core, cores[o], away, topo)[:2], sem, src[0], land) for o in others if o not in afar])
+        far = [([cores[o] for o in afar], away, sem, src[0], land)]
+        near = [([cores[o]], _near(core, cores[o], away, topo)[:2 if t else len(away)], sem, src[0], land) for o in others if o not in afar]
+        for call in ([far + near] if t else [far, near]):
+            fused([src], call)
 
-    def score_count():
-        return sum(len(away) if s in afar else 2 for s in others)
+    def score_count(t):
+        return sum(len(away) if s in afar or t == 0 else 2 for s in others)
 
     def delta_count(s):
-        direct = s // HALF == me // HALF
-        scales = _mask(s, me, _half(s // HALF, s), cores[s], cores, topo) if direct else _hand_mask(s, me, _helpers(s, cores, topo)[2], cores, topo)
-        codes = _hand_mask(s, me, _helpers(s, cores, topo)[me // HALF], cores, topo)
-        return len(codes) + len(scales)
+        return 2 + (_sent(s, "scale", me, cores, topo) if s // HALF == me // HALF else 2)
 
-    QB = me % 4
-    DB = QB + 1 if QB < 3 else 2
-    CLASH = r % 4 == 0
+    lay = _blocks(me)
+    QB, DB = lay.index("R"), lay.index("D")
+    moves, ccol = _fetch(r)
 
     load("s", w("PT", 128 * DB, 128 * DB + 128), T.pd[:, :])
     load("y", w("PT", 128 * QB, 128 * QB + 128), T.pr[:, :])
@@ -334,63 +361,53 @@ def rank_program(g, core, T, topo):
     load("s", w("z_W", 0, 512), T.ws[:, :])
     cw = w("c_W", 0, 512)
     load("y", (cw[0].bitcast(dt.uint8), cw[1]), T.wc[:, :])
-    load("y", w("UB", 0, 512), T.u[:, :])
-    load("y", w("VB", 0, 512), T.v[:, :])
 
     TMP = [0]
     def ftmp(n):
         a = TMP[0]
         TMP[0] += n
-        return w("TMPF", a, a + n)
-    kt, ioi, mp = w("KTB", 0, 64), w("IOI", 0, 64), w("MAP", 0, 64)
-    fnat, fbl, frg, fsh, fsn, fout, fr2, fc1, f1, fa, fb, fh, fkp, ktf, fm = [ftmp(n) for n in (16, 4, 4, 4, 4, 16, 2, 16, 64, 2, 2, 2, 32, 32, 64)]
-    iota(w("PI", 0, 1), [[0, 1]], 0, 1, small=False)
+        return w("TMPF", a, a + n) + (a,)
+    fnat, fh, frg, fbl, flv, fkp = [ftmp(n) for n in (16, 4, 8, 8, 4, 32)]
     fill(w("ONE", 0, 520), 1.0)
-    iota(fnat, [[1, 8], [128, 2]])
-    iota(fbl, [[4, 2], [0, 2]])
-    sa(w("UV", 32, 512), w("ONE", 0, 480), 0.0)
-    sa(w("ZB", 0, 512), w("ONE", 0, 512), 0.0)
+    iota(w("PI", 0, 1), [[0, 1]], 0, 1, small=False)
+    iota(fnat, [[1, 2], [2, 4], [128, 2]])
+    iota(fh, [[1, 2], [0, 2]])
+    eb, one = w("EB", 0, 520), w("ONE", 0, 520)
+    run("g", lambda: g.affine_select(eb[0], one[0], [[-1, 520]], A.is_equal, 0.0, 4, 4), [one], [eb])
+    iota(frg, [[2, 4], [0, 2]])
+    iota(w("XI", 0, 8), [[32, 2], [64, 2], [0, 2]], 0, 1, small=False)
+    iota(w("RST", 0, 128), [[0, 2], [1, 64]])
+    sfill("UV", 32, 512, 0.0)
 
     def col(j):
         return w("FC", j, j + 1)
-    P16, P31, KK, QQ, B2, B3, Q0, Q1, M, ODD, B0, B1, K1, P8, K2 = range(15)
-    for j, (sh, an) in enumerate(((0, 15), (0, 31), (2, 3), (5, 3), (2, 1), (3, 1), (5, 1), (6, 1), (0, 3), (4, 1), (0, 1), (1, 1), (1, 7), (0, 7), (2, 7))):
-        o, i = w("INTC", j, j + 1), w("PI", 0, 1)
+    P16, P31, KK, QQ, B2, B3, Q1, K2, P8, M, B0, B1, K1 = range(13)
+    FIELD = ((0, 15), (0, 31), (2, 3), (5, 3), (2, 1), (3, 1), (6, 1), (2, 7), (0, 7), (0, 3), (0, 1), (1, 1), (1, 3))
+
+    def field(j):
+        o, i, (sh, an) = w("INTC", j, j + 1), w("PI", 0, 1), FIELD[j]
         if sh:
             ts(o, i, sh, A.arith_shift_right, an, A.bitwise_and)
         else:
             ts(o, i, an, A.bitwise_and)
-    C8P, CX, CSN, C16, CW2, CNX, CND, KK4, COUT, KR, SHF, PC, PC3, VP, VD, OP, C1P, MK1, SU, Y0, Y2 = range(16, 37)
-    fill(w("SEG", 0, 64), 1.0)
-    cp("v", w("FC", 0, 15), w("INTC", 0, 15))
-    fill(w("SEG", 32, 33), 0.0)
-    for h in range(2):
-        fill(lst("ac", 2, 2 * h), h)
-    eb, one = w("EB", 0, 520), w("ONE", 0, 520)
-    run("g", lambda: g.affine_select(eb[0], one[0], [[-1, 520]], A.is_equal, 0.0, 4, 4), [one], [eb])
-    iota(fsh, [[0, 2], [16, 2]])
-    iota(frg, [[1, 2], [0, 2]])
-    iota(fsn, [[2, 4]])
-    iota(fr2, [[4, 2]])
-    iota(w("MT", 0, 64), [[0, 16], [1, 4]])
-    scan(ioi, w("SEG", 0, 64), w("ONE", 0, 64))
-    ts(col(C8P), col(P16), 8.0, A.mult)
-    ts(col(KK4), col(KK), 4.0, A.add)
-    ts(ioi, ioi, -1.0, A.add)
-    tt(col(CNX), col(B2), col(Q0), A.not_equal)
-    tt(col(CND), col(B3), col(Q1), A.not_equal)
-    ts(lst("nat", 16), fnat, col(C8P), A.add)
-    for h in range(2):
-        sa(w("KTB", 32 * h, 32 * h + 32), w("ONE", 0, 32), 0.0, col(KK4 if h else KK))
-    sa(f1, kt, 32.0)
-    sa(col(C16), col(ODD), 16.0)
-    sa(w("NB", 0, 520), eb, -1.0)
+    C8P, CA, CB, CQ, SHF, PC, PC3, VP, VD, OP, C1P, MK1, SU, Y2, Y3, PP, PD, P3, VPB, VDB, W0, W1, W2 = range(16, 39)
+    for j in range(M):
+        field(j)
+    cp("v", w("FC", 0, M), w("INTC", 0, M))
 
+    turn = 0
     for b in range(4):
-        if b not in (QB, DB):
-            cp("v", w("PT", 128 * b, 128 * b + 128), w("PT", 128 * DB, 128 * DB + 128))
-    quant("S", 0, w("UV", 0, 512))
-    quant("PB0", OLD, w("PT", 0, 512))
+        a, d = 128 * b, 128 * DB
+        for o0, o1, i0 in {"R": [], "D": [(0, 128, 0)] if b != DB else [], "S": [(4, 128, 0), (0, 4, 124)]}[lay[b]]:
+            cp("vs"[turn % 2], w("PT", a + o0, a + o1), w("PT", d + i0, d + i0 + o1 - o0))
+            turn += 1
+    quant("S", 0, ("UV", 0), 128)
+    quant("PB0", OLD, ("PT", 0), 128)
+    sa(col(CA), col(B2), float(r), col(B3))
+    sa(col(CB), col(Q1), float(r), col(KK))
+    sa(col(CQ), col(QQ), -2.0, 8.0)
+    sa(col(C8P), col(P16), 8.0)
+    ts(col(SHF), col(K2), float(8 - r), A.is_ge, col(Q1), A.mult)
 
     def scores(t):
         sc, n = "SC%d" % t, "N%d" % t
@@ -398,335 +415,281 @@ def rank_program(g, core, T, topo):
         cp("s", w(sc, 0, 1), w("ps", 4 + t, 5 + t))
         send_scores(t)
         run("y", lambda: g.sync.dma_start(T[n][:, me:me + 1], T[sc][:, 0:1]), [w(sc, 0, 1)], [w(n, me, me + 1)], dma=True)
-        arrive([w(n, a, b) for a, b in ((0, me), (me + 1, 8)) if b > a], "sc%d" % t, score_count())
+        arrive([w(n, a, b) for a, b in ((0, me), (me + 1, 8)) if b > a], "sc%d" % t, score_count(t))
 
     scores(0)
-    own16, c1, sq = w("OWN", 0, 16), w("C1", 0, 16), w("SQ", 0, 4)
-    iota(sq, [[16, 4]])
-    iota(own16, [[16, 16]])
-    iota(fc1, [[4, 8], [0, 2]])
-    iota(w("VALS", 0, 32), [[0, 8], [1, 4]])
+    ts(w("NB", 0, 520), eb, -1.0, A.mult)
+    iota(w("MT", 0, 128), [[0, 32], [1, 4]])
     iota(fkp, [[8, 32]], -MID)
-    iota(fm, [[16, 2], [0, 2], [1, 16]])
-    iota(w("WT", 0, 128), [[16, 4], [0, 2], [1, 16]])
-    iota(fout, [[2, 16]])
+    iota(flv, [[256, 4]])
+    iota(w("SQ", 0, 2), [[16, 2]])
+    iota(w("MASK", 0, 64), [[16, 2], [0, 2], [1, 16]])
+    iota(w("MASK", 64, 128), [[16, 2], [0, 2], [1, 16]], -1)
+    iota(w("WT", 0, 128), [[32, 4], [0, 2], [2, 16]], -63)
+    iota(w("EM", 0, 32), [[0, 2], [1, 2], [0, 8]])
 
-    bi, shi, sni = w("TMPI", 12, 16), w("TMPI", 0, 4), w("TMPI", 4, 8)
-    t0, b0, b1, hh = [w("TMPI", a, a + 2) for a in (144, 146, 148, 150)]
-    kti, k0 = w("TMPI", 80, 112), ktf[1][0][1]
-    ts(col(KR), col(Q1), float(r), A.mult, col(KK), A.add)
-    ts(bi, fbl, col(QQ), A.add, float(8 - r), A.add)
-    ts(shi, fsh, col(P16), A.add)
-    ts(t0, fr2, col(KR), A.add)
-    ts(col(CX), col(CND), 2.0, A.mult, col(CNX), A.add)
-    ts(col(CSN), col(B2), float(r), A.mult, col(B3), A.add)
-    ts(bi, bi, 7, A.bitwise_and)
-    for h in range(2):
-        n = min(max(r - 4 * h, 0), 4)
-        if n:
-            v = w("TMPI", 2 * h, 2 * h + 2, 1, 0, 32 * n)
-            ts(v, v, 31.0, A.add)
-    ts(t0, t0, 7, A.bitwise_and)
-    ts(col(CX), col(CX), 2.0, A.mult)
-    ts(sni, fsn, col(CSN), A.add)
-    ts(lst("bl", 4, 4), bi, 8.0 if CLASH else 0.0, A.add)
+    ti, b1, b2, xi = w("TMPI", 0, 12), w("TMPI", 16, 28), w("TMPI", 32, 44), w("XI", 0, 8)
+    ts(w("TMPI", 0, 8), frg, col(CA), A.add, col(CQ), A.add)
+    ts(w("TMPI", 8, 10), part(frg, 0, 8, step=4), col(CB), A.add, col(CQ), A.add)
+    ts(w("TMPI", 10, 12), w("ONE", 0, 2), col(P8), A.mult, col(CQ), A.add)
+    ts(lst("nat", 16), fnat, col(C8P), A.add)
+    weave([lambda b=b: quant("E", 128 * b, ("EB", 4 - b), 128) for b in range(4)],
+          [lambda: ts(ti, ti, 7, A.bitwise_and), lambda: ts(b1, ti, 1, A.arith_shift_right, 1, A.bitwise_and), lambda: tt(b1, b1, b2, A.subtract),
+           lambda: ts(b1, b1, 2.0, A.mult)],
+          [lambda: ts(xi, xi, 127, A.bitwise_and), lambda: ts(b2, ti, 2, A.arith_shift_right)])
+    sfill("AV1", 0, 16, 0.0)
+    for q in range(4):
+        sa(part(fbl, 0, 4, 32 * q, 32 * q + 32), part(fh, 0, 4, 32 * q, 32 * q + 32), 1.0, 2.0 * q)
+        sa(part(fbl, 4, 8, 32 * q, 32 * q + 32), part(fh, 0, 4, 32 * q, 32 * q + 32), float(ccol[2 * q + 1] - ccol[2 * q]), float(ccol[2 * q]))
+    sa(col(W0), col(P31), 1.0, float(LAP))
+    sa(col(W1), col(P31), 1.0, OLD + 32.0 * QB)
+    sa(col(W2), col(P31), -1.0, 31.0 - OLD - 32.0 * QB)
+    sa(col(VP), col(K2), 8.0, 16.0)
+    sa(col(PC), col(P31), 8.0, -MID - 0.5)
+    sa(col(PC3), col(P31), 8.0, 7.25 - MID)
+    sa(col(VPB), col(Q1), 32.0, col(W0))
+    sa(col(OP), col(Q1), 32.0 * (DB - QB), col(W1))
+    sa(col(C1P), col(Q1), 64.0 - 32.0 * (DB - QB), col(W2))
+    sfill("DMP", 0, 128, -1.0)
+    if moves:
+        sfill("N0", 8, 32, 0.0)
+    sfill("DK", 1, 31, -8.0)
+    sfill("DK", 32, 64, 0.0)
+    sfill("MK", 32, 64, 1.0)
+    sa(w("DK", 0, 1), col(SHF), 256.0, -8.0)
+    sa(w("DK", 31, 32), col(SHF), -8.0, float(248 + r - MID))
 
-    quant("X", 0, w("XB", 0, 1024))
-    ts(shi, shi, 31, A.bitwise_and)
-    ts(b0, t0, 1, A.bitwise_and)
-    pick("D0", 0, 256, "X", 256, ("LST", LISTS["nat"]))
-    tt(mp, ioi, f1, A.add)
-    for h in range(2):
-        mm(4 + h, 128, "D0", 128 * h, "S", 0)
-    for b in range(4):
-        mm(b, 256, "W", 128 * b, "D0", 0)
-    for b in range(4):
-        quant("E", 512 + 128 * b, w("NB", 4 - b, 516 - b))
+    quant("X", 0, ("XB", 0), 256)
+    tt(ti, ti, b1, A.add)
+    pick("XA", 0, 256, "X", 256, ("LST", LISTS["nat"]))
 
-    def relu(tile, b, cols, bk):
-        o, i = w(tile, b, 4 * cols, 4), bank(bk, cols)
+    def with_u(v, bk):
+        for h in range(2):
+            mm(bk + h, 128, "XA", 256 * v + 128 * h, "S", 0)
+        for t in range(v, R):
+            cp("s" if v else "v", w("AV%d" % t, v, 8, 4) if t else w("ACOL", 0, 2), w("ps", 512 * bk + t, 512 * bk + 1024, 512))
+
+    def with_w(v):
+        for b in range(4):
+            mm(b, 256, "W", 128 * b, "XA", 256 * v)
+
+    def relu(b):
+        o, i = w("HT", b, 1024, 4), bank(b, 256)
         run("s", lambda: g.scalar.activation(o[0], i[0], F.Relu, scale=0.0625), [i], [o])
 
-    cp("s", w("ACOL", 0, 2), w("ps", 2048, 3072, 512))
-    sa(w("DMP", 0, 64), mp, 0.0, -1.0)
-    cp("s", w("DMP", 31, 64, 32), w("MAP", 31, 64, 32))
-    for b in range(4):
-        relu("HT0", b, 256, b)
-    for b in range(4):
-        mm(4 + b, 256, "E", 512 + 128 * b, "D0", 0, True, False)
-    ts(lst("rg", 4), frg, col(CX), A.add)
-    ts(sni, sni, 7, A.bitwise_and)
-    cp("v", lst("sh", 2), w("TMPI", 0, 2))
-    ts(lst("sh", 2, 2), w("TMPI", 2, 4), 32.0, A.add)
-    ts(lst("bl", 4), fbl, col(QQ), A.add)
-    ts(lst("sn", 4), sni, 4.0, A.mult, col(M), A.add)
-    ts(w("LM", 0, 64), ioi, col(P31), A.is_lt, TINY, A.mult)
-    for b in range(4):
-        quant("E", 128 * b, w("EB", 4 - b, 516 - b))
+    def unpack(v, new):
+        for b in range(4):
+            mm(4 + b, 256, "E", (0 if new else 512) + 128 * b, "XA", 256 * (v + new), not new, bool(new))
 
-    def arow():
-        cp("v", w("RA", 0, 64), ind(w("ACOL", 0, 2), lst("ac", 4)))
+    def deltas(engines):
+        for b in range(4):
+            cp(engines[b], w("DT", b, 1024, 4), bank(4 + b, 256))
 
-    def differences(name, c, src):
-        tt(w(name, c, c + 63), w(src, 0, 63), w(src, 1, 64), A.subtract)
-        cp("s", w(name, c + 31, c + 64, 32), w(src, 31, 64, 32))
+    def arow(t):
+        cp("v", w("RA", 0, 64), ind(w("ACOL", 8 * t, 8 * t + 2), lst("ac", 4)))
 
-    x1 = w("TMPI", 16, 80)
-    gaps = [
-        lambda: ts(col(SHF), col(K2), float(8 - r), A.is_ge, 31.0, A.mult),
-        lambda: ts(b1, t0, 1, A.arith_shift_right, 1, A.bitwise_and),
-        lambda: ts(col(SHF), col(SHF), col(Q1), A.mult),
-        lambda: ts(fa, b0, col(Q0), A.not_equal, 2.0, A.mult),
-        lambda: ts(kti, w("IOI", 0, 32), col(SHF), A.add),
-        lambda: ts(fb, b1, col(Q1), A.not_equal, 4.0, A.mult),
-        lambda: ts(hh, t0, 2, A.arith_shift_right, 1, A.bitwise_and),
-        lambda: ts(kti, kti, 31, A.bitwise_and),
-        lambda: tt(fa, fa, fb, A.add),
-        lambda: ts(fh, hh, 1.0, A.mult),
-        lambda: ts(ktf, kti, 8.0, A.mult, float(r - MID), A.add),
-        lambda: ts(x1, ioi, col(C16), A.add),
-        lambda: tt(fa, fa, fh, A.add),
-        lambda: tt(w("DK", 0, 31), w("TMPF", k0, k0 + 31), w("TMPF", k0 + 1, k0 + 32), A.subtract),
-        lambda: cp("v", w("DK", 31, 32), w("TMPF", k0 + 31, k0 + 32)),
-        lambda: cp("v", lst("r2", 2), fa)]
-    after = [
-        lambda: ts(x1, x1, 31, A.bitwise_and),
-        lambda: tt(col(CNX), col(B0), col(ODD), A.not_equal),
-        lambda: ts(sq, sq, col(P16), A.add, 32.0 * QB, A.add),
-        lambda: tt(w("OFR", 0, 64), f1, x1, A.add),
-        lambda: ts(col(CW2), col(CNX), 16.0, A.mult),
-        lambda: ts(col(Y0), col(B2), 4.0 * ((2 * r) % 8 - r), A.mult, col(M), A.add),
-        lambda: differences("DF", 0, "OFR"),
-        lambda: ts(lst("w2", 1), col(K1), 32.0, A.mult, col(CW2), A.add),
-        lambda: ts(w("SQ", 2, 4), w("SQ", 2, 4), 32.0 * (DB - QB - 1) if DB < QB else 0.0, A.add),
-        lambda: ts(lst("ow", 1), col(Y0), 4.0 * r, A.add),
-        lambda: ts(own16, own16, col(P16), A.add),
-        lambda: quant("D0", 256, w("ZB", 0, 512)),
-        lambda: cp("v", lst("pp", 4), sq),
-        lambda: tt(c1, fc1, own16, A.subtract)]
+    for b in range(4):
+        quant("E", 512 + 128 * b, ("NB", 4 - b), 128)
+    cp("v", lst("rg", 12), ti)
+    cp("v", lst("bl", 8), fbl)
+    cp("v", lst("ac", 4), fh)
+    ts(w("XL", 0, 8, 2), w("XI", 0, 8, 2), 0.0, A.add)
+    ts(w("XL", 1, 8, 2), w("XI", 1, 8, 2), 128.0, A.add)
+    ts(w("RST", 0, 128), w("RST", 0, 128), col(P31), A.not_equal)
+    with_u(0, 4)
+    with_w(0)
+    for b in range(4):
+        relu(b)
+    unpack(0, 0)
+    arow(0)
+    cp("v", w("RG", 0, 128), ind(w("XL", 0, 8), lst("rg", 8)))
+    tr(w("MM", 0, 128), w("RG", 0, 128))
+    sfill("TBL", 0, LAP, 1.0)
+    sfill("TBL", LAP, 144, 0.0)
+    if moves:
+        sfill("N1", 8, 32, 0.0)
+        sfill("N2", 8, 32, 0.0)
+    quant("XA", 256, ("HT", 0), 256)
+    unpack(0, 1)
+    cp("v", w("DMP", 31, 128, 32), w("MM", 31, 128, 32))
+    deltas("ssss")
+    with_u(1, 0)
+    with_w(1)
+    load("y", w("UB", 0, 512), T.u[:, :], [w("N0", 0, 8)])
+    load("y", w("VB", 0, 512), T.v[:, :])
+
     owner = [
-        lambda: ts(col(VP), col(Q1), 32.0, A.mult, float(LAP), A.add),
+        lambda: field(M), lambda: field(B0), lambda: field(B1), lambda: field(K1),
         lambda: ts(col(VD), col(K2), 7.0, A.is_equal, -72.0, A.mult),
-        lambda: ts(c1, c1, 256.0, A.add),
-        lambda: ts(col(SU), col(K2), 8.0, A.mult, 16.0, A.add),
-        lambda: ts(col(OP), col(Q1), 32.0 * (DB - QB), A.mult, OLD + 32.0 * QB, A.add),
-        lambda: tt(w("VPB", 0, 1), col(VP), col(P31), A.add),
-        lambda: tt(col(VD), col(VD), col(M), A.add),
-        lambda: ts(col(C1P), col(Q1), 64.0, A.mult, -1.0, A.add),
-        lambda: tt(col(OP), col(OP), col(P31), A.add),
-        lambda: tt(col(VD), col(VD), col(SU), A.add),
-        lambda: ts(col(SU), col(Q1), 4.0, A.mult),
-        lambda: ts(col(PC), col(P31), 8.0, A.mult, -MID - 0.5, A.add),
-        lambda: tt(col(C1P), col(C1P), col(OP), A.subtract),
-        lambda: tt(w("VDB", 0, 1), col(VD), col(SU), A.add),
-        lambda: ts(col(PC3), col(P31), 8.0, A.mult, 7.5 - MID, A.add),
-        lambda: fill(w("TBL", 0, LAP), 1.0),
-        lambda: fill(w("TBL", LAP, 144), 0.0),
-        lambda: ts(w("MASK", 0, 64), fm, col(P31), A.is_equal),
-        lambda: ts(col(Y2), col(K1), float(QB), A.is_equal, -2.0, A.mult),
-        lambda: cp("v", lst("sl", 1), col(M)),
+        lambda: cp("v", w("FC", M, K1 + 1), w("INTC", M, K1 + 1)),
+        lambda: ts(lst("pp", 2), w("SQ", 0, 2), col(P16), A.add, 32.0 * QB, A.add),
+        lambda: ts(lst("pp", 2, 2), w("SQ", 0, 2), col(P16), A.add, 32.0 * DB, A.add),
+        lambda: ts(col(VD), col(VD), col(M), A.add, col(VP), A.add),
+        lambda: ts(w("MASK", 0, 128), w("MASK", 0, 128), col(P31), A.is_equal),
+        lambda: ts(col(Y2), col(K1), float(QB), A.is_equal, -4.0, A.mult),
+        lambda: (ts(col(Y3), col(K1), 3.0, A.is_ge, 2.0, A.mult) if QB == 0 else ts(col(Y3), col(K1), float(lay.count("S")), A.is_lt, 2.0, A.mult)),
+        lambda: ts(col(VDB), col(Q1), 4.0, A.mult, col(VD), A.add),
         lambda: pick("LA0", LAP, 64, "PB0", 128, ("LST", LISTS["pp"]), OLD),
-        lambda: ts(lst("se", 1), col(Y2), col(B0), A.add, 2.0, A.add)]
-
-    def gap(n=1):
-        for i in range(n):
-            if gaps:
-                gaps.pop(0)()
-
-    arow()
-    gap(8)
-    quant("NX", 0, w("HT0", 0, 1024))
-    gap(8)
-    for b in range(4):
-        mm(4 + b, 256, "E", 128 * b, "NX", 0, False, True)
-    for b in range(4):
-        cp("s", w("DT0", b, 1024, 4), bank(4 + b, 256))
-    gaps.extend(after)
+        lambda: ts(col(Y2), col(Y2), col(Y3), A.add, col(B0), A.add),
+        lambda: ts(lst("sl", 1), col(B1), 4.0, A.mult, col(B0), A.add),
+        lambda: ts(w("EM", 0, 32), w("EM", 0, 32), col(B0), A.is_equal),
+        lambda: ts(lst("se", 1), col(Y2), 4.0, A.add)]
 
     def choose(t):
         n = "N%d" % t
-        if CLASH:
-            for h, q in enumerate("vs" if t else "vv"):
-                cp(q, w(n, 8, 16, 1, 64 * h, 64 * h + 64), w(n, 0, 8, 1, 64 - 64 * h, 128 - 64 * h))
-        rb, tb = w("RB", 0, 128), w("TB", 0, 128)
-        tt(w("RB", 0, 64), ind(w(n, 0, 8), lst("bl", 4)), w("RA", 0, 64), A.subtract)
-        cp("s" if t else "v", w("RB", 64, 128), ind(w(n, 0, 16 if CLASH else 8), lst("bl", 4, 4)))
-        gap(2)
-        tr(tb, rb)
-        gap(2)
-        st, rr, g1, g2, cc = [w(x, 0, 64) for x in ("ST", "RR", "G1", "G2", "CC")]
-        tt(st, ind(w("TB", 64, 128), lst("sh", 4)), w("TB", 0, 64), A.add)
-        gap(2)
-        tr(rr, st)
-        gap(2)
-        tt(g1, st, rr, A.subtract)
-        gap(2)
-        tt(g2, g1, w("LM", 0, 64), A.is_lt)
-        gap(2)
-        scan(cc, w("SEG", 0, 64), g2)
-        gap(2)
+        rb, rr, st = w("RB", 0, 64), w("RR", 0, 64), w("ST", 0, 64)
+        tt(rb, ind(w(n, 0, 8), lst("bl", 4)), w("RA", 0, 64), A.subtract)
+        for j, (to, frm, k) in enumerate(moves):
+            cp("v" if t == 0 or j == 2 else "s", w(n, 8 + 8 * j, 16 + 8 * j, 1, to, to + k), w(n, 0, 8, 1, frm, frm + k))
+        tt(rr, ind(w(n, 0, 32 if moves else 8), lst("bl", 4, 4)), rb, A.add)
+        tr(st, rr)
+        for h in range(2):
+            a, z = w("ST", 32 * h, 32 * h + 32), w("RR", 32 * h, 32 * h + 1)
+            ts(w("EL", 64 * h, 64 * h + 32), a, z, A.is_equal, -1.0, A.mult)
+            ts(w("EL", 64 * h + 32, 64 * h + 64), a, z, A.is_le)
+        scan(w("CC", 0, 128), w("RST", 0, 128), w("EL", 0, 128))
+        for h in range(2):
+            scan(w("CC", 128, 256, 1, 64 * h, 64 * h + 64), w("RST", 0, 128, 1, 64 - 64 * h, 128 - 64 * h), w("EL", 0, 128, 1, 64 - 64 * h, 128 - 64 * h))
         for q in range(4):
-            cp("vs"[q % 2], w("XR", 2, 4, 1, 32 * q, 32 * q + 32), w("CC", 31, 64, 32, 32 * (q ^ 1), 32 * (q ^ 1) + 32))
-        cp("v", w("XR", 0, 2), w("CC", 31, 64, 32))
-        cp("v", w("XR", 4, 8, 1, 0, 64), w("XR", 0, 4, 1, 64, 128))
-        cp("s", w("XR", 4, 8, 1, 64, 128), w("XR", 0, 4, 1, 0, 64))
-        gap(len(gaps))
-        rg, m, xr = w("RG", 0, 64), w("MM", 0, 64), w("XR", 0, 8)
-        wk = "WK%d" % t
-        tt(rg, ind(xr, lst("rg", 4)), w("MT", 0, 64), A.not_equal)
+            cp("vs"[q % 2], w("XR", 4, 8, 1, 32 * q, 32 * q + 32), w("CC", 63, 256, 64, 32 * ((q + 1) % 4), 32 * ((q + 1) % 4) + 32))
+        cp("v", w("XR", 0, 4), w("CC", 63, 256, 64))
+        if t == 0:
+            quant("DL", 0, ("DT", 0), 256)
+        rg, m, xr = w("RG", 0, 128), w("MM", 0, 128), w("XR", 0, 8)
+        wk, sn, la, kx = "WK%d" % t, "SN%d" % t, "LA%d" % t, "KX%d" % t
         tt(w("RGK", 0, 32), ind(xr, lst("r2", 2)), w("MT", 0, 32), A.not_equal)
-        tr(m, rg)
+        tt(rg, ind(xr, lst("rg", 8)), w("MT", 0, 128), A.not_equal)
         tr(w("MK", 0, 32), w("RGK", 0, 32))
-        scan(w("SCN", 0, 64), m, w("DMP", 0, 64))
-        scan(w("SK", 0, 32), w("MK", 0, 32), w("DK", 0, 32))
-        cp("v", w("L1U", 0, 2), w("SCN", 31, 64, 32))
-        ts(w("KB", 0, 32), w("ONE", 0, 32), w("SK", 31, 32), A.mult)
-        dc, sn, la, kx = "DC%d" % t, "SN%d" % t, "LA%d" % t, "KX%d" % t
-        if t == 0:
-            quant("DL", 0, w("DT0", 0, 1024))
-            tr(w(wk, 0, 32), w("KB", 0, 32))
-        pick(dc, 0, 32, "DL", 256 + 32 * t, ("L1U", 0))
-        if t:
-            tr(w(wk, 0, 32), w("KB", 0, 32))
+        tr(m, rg)
+        scan(w("SK", 0, 64), w("MK", 0, 64), w("DK", 0, 64))
+        scan(w("SCN", 0, 128), m, w("DMP", 0, 128))
+        tr(w(wk, 0, 32), w("SK", 32, 64))
+        cp("v", w("L", 0, 4), w("SCN", 31, 128, 32))
+        pick(sn, 0, 64, "DL", 256 * (t + 1), ("L", 0))
+        hs, a = T.sem["hs%d" % t], 32 * (1 - me // HALF)
 
-        def keys(part):
-            fused([w(wk, 0, 32)], [([cores[o]], _list_mask(me, o, cores, topo), T.sem["ls%d" % t], T[wk][:, 4 * o:4 * o + 4],
-                                    T[kx][:, 32 + 4 * pos(me, o):36 + 4 * pos(me, o)]) for o in part])
-        parts = _calls(me, cores, topo)
-        keys(parts[0])
-        scan(w("SCN", 64, 128), m, w("DF", 0, 64))
-        pick(sn, 0, 64, dc, 32, ("LST", LISTS["sn"]))
-        hs, close = T.sem["hs%d" % t], _near(core, helpers[0], away, topo)
-        fused([w("c_" + sn, 0, 64)], [([helpers[h]], close[NHAND * h:NHAND * h + NHAND], hs, T["c_" + sn][:, 32 * h:32 * h + 32].bitcast(dt.uint8),
-                                       T["c_HC%d" % t][:, 0:32].bitcast(dt.uint8)) for h in range(2)])
-        a = 32 * (1 - me // HALF)
-        fused([w("z_" + sn, 0, 64)], [([helpers[2]], close[:2 * NHAND], hs, T["z_" + sn][:, a:a + 32], T["z_HZ%d" % t][:, 0:32])])
-        keys(parts[1])
-        fused([w("z_" + sn, 0, 64)], [([cores[o]], _mask(me, o, mine, core, cores, topo), T.sem["dl%d" % t], T["z_" + sn][:, 8 * o:8 * o + 8],
-                                       T["z_" + la][:, 16 + 8 * pos(me, o):24 + 8 * pos(me, o)]) for o in mine])
+        def transfer(kind, o, e):
+            if kind == "key":
+                return ([cores[o]], e, T.sem["ls%d" % t], T[wk][:, 4 * o:4 * o + 4], T[kx][:, 32 + 4 * pos(me, o):36 + 4 * pos(me, o)])
+            if kind == "scale":
+                return ([cores[o]], e, T.sem["dl%d" % t], T["z_" + sn][:, 8 * o:8 * o + 8], T["z_" + la][:, 16 + 8 * pos(me, o):24 + 8 * pos(me, o)])
+            if kind == "code":
+                return ([helpers[o]], e, hs, T["c_" + sn][:, 32 * o:32 * o + 32].bitcast(dt.uint8), T["c_HC%d" % t][:, 0:32].bitcast(dt.uint8))
+            return ([helpers[o]], e, hs, T["z_" + sn][:, a:a + 32], T["z_HZ%d" % t][:, 0:32])
+        src = {"key": w(wk, 0, 32), "scale": w("z_" + sn, 0, 64), "code": w("c_" + sn, 0, 64), "hand": w("z_" + sn, 0, 64)}
+        for call in _calls(me, cores, topo):
+            fused([src[x[0]] for x in call], [transfer(*x) for x in call])
         run("y", lambda: g.sync.dma_start(T[kx][:, 60:64], T[wk][:, 4 * me:4 * me + 4]), [w(wk, 4 * me, 4 * me + 4)], [w(kx, 60, 64)], dma=True)
-        arrive([w(kx, 32, 60)], "ls%d" % t, sum(len(_list_mask(s, me, cores, topo)) for s in others))
+        arrive([w(kx, 32, 60)], "ls%d" % t, sum(_sent(s, "key", me, cores, topo) for s in others))
         arrive([w("c_" + la, 16, 72), w("z_" + la, 16, 72)], "dl%d" % t, sum(delta_count(s) for s in others))
-        inv, vals, l2 = w("INV%d" % t, 0, 256), w("VALS", 0, 32), w("L2U", 0, 2)
-        sa(inv, w("EB", 0, 256), 0.0, 8.0)
-        if t == 0:
-            sa(w("K4", 0, 64), kt, 4.0, 256.0)
-            sa(w("HT1", 128, 512), w("ONE", 0, 384), 0.0)
-            for k in range(R):
-                sa(w("KX%d" % k, 0, 32), fkp, 1.0, -0.5)
-            sa(w("SEGG", 0, 192), w("ONE", 0, 192), 0.0, 1.0)
-            sa(w("SEGH", 0, 320), w("ONE", 0, 320), 0.0, 1.0)
-            sa(col(COUT), col(P8), 32.0, col(B3))
-            sa(w("SEGG", 0, 192, 64), w("ONE", 0, 3), 0.0)
-            sa(w("SEGH", 0, 320, 32), w("ONE", 0, 10), 0.0)
-        cp("v", l2, w("SCN", 95, 128, 32))
-        run("v", lambda: g.vector.tensor_copy(inv[0].indirect(l2[0]), vals[0]), [vals, l2], [inv])
-        pick(la, 0, 16, dc, 32, ("LST", LISTS["ow"]))
-        tr(w("INVT", 0, 256), inv)
 
     def advance(t):
-        d, dn, it = "D%d" % t, "D%d" % (t + 1), w("INVT", 0, 256)
-        pick(d, 256, 32, "NX", 256 + 32 * t, ("L1U", 0))
+        xl, la = w("XL", 0, 8), "LA%d" % t
+        if t == 0:
+            ts(lst("ow", 1), col(P8), 8.0 * me, A.add)
+            cp("v", lst("hh", 1), col(B2))
+            for h in range(2):
+                sa(w("LV", 4 * h, 4 * h + 4), flv, 1.0, w("XL", h, h + 1))
+            sfill("LV", 8, 16, 0.0)
+            sfill("MASK", 64, 96, 31.0, 16)
+        ts(w("U8", 0, 8), w("XR", 0, 8), 4.0, A.is_lt, 256.0, A.mult)
+        pick(la, 0, 16, "SN%d" % t, 64, ("LST", LISTS["ow"]))
         if t < R - 1:
             for b in range(4):
-                mm(b, 128, "W", 128 * b, d, 256)
-        wd, we, dls = w("WD", 0, 16), w("WE", 0, 16), w("DLS", 0, 16)
-        rg, rt, mask, u = w("RG", 0, 64), w("RT", 0, 64), w("UP", 0, 64), w("UP", 64, 128)
-        row = [lambda: cp("v", wd, ind(it, lst("w2", 1))), lambda: ts(we, wd, 8.0, A.not_equal), lambda: tt(wd, wd, c1, A.add),
-               lambda: tt(wd, wd, we, A.mult), lambda: tt(wd, wd, own16, A.add), lambda: cp("v", dls, wd)]
-        moved = [lambda: cp("v", rg, ind(w("XR", 0, 8), lst("rg", 4))), lambda: tr(rt, rg), lambda: ts(mask, rt, 4.0, A.is_lt),
-                 lambda: tt(u, rt, w("K4", 0, 64), A.add), lambda: tt(u, u, mp, A.subtract), lambda: tt(u, u, mask, A.mult)]
-        for i in range(6):
-            row[i]()
-            if t < R - 1:
-                moved[i]()
-            if t == 0:
-                for f in owner[4 * i:4 * i + 4]:
-                    f()
+                relu(b)
+            unpack(t + 1, 0)
+        if t == 0:
+            for k in range(R):
+                sa(w("KX%d" % k, 0, 32), fkp, 1.0, -0.5)
+            sfill("SEGH", 0, 384, 1.0)
+            sfill("SEGH", 0, 256, 0.0, 64)
+            sfill("SEGH", 256, 384, 0.0, 32)
         if t < R - 1:
-            for b in range(4):
-                relu("HT1", b, 32, b)
-            tt(mp, mp, u, A.add)
-            quant("NX", 256 + 32 * t, w("HT1", 0, 512))
+            u = t + 1
+            chain = [lambda: tt(xl, xl, w("U8", 0, 8), A.add),
+                     lambda: tt(w("VM", 0, 16), ind(xl, lst("hh", 1)), w("LV", 0, 16), A.is_equal),
+                     lambda: tt(w("PV", 0, 8), w("VM", 0, 8), w("AV%d" % u, 0, 8), A.mult),
+                     lambda: (rsum(w("ACOL", 8 * u, 8 * u + 1), w("PV", 0, 4)), rsum(w("ACOL", 8 * u + 1, 8 * u + 2), w("PV", 4, 8))),
+                     lambda: arow(u)]
+            moved = [None, lambda: cp("v", w("MP", 0, 128), ind(xl, lst("rg", 8))), None, lambda: tr(w("MPT", 0, 128), w("MP", 0, 128))]
+            own = [lambda i=i: [f() for f in owner[4 * i:4 * i + 4]] for i in range(5)] if t == 0 else []
+            weave(chain, moved, own)
             if t == 0:
-                sa(w("K4", 0, 64), w("K4", 0, 64), 1.0, 32.0)
-                sa(w("DT1", 128, 512), w("ONE", 0, 384), 0.0)
+                ts(w("HT", 0, 1024), w("HT", 0, 1024), BIG, A.min)
+            quant("XA", 256 * (t + 2), ("HT", 0), 256)
+            unpack(t + 1, 1)
         else:
-            pick(dn, 0, 256, d, 288, ("DLS", 0))
-            ts(lst("out", 16), fout, col(COUT), A.add)
-            pick("FD", 0, 256, dn, 256, ("LST", LISTS["out"]))
+            tt(xl, xl, w("U8", 0, 8), A.add)
+            tt(w("FB", 0, 32), ind(xl, lst("fo", 2)), w("EM", 0, 32), A.mult)
+            tr(w("FT", 0, 32), w("FB", 0, 32))
+            tt(w("FO", 0, 16), w("FT", 0, 32, 2), w("FT", 1, 32, 2), A.add)
+            cp("v", w("OUT", 0, 16), w("FO", 0, 16))
+            pick("FD", 0, 256, "XA", 1024, ("OUT", 0))
             mm(4, 256, "U", 0, "FD", 0)
-            cp("s", w("YB", 0, 256), w("ps", 2048, 2304))
             fd = w("c_FD", 0, 256)
             store("y", T.oc[:, 0:1024], (fd[0].bitcast(dt.uint8), fd[1]))
-            store("y", T.y[:, 0:256], w("YB", 0, 256))
             for k in range(4):
                 store("y", T.osc[4 * k:4 * k + 4, 0:256], w("z_FD", 0, 256, 1, 32 * k, 32 * k + 4))
 
     def patch(t):
         la, kx, pb, pn, last = "LA%d" % t, "KX%d" % t, "PB%d" % t, "PB%d" % (t + 1), t == R - 1
+        pp, pd, p3 = col(PP), col(PD), col(P3)
         tr(w("KT", 0, 32), w(kx, 32, 64))
-        ts(w("GG", 0, 64), w(kx, 0, 64), col(PC), A.is_lt)
-        ts(w("GG", 128, 192), w(kx, 0, 64), col(PC3), A.is_lt)
-        ts(w("GG", 64, 128), w(kx, 0, 64), w("KT", 0, 1), A.is_lt)
-        scan(w("CN", 0, 192), w("SEGG", 0, 192), w("GG", 0, 192))
-        pp, pd, p3 = w("CN", 63, 64), w("CN", 127, 128), w("CN", 191, 192)
-        ts(w("HH", 0, 128), w("WT", 0, 128), pp, A.is_equal, w("VPB", 0, 1), A.mult)
-        ts(w("HH", 128, 256), w("WT", 0, 128), pd, A.is_equal, w("VDB", 0, 1), A.mult)
+        for j, (out, key) in enumerate(((pp, col(PC)), (p3, col(PC3)), (pd, w("KT", 0, 1)))):
+            o, i = w("GG", 64 * j, 64 * j + 64), w(kx, 0, 64)
+            run("s", lambda: g.scalar.activation(o[0], i[0], F.Sign, bias=key[0], scale=-1.0, accum_out=out[0]), [i, key], [o, out])
+        wide = 64 if last else 128
+        ts(w("HH", 0, 128), w("WT", 0, 128), pp, A.is_equal, col(VPB), A.mult)
         ts(col(MK1), p3, pp, A.subtract, 1.0, A.is_gt)
-        tr(w("HHT", 0, 256), w("HH", 0, 256))
-        ts(col(SU), p3, col(C1P), A.add, col(MK1), A.mult)
+        ts(col(SU), p3, 0.5, A.mult, col(C1P), A.add)
+        ts(w("HH", 128, 256), w("WT", 0, 128), pd, A.is_equal, col(VDB), A.mult)
+        tr(w("HHT", 0, 256, 2), w("HH", 0, 128))
+        ts(col(SU), col(SU), col(MK1), A.mult, col(OP), A.add)
+        tr(w("HHT", 1, 256, 2), w("HH", 128, 256))
+        ts(w("HH", 256, 256 + wide), w("MASK", 0, wide), col(SU), A.mult)
         scan(w("SH", 0, 256), w("SEGH", 0, 256), w("HHT", 0, 256))
-        ts(col(SU), col(SU), col(OP), A.add)
-        tt(w("ALF", 0, 4), w("SH", 31, 128, 32), w("SH", 159, 256, 32), A.add)
-        ts(w("HH", 256, 320), w("MASK", 0, 64), col(SU), A.mult)
+        tr(w("HHT", 256, 256 + wide), w("HH", 256, 256 + wide))
         for k in range(2):
             for h in range(2):
-                cp("v", w("AL", 4 * k, 4 * k + 4, 1, 64 * h, 64 * h + 64), w("ALF", 0, 4, 1, 64 * k, 64 * k + 64))
+                cp("v", w("AL", 4 * k, 4 * k + 4, 1, 64 * h, 64 * h + 64), w("SH", 63, 256, 64, 64 * k, 64 * k + 64))
+        scan(w("SH", 256, 256 + wide), w("SEGH", 256, 256 + wide), w("HHT", 256, 256 + wide))
         ms, tb, al = w("MS", 0, 128), w("TBL", 0, 144), w("AL", 0, 8)
         pick("AR", 0, 128, la, 144, ("AL", 0))
-        run("s", lambda: g.scalar.activation(ms[0], tb[0].indirect(al[0]), F.Copy), [tb, al], [ms])
+        cp("v", ms, ind(tb, al))
         for b in range(4):
             mm(b, 128, "E", 128 * b, "AR", 0)
-        tr(w("HHT", 256, 320), w("HH", 256, 320))
-        scan(w("SH", 256, 320), w("SEGH", 256, 320), w("HHT", 256, 320))
         for k in range(2):
             for h in range(2):
-                cp("s", w("SX", 2 * k, 2 * k + 2, 1, 64 * h, 64 * h + 64), w("SH", 287, 320, 32, 64 * k, 64 * k + 64))
+                cp("s", w("SX", 4 * k, 4 * k + wide // 32, 1, 64 * h, 64 * h + 64), w("SH", 287, 256 + wide, 32, 64 * k, 64 * k + 64))
+        if last:
+            cp("s", w("YB", 0, 256), w("ps", 2048, 2304))
+            store("y", T.y[:, 0:256], w("YB", 0, 256))
         for b in range(4):
             scan(w("NT", b, 512, 4), ms, bank(b, 128))
-            if b == 2:
-                cp("v", w("SEL", 0, 16), ind(w("SX", 0, 4), lst("sl" if last else "se", 1)))
-        quant(pb, 0, w("NT", 0, 512))
-        pick(pn, OLD, 128, pb, 256, ("SEL", 0))
+        cp("v", w("SEL", 0, 16), ind(w("SX", 0, 8), lst("sl" if last else "se", 1)))
+        quant(pb, 0, ("NT", 0), 128)
         if not last:
+            pick(pn, OLD, 128, pb, 256, ("SEL", 0))
             scores(t + 1)
-            dn = "D%d" % (t + 1)
-            pick(dn, 0, 256, "D%d" % t, 288, ("DLS", 0))
-            for b in range(4):
-                mm(4 + b, 128, "E", 512 + 128 * b, "D%d" % t, 256, True, False)
-                mm(4 + b, 128, "E", 128 * b, "NX", 256 + 32 * t, False, True)
-            for h in range(2):
-                mm(1 + h, 128, dn, 128 * h, "S", 0)
-            for b in range(4):
-                cp("vs"[b % 2], w("DT1", b, 128, 4), bank(4 + b, 32))
-            cp("s", w("ACOL", 0, 2), w("ps", 512 + t + 1, 1536, 512))
-            differences("DMP", 0, "MAP")
-            quant("DL", 256 + 32 * t, w("DT1", 0, 512))
-            arow()
-            pick("LA%d" % (t + 1), LAP, 64, pn, 128, ("LST", LISTS["pp"]), OLD)
+            deltas("vsvs")
+            tt(w("DMP", 0, 127), w("MPT", 0, 127), w("MPT", 1, 128), A.subtract)
             if t == 0:
-                quant("D1", 256, w("ZB", 0, 512))
-            else:
-                quant("U", 0, w("UB", 0, 512))
-                quant("V", 0, w("VB", 0, 512))
+                with_u(2, 1)
+                with_w(2)
+            quant("DL", 256 * (t + 1), ("DT", 0), 256)
+            cp("v", w("DMP", 31, 128, 32), w("MPT", 31, 128, 32))
+            pick("LA%d" % (t + 1), LAP, 64, pn, 128, ("LST", LISTS["pp"]), OLD)
+            if t == 1:
+                quant("U", 0, ("UB", 0), 128)
+                quant("V", 0, ("VB", 0), 128)
         else:
-            mm(0, 128, "V", 0, pn, OLD)
-            cc = w("c_" + pn, OLD, OLD + 64)
+            pick("FD", 256, 64, pb, 256, ("SEL", 0))
+            mm(0, 128, "V", 0, "FD", 192)
+            cc = w("c_FD", 256, 320)
             store("y", T.oc[:, 1024:1280], (cc[0].bitcast(dt.uint8), cc[1]))
             for k in range(4):
-                store("ys"[k % 2], T.osc[4 * k:4 * k + 4, 256:320], w("z_" + pn, OLD, OLD + 64, 1, 32 * k, 32 * k + 4))
-            cp("v", w("YB", 256, 320), bank(0, 64))
+                store("ys"[k % 2], T.osc[4 * k:4 * k + 4, 256:320], w("z_FD", 256, 320, 1, 32 * k, 32 * k + 4))
+            cp("v", w("YB", 256, 320), bank(0, 64, 64))
             store("s", T.y[:, 256:320], w("YB", 256, 320))
 
     for t in range(R):

@@ -2,11 +2,17 @@ from concourse.bass import DstId, RemoteDMATransfer
 from concourse.mybir import dt, AluOpType as A, ActivationFunctionType as F, AxisListType as AX
 
 R = 3
-HALF = 4
+OWN = 27
+HAND = [(("code", 1, 4), ("code", 4, 7), ("scale", 1, 4))] * R
+NEAR = 4
+PLC = 134
+STEP = 22
 MID = 124
 OLD = 128
 LAP = 80
 BIG = 2.0 ** 60
+PLAN = dict(gap=210, room=20, sure=100, send=300, first=(2200, 600), small=1100, pr=1250, x=1800, w=3100, late=1600, store=1200,
+            scores=1500, places=2000, deltas=2700, cold=400, begin=2000, gfill=1, ahead0=800, ahead1=0, ahead2=0, rq="s", dq="sv", nq="v")
 FP8, U8, BF, F32, I32, U16 = "float8_e4m3fn_x4", "uint8", "bfloat16", "float32", "int32", "uint16"
 SCRATCH = {"ps": ("psum", [128, 4096], F32)}
 
@@ -21,24 +27,23 @@ def _add(d, text, mx=False):
             SCRATCH[name] = ("sbuf", [128, int(n)], d)
 
 
-_add(BF, "XB:1024 PT:512 UB:512 VB:512 UV:512 ONE:520 EB:520 NB:520 HT:1024 DT:1024 NT:512 "
-         "KX0:64 KX1:64 KX2:64 WK0:32 WK1:32 WK2:32 KW:256 CT:1072 GG:192 HH:384 HHT:384 SH:384 MS:128 "
-         "EL:128 CC:256 RG:128 MM:128 XR:16")
-_add(FP8, "X:256 U:128 V:128 S:128 W:512 E:1024 XA:1024 FD:320 DL:768 PB0:256 PB1:256 PB2:256 "
-          "SN0:64 SN1:64 SN2:64 LA0:144 LA1:144 LA2:144 AR:128", mx=True)
-_add(FP8, "c_HC0:32 c_HC1:32 c_HC2:32")
-_add(U8, "z_HZ0:32 z_HZ1:32 z_HZ2:32")
-_add(F32, "N0:32 N1:32 N2:32 SC0:1 SC1:1 SC2:1 FC:64 SM:224 TMPF:72 RA:64 RB:64 RR:64 ST:64 SCN:128 DMP:128 MP:128 MPT:128 YB:320")
-_add(I32, "PI:1 XI:8 INTC:16 TMPI:48")
+_add(BF, "XB:1024 PT:512 UB:512 VB:512 UV:528 ONE:520 EB:520 NB:520 HT:1024 DT:1024 NT:512 "
+         "KX:64 CX0:152 CX1:152 CX2:152 KW:256 CT:1072 GG:192 HH:384 HHT:384 SH:384 MS:128 "
+         "EL:128 RG:128 MM:128")
+_add(FP8, "X:256 U:128 V:128 S:256 W:512 E:1024 XA:1024 FD:320 DL:768 PB0:256 PB1:256 PB2:256 "
+          "SN0:64 SN1:64 SN2:64 LA0:144 LA1:144 LA2:144 AR:128 HC0:32 HC1:32 HC2:32", mx=True)
+_add(F32, "N0:36 N1:36 N2:36 FC:64 SM:240 TMPF:72 RA:64 RB:64 RR:64 ST:64 SCN:128 DMP:128 MP:128 MPT:128 YB:320")
+_add(I32, "PI:8 XI:8 INTC:16 TMPI:48")
 ALIAS = {}
-for _buf, _text in (("SM", "XL:0 ACOL:8 AV1:32 AV2:40 LV:48 VM:64 PV:80 U8:88 SX:96 FB:136 FT:168 FO:200 SQ:216"),
+for _buf, _text in (("SM", "XL:0 ACOL:8 AV1:32 AV2:40 LV:48 VM:64 PV:80 U8:88 SX:96 FB:136 FT:168 FO:200 SQ:216 S4:220 S8:222 LF:224"),
                     ("CT", "TBL:0 WT:144 MASK:272 SEGH:400 MT:784 RST:912 EM:1040"),
-                    ("KW", "RGK:0 MK:32 SK:96 KT:160 DK:192"),
+                    ("KW", "OH:0 MK:32 SK:96 DK:192"),
+                    ("TMPF", "FNAT:0 FBL:16 FH:24 FRG:28 FLV:36 FKP:40"),
                     ("LW", "OUT:0 SEL:16 AL:32 L:40")):
     for _item in _text.split(" "):
         ALIAS[_item.split(":")[0]] = (_buf, int(_item.split(":")[1]))
-LISTS = {"nat": 0, "bl": 16, "ac": 24, "rg": 28, "r2": 36, "fo": 38, "ow": 40, "hh": 42, "se": 44, "sl": 46, "pp": 48}
-_add(U16, "LST:52 LW:44")
+LISTS = {"nat": 0, "bl": 16, "ac": 24, "rg": 28, "fo": 36, "ow": 40, "hh": 42, "se": 44, "sl": 46, "pp": 48, "gx": 52}
+_add(U16, "LST:54 LW:44")
 SEMAPHORES = (["qg", "qv", "qs", "qt", "snt"] + [s + str(t) for s in ("sc", "dl", "ls", "hs") for t in range(R)]
               + ["m%d" % i for i in range(48)])
 
@@ -57,7 +62,7 @@ def _fetch(r):
     need, col = [], {}
     for k in range(8):
         o, q, kind = (k - r) % 8, k // 2, "D" if k >= r else "S"
-        col[k] = o
+        col[k] = OWN + (o - r) % 8
         if _blocks(o)[q] != kind:
             need.append((k, [x for x in range(4) if _blocks(o)[x] == kind]))
     ways = [[]]
@@ -66,12 +71,12 @@ def _fetch(r):
     way = min(ways, key=lambda x: len(set(x)))
     moves = sorted(set(way), key=lambda x: (-x[2], x))
     for (k, src), mv in zip(need, way):
-        col[k] += 8 + 8 * moves.index(mv)
+        col[k] += 8 * moves.index(mv) - OWN
     return moves, col
 
 
-def pos(s, d):
-    return s if s < d else s - 1
+def slot(s, d):
+    return (s - d) % 8
 
 
 def bits(e):
@@ -90,8 +95,10 @@ def _helpers(s, cores, topo):
     return [c for c in topo.cores_of(cores[s]) if topo.die(c) == topo.die(cores[s]) and c not in cores][:3]
 
 
-def _half(h, s):
-    return [o for o in range(HALF * h, HALF * h + HALF) if o != s]
+def _order(s, cores, topo):
+    fs = _far(s, cores, topo)
+    first = max(o for o in range(len(cores)) if o not in fs)
+    return [(first + j) % len(cores) for j in range(len(cores))]
 
 
 def _share(kind, dests, engines):
@@ -99,29 +106,34 @@ def _share(kind, dests, engines):
     return [(kind, d, engines[n * i:n * i + n]) for i, d in enumerate(dests)]
 
 
-def _calls(s, cores, topo):
-    fs = _far(s, cores, topo)
-    near = [o for o in range(len(cores)) if o != s and o not in fs]
-    away = topo.engines(cores[s], cores[fs[0]])
-    close = _near(cores[s], cores[near[0]], away, topo)
-    n = len(away) // 2
-    return [_share("key", fs[:n], away), _share("code", [0, 1], close), _share("hand", [2], close),
-            _share("key", fs[n:], away) + _share("key", near, close),
-            _share("scale", [o for o in _half(s // HALF, s) if o in fs], away) + _share("scale", near, close[:2])]
-
-
-def _sent(s, kind, d, cores, topo):
-    return sum(len(e) for call in _calls(s, cores, topo) for k, o, e in call if (k, o) == (kind, d))
-
-
-def _hand_mask(s, d, src, cores, topo):
-    fs = _far(s, cores, topo)
+def _waves(kind, dests, src, s, cores, topo):
+    fs = [o for o in dests if o in _far(s, cores, topo)]
     away = topo.engines(src, cores[fs[0]])
-    if d not in fs:
-        return _near(src, cores[d], away, topo)[:2]
-    fs = [o for o in _half(d // HALF, s) if o in fs]
-    i = len(away) // len(fs) * fs.index(d)
-    return away[i:i + 2]
+    calls = []
+    while fs:
+        n = max(x for x in (1, 2, 4) if x <= len(fs))
+        calls.append(_share(kind, fs[:n], away))
+        fs = fs[n:]
+    calls[0] += [(kind, o, _near(src, cores[o], away, topo)[:NEAR]) for o in dests if o not in _far(s, cores, topo)]
+    return calls
+
+
+def _hand(t, s, k, cores, topo):
+    kind, a, b = HAND[t][k]
+    return _waves(kind, [o for o in _order(s, cores, topo)[a:b] if o != s], _helpers(s, cores, topo)[k], s, cores, topo)
+
+
+def _calls(t, s, cores, topo):
+    order = _order(s, cores, topo)
+    away = topo.engines(cores[s], cores[_far(s, cores, topo)[0]])
+    close = _near(cores[s], _helpers(s, cores, topo)[0], away, topo)
+    left = {x: [o for o in order if o != s and not any(kind == x and o in order[a:b] for kind, a, b in HAND[t])] for x in ("code", "scale")}
+    return ([_share("hand", [0, 1], close), _share("hand", [2], close)]
+            + _waves("scale", left["scale"], cores[s], s, cores, topo) + [_share("code", [o], close) for o in left["code"]])
+
+
+def _sent(calls, kind, d):
+    return sum(len(e) for call in calls for k, o, e in call if (k, o) == (kind, d))
 
 
 def _to(core, topo):
@@ -129,24 +141,68 @@ def _to(core, topo):
     return DstId(rid=rid, pnc=pid)
 
 
+def _cols(T, kind, name, a, n):
+    return T["c_" + name][:, a:a + n].bitcast(dt.uint8) if kind == "code" else T["z_" + name][:, a:a + n]
+
+
 def hand_on(g, core, s, cores, T, topo):
     k = _helpers(s, cores, topo).index(core)
-    h = k if k < 2 else 1 - s // HALF
-    dests = _half(h, s)
+    order, sent = _order(s, cores, topo), 0
     for t in range(R):
-        g.wait_ge(T.sem["hs%d" % t], _sent(s, "code" if k < 2 else "hand", k, cores, topo))
-        tf = []
-        for o in dests:
-            p, i = pos(s, o), o - HALF * h
-            if k < 2:
-                src = T["c_HC%d" % t][:, 8 * i:8 * i + 8].bitcast(dt.uint8)
-                land = T["c_LA%d" % t][:, 16 + 8 * p:24 + 8 * p].bitcast(dt.uint8)
-            else:
-                src, land = T["z_HZ%d" % t][:, 8 * i:8 * i + 8], T["z_LA%d" % t][:, 16 + 8 * p:24 + 8 * p]
-            tf.append(RemoteDMATransfer(dst_ids=[_to(cores[o], topo)], dma_engine_mask=bits(_hand_mask(s, o, core, cores, topo)),
-                                        remote_sem=T.sem["dl%d" % t], srcs=[src], dsts=[land]))
-        g.remote_dma_fused(tf, local_sem=T.sem.snt)
-    g.wait_ge(T.sem.snt, 2 * len(dests) * R)
+        g.wait_ge(T.sem["hs%d" % t], _sent(_calls(t, s, cores, topo), "hand", k))
+        for call in _hand(t, s, k, cores, topo):
+            g.remote_dma_fused([RemoteDMATransfer(dst_ids=[_to(cores[o], topo)], dma_engine_mask=bits(e), remote_sem=T.sem["dl%d" % t],
+                                                  srcs=[_cols(T, kind, "HC%d" % t, 8 * (order.index(o) - HAND[t][k][1]), 8)],
+                                                  dsts=[_cols(T, kind, "LA%d" % t, 8 + 8 * slot(s, o), 8)]) for kind, o, e in call], local_sem=T.sem.snt)
+            sent += sum(len(e) for kind, o, e in call)
+    g.wait_ge(T.sem.snt, sent)
+
+
+def _before(calls):
+    hist, sends, out = {}, [], []
+    for j, (ways, reads, writes, what, late, after) in enumerate(calls):
+        pre = {i: False for i in after}
+        for regions, wr in ((reads, False), (writes, True)):
+            for name, cols, p0, p1 in regions:
+                for c, a, b, w2, i in hist.get(name, ()):
+                    if c & cols and a < p1 and p0 < b and (wr or w2 or name == "ps"):
+                        pre[i] = pre.get(i, True) and name == "ps" and wr == w2
+        if what == "send" and sends:
+            pre.setdefault(sends[-1], True)
+        if what == "send":
+            sends.append(j)
+        for name, cols, p0, p1 in writes:
+            hist[name] = [h for h in hist.get(name, ()) if not (h[0] & ~cols == 0 and p0 <= h[1] and h[2] <= p1)] + [(cols, p0, p1, True, j)]
+        for name, cols, p0, p1 in reads:
+            hist.setdefault(name, []).append((cols, p0, p1, False, j))
+        out.append(pre)
+    return out
+
+
+def _plan(calls, ahead):
+    pre, gap = _before(calls), PLAN["gap"]
+    span = [max(min(c for f, c in x[0].values()), x[4]) for x in calls]
+    chain = list(span)
+    for j in range(len(calls) - 1, -1, -1):
+        chain[j] += ahead.get(j, 0)
+        for i, soft in pre[j].items():
+            chain[i] = max(chain[i], span[i] + (0 if soft else gap) + chain[j])
+    busy, start, done, on = {}, {}, {}, {}
+    for j in sorted(range(len(calls)), key=lambda j: (-chain[j], j)):
+        best = None
+        for q, (f, c) in calls[j][0].items():
+            t = max([0] + [done[i] + (0 if soft and on[i] == q else gap) for i, soft in pre[j].items()])
+            sure = max([0] + [done[i] + gap + PLAN["sure"] for i in pre[j] if on[i] != q])
+            for a, b in busy.get(q, ()):
+                if max(t, sure) + c + PLAN["room"] <= a:
+                    break
+                t = max(t, b)
+            if best is None or t + c < best[0]:
+                best = (t + c, t, q, c)
+        end, t, q, c = best
+        busy[q] = sorted(busy.get(q, []) + [(t, end)])
+        start[j], done[j], on[j] = t, t + max(c, calls[j][4]), q
+    return [(j, on[j]) for j in sorted(start, key=lambda j: (start[j], j))]
 
 
 def rank_program(g, core, T, topo):
@@ -159,93 +215,39 @@ def rank_program(g, core, T, topo):
                 hand_on(g, core, s, cores, T, topo)
         return
     r = me
-    Q = {"g": g, "v": g.vector, "s": g.scalar, "t": g.tensor, "y": g.sync}
-    csem = {"g": "qg", "v": "qv", "s": "qs", "t": "qt"}
-    total, known, hist = {}, {q: {} for q in Q}, {}
-    ndma = [0]
+    calls, ahead = [], {}
 
     def w(name, c0, c1, step=1, p0=0, p1=128):
         if name in ALIAS:
             name, c0, c1 = ALIAS[name][0], c0 + ALIAS[name][1], c1 + ALIAS[name][1]
-        t = T[name]
+        t, n = T[name], len(range(c0, c1, step))
         if p0 == 0 and p1 == 128:
             a = t[:, c0:c1] if step == 1 else t[:, c0:c1:step]
         else:
             a = t[p0:p1, c0:c1] if step == 1 else t[p0:p1, c0:c1:step]
         if name == "ps":
-            cols = sum(1 << b for b in range(c0 // 512, (c1 + 511) // 512))
-            return (a, [(name, cols, 0, 128)])
+            return (a, [(name, sum(1 << b for b in range(c0 // 512, (c1 + 511) // 512)), 0, 128)], n, False)
         cols = ((1 << (c1 - c0)) - 1) << c0 if step == 1 else sum(1 << c for c in range(c0, c1, step))
-        return (a, [(name, cols, p0, p1)])
-
-    def part(v, a, b, p0=0, p1=128, step=1):
-        return w("TMPF", v[2] + a, v[2] + b, step, p0, p1)
+        return (a, [(name, cols, p0, p1)], n, SCRATCH[name][2] in (BF, U16))
 
     def ind(v, o):
-        return (v[0].indirect(o[0]), v[1] + o[1])
+        return (v[0].indirect(o[0]), v[1] + o[1], 16 * o[2], None)
 
     def lst(name, n, off=0):
         a = LISTS[name] + off
         return w("LST", a, a + n)
 
-    def waits(q, reads, writes):
-        need = {}
-        def want(h):
-            sem, n, clock = h[6], h[7], h[8]
-            if known[q].get(sem, 0) >= n:
-                return
-            if sem not in need or need[sem][0] < n:
-                need[sem] = (n, clock)
-        for name, cols, p0, p1 in reads:
-            for h in hist.get(name, ()):
-                if h[0] & cols and h[1] < p1 and p0 < h[2] and (h[3] or (name == "ps" and h[4] != q)):
-                    want(h)
-        for name, cols, p0, p1 in writes:
-            for h in hist.get(name, ()):
-                if h[0] & cols and h[1] < p1 and p0 < h[2]:
-                    if name == "ps" and h[4] == q:
-                        continue
-                    want(h)
-        for sem in sorted(need):
-            n, clock = need[sem]
-            if any(s2 != sem and c2.get(sem, 0) >= n for s2, (n2, c2) in need.items()):
-                continue
-            Q[q].wait_ge(T.sem[sem], n)
-        for sem in need:
-            n, clock = need[sem]
-            for k, v in clock.items():
-                if known[q].get(k, 0) < v:
-                    known[q][k] = v
-            known[q][sem] = max(known[q].get(sem, 0), n)
+    def as_bytes(v):
+        return (v[0].bitcast(dt.uint8),) + v[1:]
 
-    def record(q, reads, writes, sem, n, clock, dma):
-        for name, cols, p0, p1 in writes:
-            hs = [h for h in hist.get(name, ()) if not (h[0] & ~cols == 0 and p0 <= h[1] and h[2] <= p1)]
-            hs.append((cols, p0, p1, True, q, dma, sem, n, clock))
-            hist[name] = hs
-        for name, cols, p0, p1 in reads:
-            hs = [h for h in hist.get(name, ()) if not (not h[3] and not dma and not h[5] and h[4] == q and (cols, p0, p1) == tuple(h[:3]))]
-            hs.append((cols, p0, p1, False, q, dma, sem, n, clock))
-            hist[name] = hs
+    def put(ways, reads, writes, what="compute", late=0, after=()):
+        calls.append((ways, [x for v in reads for x in v[1]], [x for v in writes for x in v[1]], what, late, after))
+        return len(calls) - 1
 
-    def run(q, call, reads, writes, dma=False):
-        rr = [x for v in reads for x in v[1]]
-        ww = [x for v in writes for x in v[1]]
-        waits(q, rr, ww)
-        if dma:
-            sem, inc = "m%d" % ndma[0], 16
-            ndma[0] += 1
-        else:
-            sem, inc = csem[q], 1
-        total[sem] = total.get(sem, 0) + inc
-        call().then_inc(T.sem[sem], inc)
-        clock = dict(known[q])
-        clock[sem] = total[sem]
-        record(q, rr, ww, sem, total[sem], clock, dma)
-
-    def arrive(views, sem, n):
-        total[sem] = n
-        record("x", [], [x for v in views for x in v[1]], sem, n, {sem: n}, True)
+    def cycles(q, out, a, k=1):
+        if a[3] is None:
+            return 60 + 1.6 * a[2]
+        return max(64, k * a[2] * (0.5 if q == "v" and k == 1 and out[3] and a[3] else 1))
 
     def S(x):
         return x[0] if isinstance(x, tuple) else x
@@ -253,449 +255,484 @@ def rank_program(g, core, T, topo):
     def deps(*xs):
         return [x for x in xs if isinstance(x, tuple)]
 
-    def cp(q, out, a):
-        if q == "v":
-            run("v", lambda: g.vector.tensor_copy(out[0], a[0]), [a], [out])
-        else:
-            run("s", lambda: g.scalar.activation(out[0], a[0], F.Copy), [a], [out])
+    def either(qs, out, a, on_v, on_s, more=()):
+        ways = {"v": (on_v, cycles("v", out, a)), "s": (on_s, cycles("s", out, a))}
+        put({q: ways[q] for q in qs}, [a] + list(more), [out])
 
-    def sa(out, a, scale=1.0, bias=0.0):
-        run("s", lambda: g.scalar.activation(out[0], a[0], F.Identity, bias=S(bias), scale=S(scale)), [a] + deps(scale, bias), [out])
+    def cp(qs, out, a):
+        either(qs, out, a, lambda: g.vector.tensor_copy(out[0], a[0]), lambda: g.scalar.activation(out[0], a[0], F.Copy))
+
+    def lin(out, a, scale=1.0, bias=0.0, qs="sv"):
+        either(qs, out, a, lambda: g.vector.tensor_scalar(out[0], a[0], S(scale), S(bias), A.mult, A.add),
+               lambda: g.scalar.activation(out[0], a[0], F.Identity, bias=S(bias), scale=S(scale)), deps(scale, bias))
+
+    def fill(name, a, b, c, step=1):
+        out, one = w(name, a, b, step), w("ONE", 0, len(range(a, b, step)))
+        ways = {"s": (lambda: g.scalar.activation(out[0], one[0], F.Identity, bias=c, scale=0.0), cycles("s", out, one)),
+                "v": (lambda: g.vector.memset(out[0], c), cycles("v", out, one))}
+        if step == 1 and PLAN["gfill"]:
+            ways["g"] = (lambda: g.iota(out[0], [[0, b - a]], int(c), 0, allow_small_or_imprecise_dtypes=True), 150 + 2 * out[2])
+        put(ways, [one], [out])
+
+    def sign(out, a, z, total=None):
+        if total is None:
+            put({"s": (lambda: g.scalar.activation(out[0], a[0], F.Sign, bias=z[0], scale=-1.0), cycles("s", out, a))}, [a, z], [out])
+        else:
+            put({"s": (lambda: g.scalar.activation(out[0], a[0], F.Sign, bias=z[0], scale=-1.0, accum_out=total[0]), cycles("s", out, a) + 24)}, [a, z], [out, total])
 
     def tt(out, a, b, op):
-        run("v", lambda: g.vector.tensor_tensor(out[0], a[0], b[0], op), [a, b], [out])
+        put({"v": (lambda: g.vector.tensor_tensor(out[0], a[0], b[0], op), cycles("v", out, a, 2))}, [a, b], [out])
 
     def ts(out, a, s1, op0, s2=None, op1=None):
         if op1 is None:
-            run("v", lambda: g.vector.tensor_scalar(out[0], a[0], S(s1), None, op0), [a] + deps(s1), [out])
+            put({"v": (lambda: g.vector.tensor_scalar(out[0], a[0], S(s1), None, op0), cycles("v", out, a))}, [a] + deps(s1), [out])
         else:
-            run("v", lambda: g.vector.tensor_scalar(out[0], a[0], S(s1), S(s2), op0, op1), [a] + deps(s1, s2), [out])
+            put({"v": (lambda: g.vector.tensor_scalar(out[0], a[0], S(s1), S(s2), op0, op1), cycles("v", out, a))}, [a] + deps(s1, s2), [out])
 
     def tr(out, a):
-        run("v", lambda: g.vector.transpose(out[0], a[0]), [a], [out])
+        put({"v": (lambda: g.vector.transpose(out[0], a[0]), cycles("v", out, a))}, [a], [out])
 
     def scan(out, a, b):
-        run("v", lambda: g.vector.tensor_tensor_scan(out[0], a[0], b[0], 0.0, A.mult, A.add), [a, b], [out])
+        put({"v": (lambda: g.vector.tensor_tensor_scan(out[0], a[0], b[0], 0.0, A.mult, A.add), max(cycles("v", out, a), cycles("v", out, b)))}, [a, b], [out])
 
     def rsum(out, a):
-        run("v", lambda: g.vector.tensor_reduce(out[0], a[0], AX.X, A.add), [a], [out])
-
-    def fill(out, c):
-        run("v", lambda: g.vector.memset(out[0], c), [], [out])
-
-    def sfill(name, a, b, c, step=1):
-        sa(w(name, a, b, step), w("ONE", 0, len(range(a, b, step))), 0.0, c)
+        put({"v": (lambda: g.vector.tensor_reduce(out[0], a[0], AX.X, A.add), max(64, a[2]))}, [a], [out])
 
     def iota(out, pattern, base=0, ch=0, small=True):
         if small:
-            run("g", lambda: g.iota(out[0], pattern, base, ch, allow_small_or_imprecise_dtypes=True), [], [out])
+            put({"g": (lambda: g.iota(out[0], pattern, base, ch, allow_small_or_imprecise_dtypes=True), 150 + 2 * out[2])}, [], [out])
         else:
-            run("g", lambda: g.iota(out[0], pattern, base, ch), [], [out])
+            put({"g": (lambda: g.iota(out[0], pattern, base, ch), 150 + 2 * out[2])}, [], [out])
 
     def quant(name, c0, src, n):
         c, z, a = w("c_" + name, c0, c0 + n), w("z_" + name, c0, c0 + n), w(src[0], src[1], src[1] + 4 * n)
-        run("v", lambda: g.vector.quantize_mx(c[0], z[0], a[0]), [a], [c, z])
+        put({"v": (lambda: g.vector.quantize_mx(c[0], z[0], a[0]), 15 + 1.06 * n)}, [a], [c, z])
 
     def pick(dst, d0, n, src, width, off, a0=0):
         b, k = off
         o = w(b, k, k + n // 16)
         co, ci = w("c_" + dst, d0, d0 + n), w("c_" + src, a0, a0 + width)
-        run("v", lambda: g.vector.tensor_copy(co[0].bitcast(dt.uint32), ci[0].bitcast(dt.uint32).indirect(o[0])), [ci, o], [co])
-        zo, zi = w("z_" + dst, d0, d0 + n), w("z_" + src, a0, a0 + width)
-        run("s", lambda: g.scalar.activation(zo[0], zi[0].indirect(o[0]), F.Copy), [zi, o], [zo])
+        put({"v": (lambda: g.vector.tensor_copy(co[0].bitcast(dt.uint32), ci[0].bitcast(dt.uint32).indirect(o[0])), 60 + 1.6 * n)}, [ci, o], [co])
+        cp("s", w("z_" + dst, d0, d0 + n), ind(w("z_" + src, a0, a0 + width), o))
 
     def mm(bank, n, lhs, l0, rhs, r0, start=True, stop=True):
         out = w("ps", 512 * bank, 512 * bank + n)
         a, az = w("c_" + lhs, l0, l0 + 128), w("z_" + lhs, l0, l0 + 128)
         b, bz = w("c_" + rhs, r0, r0 + n), w("z_" + rhs, r0, r0 + n)
-        run("t", lambda: g.tensor.matmul_mx(out[0], a[0], az[0], b[0], bz[0], start, stop), [a, az, b, bz], [out])
+        put({"t": (lambda: g.tensor.matmul_mx(out[0], a[0], az[0], b[0], bz[0], start, stop), 0.6 * (n + 16))}, [a, az, b, bz], [out])
 
     def bank(b, n, c0=0):
         return w("ps", 512 * b + c0, 512 * b + c0 + n)
 
-    def load(q, out, a, after=()):
-        run(q, lambda: Q[q].dma_start(out[0], a), list(after), [out], dma=True)
+    Q = {"g": g, "v": g.vector, "s": g.scalar, "t": g.tensor, "y": g.sync}
+
+    def load(q, out, a, late, after=()):
+        put({q: (lambda: Q[q].dma_start(out[0], a), 60)}, list(after), [out], "dma", PLAN[late])
 
     def store(q, a, src):
-        run(q, lambda: Q[q].dma_start(a, src[0]), [src], [], dma=True)
-
-    def weave(*chains):
-        for i in range(max(len(c) for c in chains)):
-            for c in chains:
-                if i < len(c) and c[i]:
-                    c[i]()
+        put({q: (lambda: Q[q].dma_start(a, src[0]), 60)}, [src], [], "dma", PLAN["store"])
 
     others = [o for o in range(n_ranks) if o != me]
     afar = _far(me, cores, topo)
     away = topo.engines(core, cores[afar[0]])
-    helpers = _helpers(me, cores, topo)
+    helpers, order = _helpers(me, cores, topo), _order(me, cores, topo)
+    sent = [0]
 
-    def fused(reads, transfers):
-        waits("g", [x for v in reads for x in v[1]], [])
-        g.remote_dma_fused([RemoteDMATransfer(dst_ids=[_to(c, topo) for c in ds], dma_engine_mask=bits(e), remote_sem=sem, srcs=[src], dsts=[land] * len(ds))
-                            for ds, e, sem, src, land in transfers], local_sem=T.sem.snt)
-        total["snt"] = total.get("snt", 0) + sum(len(x[1]) for x in transfers)
+    def fused(reads, transfers, cost=PLAN["send"]):
+        sent[0] += sum(len(x[1]) for x in transfers)
+        tf = [RemoteDMATransfer(dst_ids=[_to(c, topo) for c in ds], dma_engine_mask=bits(e), remote_sem=sem, srcs=[src], dsts=lands)
+              for ds, e, sem, src, lands in transfers]
+        return put({"g": (lambda: g.remote_dma_fused(tf, local_sem=T.sem.snt), cost)}, reads, [], "send")
 
-    def send_scores(t):
-        src, land, sem = w("SC%d" % t, 0, 1), T["N%d" % t][:, me:me + 1], T.sem["sc%d" % t]
-        far = [([cores[o] for o in afar], away, sem, src[0], land)]
-        near = [([cores[o]], _near(core, cores[o], away, topo)[:2 if t else len(away)], sem, src[0], land) for o in others if o not in afar]
-        for call in ([far + near] if t else [far, near]):
-            fused([src], call)
+    def arrive(views, sem, n, after, late):
+        put({sem: (n, 0)}, [], views, "arrive", late - PLAN["gap"] - sum(calls[j][0]["g"][1] for j in after), after)
 
-    def score_count(t):
-        return sum(len(away) if s in afar or t == 0 else 2 for s in others)
+    def to_all(name, a, n, sem, late, first=False):
+        src = w(name, a, a + n)
+        land = {o: T[name][:, a + n * slot(me, o):a + n + n * slot(me, o)] for o in others}
+        far = [([cores[o] for o in afar], away, T.sem[sem], src[0], [land[o] for o in afar])]
+        near = [([cores[o]], _near(core, cores[o], away, topo)[:len(away) if first else 2], T.sem[sem], src[0], [land[o]]) for o in others if o not in afar]
+        sends = [fused([src], call, cost) for call, cost in zip((far, near), PLAN["first"])] if first else [fused([src], far + near)]
+        if first:
+            ahead[sends[0]] = PLAN["ahead0"]
+        arrive([w(name, a + n, a + 8 * n)], sem, sum(len(away) if s in afar or first else 2 for s in others), sends, late)
 
-    def delta_count(s):
-        return 2 + (_sent(s, "scale", me, cores, topo) if s // HALF == me // HALF else 2)
+    def delta_count(t, s):
+        cs = _calls(t, s, cores, topo) + [c for k in range(len(helpers)) for c in _hand(t, s, k, cores, topo)]
+        return _sent(cs, "scale", me) + _sent(cs, "code", me)
 
     lay = _blocks(me)
     QB, DB = lay.index("R"), lay.index("D")
+    HR = QB // 2
     moves, ccol = _fetch(r)
 
-    load("s", w("PT", 128 * DB, 128 * DB + 128), T.pd[:, :])
-    load("y", w("PT", 128 * QB, 128 * QB + 128), T.pr[:, :])
-    load("s", w("UV", 16, 32), T.v[:, 0:16])
-    load("y", w("UV", 0, 16), T.u[:, 0:16])
-    load("y", w("XB", 0, 1024), T.x[:, :])
-    load("s", w("z_W", 0, 512), T.ws[:, :])
-    cw = w("c_W", 0, 512)
-    load("y", (cw[0].bitcast(dt.uint8), cw[1]), T.wc[:, :])
+    load("s", w("PT", 128 * DB, 128 * DB + 128), T.pd[:, :], "small")
+    load("y", w("UV", 16, 32), T.v[:, 0:16], "small")
+    load("s", w("PT", 128 * QB, 128 * QB + 128), T.pr[:, :], "pr")
+    load("y", w("XB", 0, 1024), T.x[:, :], "x")
+    load("s", w("UV", 0, 16), T.u[:, 0:16], "x")
+    load("s", w("z_W", 0, 512), T.ws[:, :], "x")
+    load("y", as_bytes(w("c_W", 0, 512)), T.wc[:, :], "w")
+    n_loads = len(calls)
 
-    TMP = [0]
-    def ftmp(n):
-        a = TMP[0]
-        TMP[0] += n
-        return w("TMPF", a, a + n) + (a,)
-    fnat, fh, frg, fbl, flv, fkp = [ftmp(n) for n in (16, 4, 8, 8, 4, 32)]
-    fill(w("ONE", 0, 520), 1.0)
-    iota(w("PI", 0, 1), [[0, 1]], 0, 1, small=False)
-    iota(fnat, [[1, 2], [2, 4], [128, 2]])
-    iota(fh, [[1, 2], [0, 2]])
+    fnat, fh, frg, fbl, flv, fkp = w("FNAT", 0, 16), w("FH", 0, 4), w("FRG", 0, 8), w("FBL", 0, 8), w("FLV", 0, 4), w("FKP", 0, 32)
     eb, one = w("EB", 0, 520), w("ONE", 0, 520)
-    run("g", lambda: g.affine_select(eb[0], one[0], [[-1, 520]], A.is_equal, 0.0, 4, 4), [one], [eb])
-    iota(frg, [[2, 4], [0, 2]])
-    iota(w("XI", 0, 8), [[32, 2], [64, 2], [0, 2]], 0, 1, small=False)
-    iota(w("RST", 0, 128), [[0, 2], [1, 64]])
-    sfill("UV", 32, 512, 0.0)
+    put({"v": (lambda: g.vector.memset(one[0], 1.0), 260)}, [], [one])
+    iota(w("PI", 3, 7), [[4 * me, 2], [64 * HR, 2]], 0, 1, small=False)
+    for k in range(3):
+        iota(w("PI", k, k + 1), [[0, 1]], 0, 8 >> k, small=False)
+    iota(fh, [[1, 2], [0, 2]])
+    iota(fnat, [[1, 2], [2, 4], [128, 2]])
+    iota(frg, [[2, 4], [0, 2]], order[0])
+    iota(w("XI", 0, 8), [[32, 4], [0, 2]], 32, 1, small=False)
+    put({"g": (lambda: g.affine_select(eb[0], one[0], [[-1, 520]], A.is_equal, 0.0, 4, 4), 1240)}, [one], [eb])
+    fill("UV", 32, 528, 0.0)
 
     def col(j):
         return w("FC", j, j + 1)
-    P16, P31, KK, QQ, B2, B3, Q1, K2, P8, M, B0, B1, K1 = range(13)
-    FIELD = ((0, 15), (0, 31), (2, 3), (5, 3), (2, 1), (3, 1), (6, 1), (2, 7), (0, 7), (0, 3), (0, 1), (1, 1), (1, 3))
-
-    def field(j):
-        o, i, (sh, an) = w("INTC", j, j + 1), w("PI", 0, 1), FIELD[j]
+    P16, P31, QQ, B0, B1, B2, B3, P8, K2, RK, M, KK, Q1 = range(13)
+    C8P, CA, CB, CQ, SHF, PC, PC3, VP, VD, OP, C1P, MK1, SU, Y2, Y3, PP, PD, P3, VPB, VDB, W0, W1, W2, W3, W4, SU2, Y4 = range(16, 43)
+    for j, n, a, step, sh, an in ((P16, 1, 3, 1, 0, 15), (P31, 1, 3, 1, 0, 31), (QQ, 1, 3, 1, 5, 3), (B0, 4, 0, 1, 3, 1), (P8, 3, 1, 2, 2, 7),
+                                  (M, 2, 1, 2, 2, 3), (Q1, 1, 4, 1, 6, 1)):
+        o, i = w("INTC", j, j + n), w("PI", a, a + step * (n - 1) + 1, step)
         if sh:
             ts(o, i, sh, A.arith_shift_right, an, A.bitwise_and)
         else:
             ts(o, i, an, A.bitwise_and)
-    C8P, CA, CB, CQ, SHF, PC, PC3, VP, VD, OP, C1P, MK1, SU, Y2, Y3, PP, PD, P3, VPB, VDB, W0, W1, W2 = range(16, 39)
-    for j in range(M):
-        field(j)
-    cp("v", w("FC", 0, M), w("INTC", 0, M))
+    cp("v", w("FC", P16, P16 + 1), w("INTC", P16, P16 + 1))
+    cp("v", w("FC", P31, Q1 + 1), w("INTC", P31, Q1 + 1))
 
-    turn = 0
     for b in range(4):
         a, d = 128 * b, 128 * DB
         for o0, o1, i0 in {"R": [], "D": [(0, 128, 0)] if b != DB else [], "S": [(4, 128, 0), (0, 4, 124)]}[lay[b]]:
-            cp("vs"[turn % 2], w("PT", a + o0, a + o1), w("PT", d + i0, d + i0 + o1 - o0))
-            turn += 1
-    quant("S", 0, ("UV", 0), 128)
+            cp("vs", w("PT", a + o0, a + o1), w("PT", d + i0, d + i0 + o1 - o0))
+    quant("S", 128, ("UV", 16), 128)
     quant("PB0", OLD, ("PT", 0), 128)
-    sa(col(CA), col(B2), float(r), col(B3))
-    sa(col(CB), col(Q1), float(r), col(KK))
-    sa(col(CQ), col(QQ), -2.0, 8.0)
-    sa(col(C8P), col(P16), 8.0)
-    ts(col(SHF), col(K2), float(8 - r), A.is_ge, col(Q1), A.mult)
 
     def scores(t):
-        sc, n = "SC%d" % t, "N%d" % t
-        mm(0, 128, "PB%d" % t, OLD, "S", 0)
-        cp("s", w(sc, 0, 1), w("ps", 4 + t, 5 + t))
-        send_scores(t)
-        run("y", lambda: g.sync.dma_start(T[n][:, me:me + 1], T[sc][:, 0:1]), [w(sc, 0, 1)], [w(n, me, me + 1)], dma=True)
-        arrive([w(n, a, b) for a, b in ((0, me), (me + 1, 8)) if b > a], "sc%d" % t, score_count(t))
+        n = "N%d" % t
+        mm(0, 128, "PB%d" % t, OLD, "S", 128)
+        cp("sv", w(n, OWN, OWN + 1), w("ps", t, t + 1))
+        to_all(n, OWN, 1, "sc%d" % t, PLAN["scores"] + (0 if t else PLAN["begin"]), t == 0)
 
     scores(0)
-    ts(w("NB", 0, 520), eb, -1.0, A.mult)
-    iota(w("MT", 0, 128), [[0, 32], [1, 4]])
+    iota(w("RST", 0, 64), [[1, 64]])
+    iota(w("MT", 0, 128), [[0, 32], [2, 4]], -32)
     iota(fkp, [[8, 32]], -MID)
     iota(flv, [[256, 4]])
-    iota(w("SQ", 0, 2), [[16, 2]])
+    iota(w("SQ", 0, 4), [[32 * (DB - QB), 2], [16, 2]], 32 * QB)
+    iota(w("S4", 0, 2), [[4, 2]], me)
+    iota(w("S8", 0, 2), [[8, 2]], PLC - 64)
     iota(w("MASK", 0, 64), [[16, 2], [0, 2], [1, 16]])
     iota(w("MASK", 64, 128), [[16, 2], [0, 2], [1, 16]], -1)
     iota(w("WT", 0, 128), [[32, 4], [0, 2], [2, 16]], -63)
     iota(w("EM", 0, 32), [[0, 2], [1, 2], [0, 8]])
 
-    ti, b1, b2, xi = w("TMPI", 0, 12), w("TMPI", 16, 28), w("TMPI", 32, 44), w("XI", 0, 8)
-    ts(w("TMPI", 0, 8), frg, col(CA), A.add, col(CQ), A.add)
-    ts(w("TMPI", 8, 10), part(frg, 0, 8, step=4), col(CB), A.add, col(CQ), A.add)
-    ts(w("TMPI", 10, 12), w("ONE", 0, 2), col(P8), A.mult, col(CQ), A.add)
+    ti, xi = w("TMPI", 0, 10), w("XI", 0, 8)
+    lin(col(C8P), col(P16), 8.0)
+    lin(col(CQ), col(QQ), -2.0, 6.0)
+    lin(col(CA), col(B2), float(r), col(B3))
     ts(lst("nat", 16), fnat, col(C8P), A.add)
-    weave([lambda b=b: quant("E", 128 * b, ("EB", 4 - b), 128) for b in range(4)],
-          [lambda: ts(ti, ti, 7, A.bitwise_and), lambda: ts(b1, ti, 1, A.arith_shift_right, 1, A.bitwise_and), lambda: tt(b1, b1, b2, A.subtract),
-           lambda: ts(b1, b1, 2.0, A.mult)],
-          [lambda: ts(xi, xi, 127, A.bitwise_and), lambda: ts(b2, ti, 2, A.arith_shift_right)])
-    sfill("AV1", 0, 16, 0.0)
+    ts(w("TMPI", 0, 8), frg, col(CA), A.add, col(CQ), A.add)
+    ts(w("TMPI", 8, 10), w("ONE", 0, 2), col(P8), A.mult, col(CQ), A.add)
+    ts(ti, ti, 7, A.bitwise_and)
+    cp("v", lst("rg", 10), ti)
     for q in range(4):
-        sa(part(fbl, 0, 4, 32 * q, 32 * q + 32), part(fh, 0, 4, 32 * q, 32 * q + 32), 1.0, 2.0 * q)
-        sa(part(fbl, 4, 8, 32 * q, 32 * q + 32), part(fh, 0, 4, 32 * q, 32 * q + 32), float(ccol[2 * q + 1] - ccol[2 * q]), float(ccol[2 * q]))
-    sa(col(W0), col(P31), 1.0, float(LAP))
-    sa(col(W1), col(P31), 1.0, OLD + 32.0 * QB)
-    sa(col(W2), col(P31), -1.0, 31.0 - OLD - 32.0 * QB)
-    sa(col(VP), col(K2), 8.0, 16.0)
-    sa(col(PC), col(P31), 8.0, -MID - 0.5)
-    sa(col(PC3), col(P31), 8.0, 7.25 - MID)
-    sa(col(VPB), col(Q1), 32.0, col(W0))
-    sa(col(OP), col(Q1), 32.0 * (DB - QB), col(W1))
-    sa(col(C1P), col(Q1), 64.0 - 32.0 * (DB - QB), col(W2))
-    sfill("DMP", 0, 128, -1.0)
-    if moves:
-        sfill("N0", 8, 32, 0.0)
-    sfill("DK", 1, 31, -8.0)
-    sfill("DK", 32, 64, 0.0)
-    sfill("MK", 32, 64, 1.0)
-    sa(w("DK", 0, 1), col(SHF), 256.0, -8.0)
-    sa(w("DK", 31, 32), col(SHF), -8.0, float(248 + r - MID))
+        for a, c0, c1 in ((0, OWN % 8 + slot(2 * q, me), OWN % 8 + slot(2 * q + 1, me)), (4, ccol[2 * q], ccol[2 * q + 1])):
+            lin(w("FBL", a, a + 4, 1, 32 * q, 32 * q + 32), w("FH", 0, 4, 1, 32 * q, 32 * q + 32), float(c1 - c0), float(c0))
+    cp("v", lst("bl", 12), w("FBL", 0, 12))
+    for t in range(R):
+        fill("N%d" % t, 0, OWN, 0.0)
+    ts(w("RST", 0, 64), w("RST", 0, 64), col(P31), A.is_equal, -2.0, A.mult)
+    lin(w("RST", 0, 64), w("RST", 0, 64), 1.0, 1.0)
+    ts(xi, xi, 127, A.bitwise_and)
+    cp("v", w("XL", 0, 8), xi)
+    lin(w("XL", 1, 8, 2), w("XL", 1, 8, 2), 1.0, 128.0)
+    fill("DMP", 0, 128, -1.0)
+    cp("vs", w("RG", 0, 128), ind(w("XL", 0, 8), lst("rg", 8)))
+    tr(w("MM", 0, 128), w("RG", 0, 128))
+    cp("vs", w("DMP", 31, 128, 32), w("MM", 31, 128, 32))
+    for h in range(2):
+        lin(w("LV", 4 * h, 4 * h + 4), flv, 1.0, w("XL", 6 + h, 7 + h))
+    fill("LV", 8, 16, 0.0)
+    fill("AV1", 0, 16, 0.0)
 
-    quant("X", 0, ("XB", 0), 256)
-    tt(ti, ti, b1, A.add)
-    pick("XA", 0, 256, "X", 256, ("LST", LISTS["nat"]))
+    lin(col(W0), col(P31), 1.0, float(LAP))
+    lin(col(W1), col(P31), 1.0, OLD + 32.0 * QB)
+    lin(col(W2), col(P31), -1.0, 31.0 - OLD - 32.0 * QB)
+    lin(col(PC), col(P31), 8.0, -MID - 0.5)
+    lin(col(PC3), col(P31), 8.0, 7.25 - MID)
+    lin(col(VPB), col(Q1), 32.0, col(W0))
+    lin(col(OP), col(Q1), 32.0 * (DB - QB), col(W1))
+    lin(col(C1P), col(Q1), 64.0 - 32.0 * (DB - QB), col(W2))
+    lin(w("KX", 0, 32), fkp, 1.0, -0.5)
+    ts(col(SHF), col(RK), float(8 - r), A.is_ge, col(Q1), A.mult)
+    lin(col(W3), col(RK), 1.0, 248.0 - MID)
+    lin(w("DK", 0, 1), col(SHF), 256.0, -8.0)
+    fill("DK", 1, 31, -8.0)
+    lin(w("DK", 31, 32), col(SHF), -8.0, col(W3))
+    fill("DK", 32, 64, 0.0)
+    fill("MK", 32, 64, 1.0)
+    gu, gd = w("TMPI", 16, 18), w("TMPI", 20, 22)
+    fill("LF", 0, 14, 0.0)
+
+    def stage(name, n):
+        a = LISTS[name] - LISTS["ow"]
+        return w("LF", a, a + n)
+    lin(col(VP), col(KK), 2.0)
+    lin(col(CB), col(QQ), -2.0, 8.0 + me)
+    lin(w("S4", 0, 2), w("S4", 0, 2), 1.0, col(KK))
+    ts(gu, w("S4", 0, 2), col(Q1), A.mult, col(CB), A.add)
+    ts(gu, gu, 7, A.bitwise_and)
+    ts(gd, gu, 1, A.arith_shift_right)
+    lin(w("S8", 0, 2), w("S8", 0, 2), 1.0, col(VP))
+    tt(w("S8", 0, 2), w("S8", 0, 2), gu, A.add)
+    ts(w("S4", 0, 2), gd, -2.0 - STEP, A.mult)
+    tt(stage("gx", 2), w("S8", 0, 2), w("S4", 0, 2), A.add)
+    lin(col(VD), col(K2), 8.0, col(M))
+    lin(col(W4), col(Q1), 4.0, 8.0)
+    lin(col(VDB), col(VD), 1.0, col(W4))
+    lin(stage("pp", 4), w("SQ", 0, 4), 1.0, col(P16))
+    lin(stage("ow", 1), col(P8), 1.0, 8.0 * order.index(me))
+    lin(stage("hh", 1), col(B2), 1.0, 6.0)
+    lin(stage("sl", 1), col(B1), 4.0, col(B0))
+    c0, c1, c2, c3 = [{"R": 0.0, "D": 4.0, "S": 6.0}[x] for x in lay]
+    lin(col(Y2), col(B1), c3 - c2 - c1 + c0, c2 - c0)
+    lin(col(Y3), col(B2), col(Y2), col(B0))
+    lin(col(Y4), col(B1), c1 - c0, c0)
+    lin(stage("se", 1), col(Y3), 1.0, col(Y4))
+    cp("v", lst("ow", 14), stage("ow", 14))
+    pick("LA0", LAP, 64, "PB0", 128, ("LST", LISTS["pp"]), OLD)
+    fill("TBL", 0, LAP, 1.0)
+    fill("TBL", LAP, 144, 0.0)
+    fill("SEGH", 0, 384, 1.0)
+    fill("SEGH", 0, 256, 0.0, 64)
+    fill("SEGH", 256, 384, 0.0, 32)
+    fill("MASK", 64, 96, 31.0, 16)
+    ts(w("MASK", 0, 128), w("MASK", 0, 128), col(P31), A.is_equal)
+    ts(w("EM", 0, 32), w("EM", 0, 32), col(B0), A.is_equal)
 
     def with_u(v, bk):
         for h in range(2):
             mm(bk + h, 128, "XA", 256 * v + 128 * h, "S", 0)
         for t in range(v, R):
-            cp("s" if v else "v", w("AV%d" % t, v, 8, 4) if t else w("ACOL", 0, 2), w("ps", 512 * bk + t, 512 * bk + 1024, 512))
+            cp("sv", w("AV%d" % t, v, 8, 4) if t else w("ACOL", 0, 2), w("ps", 512 * bk + t, 512 * bk + 1024, 512))
 
-    def with_w(v):
-        for b in range(4):
-            mm(b, 256, "W", 128 * b, "XA", 256 * v)
-
-    def relu(b):
-        o, i = w("HT", b, 1024, 4), bank(b, 256)
-        run("s", lambda: g.scalar.activation(o[0], i[0], F.Relu, scale=0.0625), [i], [o])
+    def relu(b, bk):
+        o, i = w("HT", b, 1024, 4), bank(bk, 256)
+        either(PLAN["rq"] if bk < 4 else "s", o, i, lambda: g.vector.tensor_scalar(o[0], i[0], 0.0, 0.0625, A.max, A.mult),
+               lambda: g.scalar.activation(o[0], i[0], F.Relu, scale=0.0625))
 
     def unpack(v, new):
         for b in range(4):
             mm(4 + b, 256, "E", (0 if new else 512) + 128 * b, "XA", 256 * (v + new), not new, bool(new))
 
-    def deltas(engines):
+    def version(v):
+        bk = 4 if v else 0
         for b in range(4):
-            cp(engines[b], w("DT", b, 1024, 4), bank(4 + b, 256))
+            mm(bk + b, 256, "W", 128 * b, "XA", 256 * v)
+        if v == 0:
+            with_u(0, 4)
+            arow(0)
+        for b in range(4):
+            relu(b, bk + b)
+        unpack(v, 0)
+        for k in range(0, 256, 128):
+            if v == 1:
+                for j in range(4 * k, 4 * k + 512, 128):
+                    ts(w("HT", j, j + 128), w("HT", j, j + 128), BIG, A.min)
+            quant("XA", 256 * (v + 1) + k, ("HT", 4 * k), 128)
+        unpack(v, 1)
+        for b in range(4):
+            cp("s" if v else PLAN["dq"], w("DT", b, 1024, 4), bank(4 + b, 256))
+            ahead[len(calls) - 1] = PLAN["ahead%d" % v]
+        for k in range(0, 256, 128):
+            quant("DL", 256 * v + k, ("DT", 4 * k), 128)
 
     def arow(t):
-        cp("v", w("RA", 0, 64), ind(w("ACOL", 8 * t, 8 * t + 2), lst("ac", 4)))
+        cp("vs", w("RA", 0, 64), ind(w("ACOL", 8 * t, 8 * t + 2), lst("ac", 4)))
 
+    quant("X", 0, ("XB", 0), 256)
+    quant("S", 0, ("UV", 0), 128)
+    pick("XA", 0, 256, "X", 256, ("LST", LISTS["nat"]))
+    lin(w("NB", 0, 520), eb, -1.0, qs=PLAN["nq"])
     for b in range(4):
         quant("E", 512 + 128 * b, ("NB", 4 - b), 128)
-    cp("v", lst("rg", 12), ti)
-    cp("v", lst("bl", 8), fbl)
-    cp("v", lst("ac", 4), fh)
-    ts(w("XL", 0, 8, 2), w("XI", 0, 8, 2), 0.0, A.add)
-    ts(w("XL", 1, 8, 2), w("XI", 1, 8, 2), 128.0, A.add)
-    ts(w("RST", 0, 128), w("RST", 0, 128), col(P31), A.not_equal)
-    with_u(0, 4)
-    with_w(0)
-    for b in range(4):
-        relu(b)
-    unpack(0, 0)
-    arow(0)
-    cp("v", w("RG", 0, 128), ind(w("XL", 0, 8), lst("rg", 8)))
-    tr(w("MM", 0, 128), w("RG", 0, 128))
-    sfill("TBL", 0, LAP, 1.0)
-    sfill("TBL", LAP, 144, 0.0)
-    if moves:
-        sfill("N1", 8, 32, 0.0)
-        sfill("N2", 8, 32, 0.0)
-    quant("XA", 256, ("HT", 0), 256)
-    unpack(0, 1)
-    cp("v", w("DMP", 31, 128, 32), w("MM", 31, 128, 32))
-    deltas("ssss")
+        quant("E", 128 * b, ("EB", 4 - b), 128)
+    version(0)
     with_u(1, 0)
-    with_w(1)
-    load("y", w("UB", 0, 512), T.u[:, :], [w("N0", 0, 8)])
-    load("y", w("VB", 0, 512), T.v[:, :])
+    version(1)
+    version(2)
+    load("y", w("UB", 0, 512), T.u[:, :], "late", [w("N0", OWN + 1, OWN + 8)])
+    load("y", w("VB", 0, 512), T.v[:, :], "late", [w("N0", OWN + 1, OWN + 8)])
+    quant("U", 0, ("UB", 0), 128)
+    quant("V", 0, ("VB", 0), 128)
 
-    owner = [
-        lambda: field(M), lambda: field(B0), lambda: field(B1), lambda: field(K1),
-        lambda: ts(col(VD), col(K2), 7.0, A.is_equal, -72.0, A.mult),
-        lambda: cp("v", w("FC", M, K1 + 1), w("INTC", M, K1 + 1)),
-        lambda: ts(lst("pp", 2), w("SQ", 0, 2), col(P16), A.add, 32.0 * QB, A.add),
-        lambda: ts(lst("pp", 2, 2), w("SQ", 0, 2), col(P16), A.add, 32.0 * DB, A.add),
-        lambda: ts(col(VD), col(VD), col(M), A.add, col(VP), A.add),
-        lambda: ts(w("MASK", 0, 128), w("MASK", 0, 128), col(P31), A.is_equal),
-        lambda: ts(col(Y2), col(K1), float(QB), A.is_equal, -4.0, A.mult),
-        lambda: (ts(col(Y3), col(K1), 3.0, A.is_ge, 2.0, A.mult) if QB == 0 else ts(col(Y3), col(K1), float(lay.count("S")), A.is_lt, 2.0, A.mult)),
-        lambda: ts(col(VDB), col(Q1), 4.0, A.mult, col(VD), A.add),
-        lambda: pick("LA0", LAP, 64, "PB0", 128, ("LST", LISTS["pp"]), OLD),
-        lambda: ts(col(Y2), col(Y2), col(Y3), A.add, col(B0), A.add),
-        lambda: ts(lst("sl", 1), col(B1), 4.0, A.mult, col(B0), A.add),
-        lambda: ts(w("EM", 0, 32), w("EM", 0, 32), col(B0), A.is_equal),
-        lambda: ts(lst("se", 1), col(Y2), 4.0, A.add)]
+    def across(name, a, n, moves):
+        for q, d, c in moves:
+            k = 64 if d == 2 and (q ^ 1, d, c) in moves else 32
+            if k == 32 or q % 2 == 0:
+                f = 32 * ((q + d) % 4)
+                cp("vs", w(name, c, c + n, 1, 32 * q, 32 * q + k), w(name, a, a + n, 1, f, f + k))
 
     def choose(t):
         n = "N%d" % t
         rb, rr, st = w("RB", 0, 64), w("RR", 0, 64), w("ST", 0, 64)
-        tt(rb, ind(w(n, 0, 8), lst("bl", 4)), w("RA", 0, 64), A.subtract)
+        tt(rb, ind(w(n, OWN - OWN % 8, OWN + 8), lst("bl", 4)), w("RA", 0, 64), A.subtract)
         for j, (to, frm, k) in enumerate(moves):
-            cp("v" if t == 0 or j == 2 else "s", w(n, 8 + 8 * j, 16 + 8 * j, 1, to, to + k), w(n, 0, 8, 1, frm, frm + k))
-        tt(rr, ind(w(n, 0, 32 if moves else 8), lst("bl", 4, 4)), rb, A.add)
+            cp("sv", w(n, 8 * j, 8 + 8 * j, 1, to, to + k), w(n, OWN, OWN + 8, 1, frm, frm + k))
+        tt(rr, ind(w(n, 0, OWN + 8), lst("bl", 4, 4)), rb, A.add)
         tr(st, rr)
         for h in range(2):
             a, z = w("ST", 32 * h, 32 * h + 32), w("RR", 32 * h, 32 * h + 1)
             ts(w("EL", 64 * h, 64 * h + 32), a, z, A.is_equal, -1.0, A.mult)
-            ts(w("EL", 64 * h + 32, 64 * h + 64), a, z, A.is_le)
-        scan(w("CC", 0, 128), w("RST", 0, 128), w("EL", 0, 128))
+            sign(w("EL", 64 * h + 32, 64 * h + 64), a, z)
+        cx, sn, la = "CX%d" % t, "SN%d" % t, "LA%d" % t
         for h in range(2):
-            scan(w("CC", 128, 256, 1, 64 * h, 64 * h + 64), w("RST", 0, 128, 1, 64 - 64 * h, 128 - 64 * h), w("EL", 0, 128, 1, 64 - 64 * h, 128 - 64 * h))
-        for q in range(4):
-            cp("vs"[q % 2], w("XR", 4, 8, 1, 32 * q, 32 * q + 32), w("CC", 63, 256, 64, 32 * ((q + 1) % 4), 32 * ((q + 1) % 4) + 32))
-        cp("v", w("XR", 0, 4), w("CC", 63, 256, 64))
-        if t == 0:
-            quant("DL", 0, ("DT", 0), 256)
-        rg, m, xr = w("RG", 0, 128), w("MM", 0, 128), w("XR", 0, 8)
-        wk, sn, la, kx = "WK%d" % t, "SN%d" % t, "LA%d" % t, "KX%d" % t
-        tt(w("RGK", 0, 32), ind(xr, lst("r2", 2)), w("MT", 0, 32), A.not_equal)
-        tt(rg, ind(xr, lst("rg", 8)), w("MT", 0, 128), A.not_equal)
-        tr(w("MK", 0, 32), w("RGK", 0, 32))
-        tr(m, rg)
-        scan(w("SK", 0, 64), w("MK", 0, 64), w("DK", 0, 64))
-        scan(w("SCN", 0, 128), m, w("DMP", 0, 128))
-        tr(w(wk, 0, 32), w("SK", 32, 64))
-        cp("v", w("L", 0, 4), w("SCN", 31, 128, 32))
-        pick(sn, 0, 64, "DL", 256 * (t + 1), ("L", 0))
-        hs, a = T.sem["hs%d" % t], 32 * (1 - me // HALF)
+            scan(w(cx, PLC - 126 + h, PLC + 2, 2), w("RST", 0, 64), w("EL", 64 * h, 64 * h + 64))
+        to_all(cx, PLC, 2, "ls%d" % t, PLAN["places"])
+        across(cx, PLC, 2, [(q, d, PLC - 8 + 2 * d) for d in (1, 2, 3) for q in range(4)])
+        rg, m, xr = w("RG", 0, 128), w("MM", 0, 128), w(cx, PLC - 6, PLC + 2)
 
         def transfer(kind, o, e):
-            if kind == "key":
-                return ([cores[o]], e, T.sem["ls%d" % t], T[wk][:, 4 * o:4 * o + 4], T[kx][:, 32 + 4 * pos(me, o):36 + 4 * pos(me, o)])
-            if kind == "scale":
-                return ([cores[o]], e, T.sem["dl%d" % t], T["z_" + sn][:, 8 * o:8 * o + 8], T["z_" + la][:, 16 + 8 * pos(me, o):24 + 8 * pos(me, o)])
-            if kind == "code":
-                return ([helpers[o]], e, hs, T["c_" + sn][:, 32 * o:32 * o + 32].bitcast(dt.uint8), T["c_HC%d" % t][:, 0:32].bitcast(dt.uint8))
-            return ([helpers[o]], e, hs, T["z_" + sn][:, a:a + 32], T["z_HZ%d" % t][:, 0:32])
-        src = {"key": w(wk, 0, 32), "scale": w("z_" + sn, 0, 64), "code": w("c_" + sn, 0, 64), "hand": w("z_" + sn, 0, 64)}
-        for call in _calls(me, cores, topo):
-            fused([src[x[0]] for x in call], [transfer(*x) for x in call])
-        run("y", lambda: g.sync.dma_start(T[kx][:, 60:64], T[wk][:, 4 * me:4 * me + 4]), [w(wk, 4 * me, 4 * me + 4)], [w(kx, 60, 64)], dma=True)
-        arrive([w(kx, 32, 60)], "ls%d" % t, sum(_sent(s, "key", me, cores, topo) for s in others))
-        arrive([w("c_" + la, 16, 72), w("z_" + la, 16, 72)], "dl%d" % t, sum(delta_count(s) for s in others))
+            if kind == "hand":
+                what, a, b = HAND[t][o]
+                return ([helpers[o]], e, T.sem["hs%d" % t], _cols(T, what, sn, 8 * a, 8 * (b - a)), [_cols(T, what, "HC%d" % t, 0, 8 * (b - a))])
+            return ([cores[o]], e, T.sem["dl%d" % t], _cols(T, kind, sn, 8 * order.index(o), 8), [_cols(T, kind, la, 8 + 8 * slot(me, o), 8)])
+
+        def send():
+            src = {"scale": w("z_" + sn, 0, 64), "code": w("c_" + sn, 0, 64)}
+            return [fused([src[HAND[t][call[0][1]][0] if call[0][0] == "hand" else call[0][0]]], [transfer(*x) for x in call])
+                    for call in _calls(t, me, cores, topo)]
+        tt(rg, ind(xr, lst("rg", 8)), w("MT", 0, 128), A.not_equal)
+        tr(m, rg)
+        scan(w("SCN", 0, 128), m, w("DMP", 0, 128))
+        cp("v", w("L", 0, 4), w("SCN", 31, 128, 32))
+        pick(sn, 0, 64, "DL", 256 * (t + 1), ("L", 0))
+        arrive([w("c_" + la, 16, 72), w("z_" + la, 16, 72)], "dl%d" % t, sum(delta_count(t, s) for s in others),
+               send(), PLAN["deltas"] + (0 if t else PLAN["cold"]))
+        pick(la, 0, 16, sn, 64, ("LST", LISTS["ow"]))
 
     def advance(t):
-        xl, la = w("XL", 0, 8), "LA%d" % t
-        if t == 0:
-            ts(lst("ow", 1), col(P8), 8.0 * me, A.add)
-            cp("v", lst("hh", 1), col(B2))
-            for h in range(2):
-                sa(w("LV", 4 * h, 4 * h + 4), flv, 1.0, w("XL", h, h + 1))
-            sfill("LV", 8, 16, 0.0)
-            sfill("MASK", 64, 96, 31.0, 16)
-        ts(w("U8", 0, 8), w("XR", 0, 8), 4.0, A.is_lt, 256.0, A.mult)
-        pick(la, 0, 16, "SN%d" % t, 64, ("LST", LISTS["ow"]))
+        xl, u = w("XL", 0, 8), t + 1
+        ts(w("U8", 0, 8), w("CX%d" % t, PLC - 6, PLC + 2), -25.0, A.is_lt, 256.0, A.mult)
+        tt(xl, xl, w("U8", 0, 8), A.add)
         if t < R - 1:
-            for b in range(4):
-                relu(b)
-            unpack(t + 1, 0)
-        if t == 0:
-            for k in range(R):
-                sa(w("KX%d" % k, 0, 32), fkp, 1.0, -0.5)
-            sfill("SEGH", 0, 384, 1.0)
-            sfill("SEGH", 0, 256, 0.0, 64)
-            sfill("SEGH", 256, 384, 0.0, 32)
-        if t < R - 1:
-            u = t + 1
-            chain = [lambda: tt(xl, xl, w("U8", 0, 8), A.add),
-                     lambda: tt(w("VM", 0, 16), ind(xl, lst("hh", 1)), w("LV", 0, 16), A.is_equal),
-                     lambda: tt(w("PV", 0, 8), w("VM", 0, 8), w("AV%d" % u, 0, 8), A.mult),
-                     lambda: (rsum(w("ACOL", 8 * u, 8 * u + 1), w("PV", 0, 4)), rsum(w("ACOL", 8 * u + 1, 8 * u + 2), w("PV", 4, 8))),
-                     lambda: arow(u)]
-            moved = [None, lambda: cp("v", w("MP", 0, 128), ind(xl, lst("rg", 8))), None, lambda: tr(w("MPT", 0, 128), w("MP", 0, 128))]
-            own = [lambda i=i: [f() for f in owner[4 * i:4 * i + 4]] for i in range(5)] if t == 0 else []
-            weave(chain, moved, own)
-            if t == 0:
-                ts(w("HT", 0, 1024), w("HT", 0, 1024), BIG, A.min)
-            quant("XA", 256 * (t + 2), ("HT", 0), 256)
-            unpack(t + 1, 1)
+            tt(w("VM", 0, 16), ind(xl, lst("hh", 1)), w("LV", 0, 16), A.is_equal)
+            tt(w("PV", 0, 8), w("VM", 0, 8), w("AV%d" % u, 0, 8), A.mult)
+            rsum(w("ACOL", 8 * u, 8 * u + 1), w("PV", 0, 4))
+            rsum(w("ACOL", 8 * u + 1, 8 * u + 2), w("PV", 4, 8))
+            arow(u)
+            cp("sv", w("MP", 0, 128), ind(xl, lst("rg", 8)))
+            tr(w("MPT", 0, 128), w("MP", 0, 128))
+            tt(w("DMP", 0, 127), w("MPT", 0, 127), w("MPT", 1, 128), A.subtract)
+            cp("sv", w("DMP", 31, 128, 32), w("MPT", 31, 128, 32))
         else:
-            tt(xl, xl, w("U8", 0, 8), A.add)
             tt(w("FB", 0, 32), ind(xl, lst("fo", 2)), w("EM", 0, 32), A.mult)
             tr(w("FT", 0, 32), w("FB", 0, 32))
             tt(w("FO", 0, 16), w("FT", 0, 32, 2), w("FT", 1, 32, 2), A.add)
             cp("v", w("OUT", 0, 16), w("FO", 0, 16))
             pick("FD", 0, 256, "XA", 1024, ("OUT", 0))
             mm(4, 256, "U", 0, "FD", 0)
-            fd = w("c_FD", 0, 256)
-            store("y", T.oc[:, 0:1024], (fd[0].bitcast(dt.uint8), fd[1]))
+            store("y", T.oc[:, 0:1024], as_bytes(w("c_FD", 0, 256)))
             for k in range(4):
                 store("y", T.osc[4 * k:4 * k + 4, 0:256], w("z_FD", 0, 256, 1, 32 * k, 32 * k + 4))
+            cp("sv", w("YB", 0, 256), w("ps", 2048, 2304))
+            store("y", T.y[:, 0:256], w("YB", 0, 256))
 
     def patch(t):
-        la, kx, pb, pn, last = "LA%d" % t, "KX%d" % t, "PB%d" % t, "PB%d" % (t + 1), t == R - 1
+        la, cx, pb, pn, last = "LA%d" % t, "CX%d" % t, "PB%d" % t, "PB%d" % (t + 1), t == R - 1
+        across(cx, PLC, 16, [(q, d, PLC - STEP * d) for d in (1, 2, 3) for q in range(4) if q // 2 != HR or (q + d) % 4 == QB])
+        tt(w("OH", 0, 32), ind(w(cx, 64, PLC + 16), lst("gx", 2)), w("MT", 0, 32), A.not_equal)
+        tr(w("MK", 0, 32), w("OH", 0, 32))
+        scan(w("SK", 0, 64), w("MK", 0, 64), w("DK", 0, 64))
+        tr(w("KX", 32, 64), w("SK", 32, 64))
         pp, pd, p3 = col(PP), col(PD), col(P3)
-        tr(w("KT", 0, 32), w(kx, 32, 64))
-        for j, (out, key) in enumerate(((pp, col(PC)), (p3, col(PC3)), (pd, w("KT", 0, 1)))):
-            o, i = w("GG", 64 * j, 64 * j + 64), w(kx, 0, 64)
-            run("s", lambda: g.scalar.activation(o[0], i[0], F.Sign, bias=key[0], scale=-1.0, accum_out=out[0]), [i, key], [o, out])
-        wide = 64 if last else 128
-        ts(w("HH", 0, 128), w("WT", 0, 128), pp, A.is_equal, col(VPB), A.mult)
-        ts(col(MK1), p3, pp, A.subtract, 1.0, A.is_gt)
-        ts(col(SU), p3, 0.5, A.mult, col(C1P), A.add)
+        for j, (out, key) in enumerate(((pd, w("SK", 31, 32)), (pp, col(PC)), (p3, col(PC3)))):
+            sign(w("GG", 64 * j, 64 * j + 64), w("KX", 0, 64), key, out)
         ts(w("HH", 128, 256), w("WT", 0, 128), pd, A.is_equal, col(VDB), A.mult)
-        tr(w("HHT", 0, 256, 2), w("HH", 0, 128))
-        ts(col(SU), col(SU), col(MK1), A.mult, col(OP), A.add)
+        ts(w("HH", 0, 128), w("WT", 0, 128), pp, A.is_equal, col(VPB), A.mult)
         tr(w("HHT", 1, 256, 2), w("HH", 128, 256))
-        ts(w("HH", 256, 256 + wide), w("MASK", 0, wide), col(SU), A.mult)
+        tr(w("HHT", 0, 256, 2), w("HH", 0, 128))
         scan(w("SH", 0, 256), w("SEGH", 0, 256), w("HHT", 0, 256))
-        tr(w("HHT", 256, 256 + wide), w("HH", 256, 256 + wide))
         for k in range(2):
             for h in range(2):
-                cp("v", w("AL", 4 * k, 4 * k + 4, 1, 64 * h, 64 * h + 64), w("SH", 63, 256, 64, 64 * k, 64 * k + 64))
+                cp("v", w("AL", 4 * k, 4 * k + 4, 1, 64 * h, 64 * h + 64), w("SH", 63, 256, 64, 64 * (k ^ HR), 64 * (k ^ HR) + 64))
+        wide = 64 if last else 128
+        ts(col(MK1), p3, pp, A.subtract, 1.0, A.is_gt)
+        lin(col(SU), p3, 0.5, col(C1P))
+        lin(col(SU2), col(SU), col(MK1), col(OP))
+        lin(w("HH", 256, 256 + wide), w("MASK", 0, wide), col(SU2))
+        tr(w("HHT", 256, 256 + wide), w("HH", 256, 256 + wide))
         scan(w("SH", 256, 256 + wide), w("SEGH", 256, 256 + wide), w("HHT", 256, 256 + wide))
-        ms, tb, al = w("MS", 0, 128), w("TBL", 0, 144), w("AL", 0, 8)
+        for k in range(2):
+            for h in range(2):
+                cp("sv", w("SX", 4 * k, 4 * k + wide // 32, 1, 64 * h, 64 * h + 64), w("SH", 287, 256 + wide, 32, 64 * (k ^ HR), 64 * (k ^ HR) + 64))
+        cp("v", w("SEL", 0, 16), ind(w("SX", 0, 8), lst("sl" if last else "se", 1)))
+        ms = w("MS", 0, 128)
         pick("AR", 0, 128, la, 144, ("AL", 0))
-        cp("v", ms, ind(tb, al))
+        for k in range(2):
+            cp("sv", w("MS", 64 * k, 64 * k + 64), ind(w("TBL", 0, 144), w("AL", 4 * k, 4 * k + 4)))
         for b in range(4):
             mm(b, 128, "E", 128 * b, "AR", 0)
-        for k in range(2):
-            for h in range(2):
-                cp("s", w("SX", 4 * k, 4 * k + wide // 32, 1, 64 * h, 64 * h + 64), w("SH", 287, 256 + wide, 32, 64 * k, 64 * k + 64))
-        if last:
-            cp("s", w("YB", 0, 256), w("ps", 2048, 2304))
-            store("y", T.y[:, 0:256], w("YB", 0, 256))
         for b in range(4):
             scan(w("NT", b, 512, 4), ms, bank(b, 128))
-        cp("v", w("SEL", 0, 16), ind(w("SX", 0, 8), lst("sl" if last else "se", 1)))
         quant(pb, 0, ("NT", 0), 128)
         if not last:
             pick(pn, OLD, 128, pb, 256, ("SEL", 0))
             scores(t + 1)
-            deltas("vsvs")
-            tt(w("DMP", 0, 127), w("MPT", 0, 127), w("MPT", 1, 128), A.subtract)
             if t == 0:
                 with_u(2, 1)
-                with_w(2)
-            quant("DL", 256 * (t + 1), ("DT", 0), 256)
-            cp("v", w("DMP", 31, 128, 32), w("MPT", 31, 128, 32))
             pick("LA%d" % (t + 1), LAP, 64, pn, 128, ("LST", LISTS["pp"]), OLD)
-            if t == 1:
-                quant("U", 0, ("UB", 0), 128)
-                quant("V", 0, ("VB", 0), 128)
         else:
             pick("FD", 256, 64, pb, 256, ("SEL", 0))
             mm(0, 128, "V", 0, "FD", 192)
-            cc = w("c_FD", 256, 320)
-            store("y", T.oc[:, 1024:1280], (cc[0].bitcast(dt.uint8), cc[1]))
+            store("y", T.oc[:, 1024:1280], as_bytes(w("c_FD", 256, 320)))
             for k in range(4):
                 store("ys"[k % 2], T.osc[4 * k:4 * k + 4, 256:320], w("z_FD", 256, 320, 1, 32 * k, 32 * k + 4))
-            cp("v", w("YB", 256, 320), bank(0, 64, 64))
+            cp("vs", w("YB", 256, 320), bank(0, 64, 64))
             store("s", T.y[:, 256:320], w("YB", 256, 320))
 
     for t in range(R):
         choose(t)
         advance(t)
         patch(t)
+
+    csem = {"g": "qg", "v": "qv", "s": "qs", "t": "qt"}
+    pre = _before(calls)
+    total, known, ends, on = {"snt": sent[0]}, {q: {} for q in Q}, {}, {}
+    ndma = 0
+    plan = _plan(calls, ahead)
+    for j, q in sorted(x for x in plan if x[0] < n_loads) + [x for x in plan if x[0] >= n_loads]:
+        ways, reads, writes, what, late, after = calls[j]
+        on[j] = q
+        if what == "arrive":
+            total[q] = ways[q][0]
+            ends[j] = (q, total[q], {q: total[q]})
+            continue
+        need = {}
+        for i, soft in pre[j].items():
+            if i in ends and not (soft and on[i] == q):
+                sem, n, clock = ends[i]
+                if known[q].get(sem, 0) < n and need.get(sem, (0,))[0] < n:
+                    need[sem] = (n, clock)
+        for sem in sorted(need):
+            if not any(s2 != sem and c2.get(sem, 0) >= need[sem][0] for s2, (n2, c2) in need.items()):
+                Q[q].wait_ge(T.sem[sem], need[sem][0])
+        for n, clock in need.values():
+            for k, v in clock.items():
+                known[q][k] = max(known[q].get(k, 0), v)
+        if what == "send":
+            ways[q][0]()
+            continue
+        if what == "dma":
+            sem, inc = "m%d" % ndma, 16
+            ndma += 1
+        else:
+            sem, inc = csem[q], 1
+        total[sem] = total.get(sem, 0) + inc
+        ways[q][0]().then_inc(T.sem[sem], inc)
+        ends[j] = (sem, total[sem], dict(known[q], **{sem: total[sem]}))
     for sem in sorted(total):
         if known["g"].get(sem, 0) < total[sem]:
             g.wait_ge(T.sem[sem], total[sem])

from concourse.bass import DstId, RemoteDMATransfer
from concourse.mybir import dt, AluOpType as A, ActivationFunctionType as F, AxisListType as AX

R = 3
OWN = 27
HAND = [(("code", 1, 4), ("code", 4, 7), ("scale", 1, 4))] * R
NEAR = 4
PLC = 134
STEP = 22
MID = 124
OLD = 128
LAP = 80
BIG = 2.0 ** 60
PLAN = dict(gap=210, room=20, sure=100, send=300, first=(2200, 600), small=1100, pr=1250, x=1800, w=3100, late=1600, store=1200,
            scores=1500, places=2000, deltas=2700, cold=400, begin=2000, gfill=1, ahead0=800, ahead1=0, ahead2=0, rq="s", dq="sv", nq="v")
FP8, U8, BF, F32, I32, U16 = "float8_e4m3fn_x4", "uint8", "bfloat16", "float32", "int32", "uint16"
SCRATCH = {"ps": ("psum", [128, 4096], F32)}


def _add(d, text, mx=False):
    for item in text.split():
        name, n = item.split(":")
        if mx:
            SCRATCH["c_" + name] = ("sbuf", [128, int(n)], FP8)
            SCRATCH["z_" + name] = ("sbuf", [128, int(n)], U8)
        else:
            SCRATCH[name] = ("sbuf", [128, int(n)], d)


_add(BF, "XB:1024 PT:512 UB:512 VB:512 UV:528 ONE:520 EB:520 NB:520 HT:1024 DT:1024 NT:512 "
         "KX:64 CX0:152 CX1:152 CX2:152 KW:256 CT:1072 GG:192 HH:384 HHT:384 SH:384 MS:128 "
         "EL:128 RG:128 MM:128")
_add(FP8, "X:256 U:128 V:128 S:256 W:512 E:1024 XA:1024 FD:320 DL:768 PB0:256 PB1:256 PB2:256 "
          "SN0:64 SN1:64 SN2:64 LA0:144 LA1:144 LA2:144 AR:128 HC0:32 HC1:32 HC2:32", mx=True)
_add(F32, "N0:36 N1:36 N2:36 FC:64 SM:240 TMPF:72 RA:64 RB:64 RR:64 ST:64 SCN:128 DMP:128 MP:128 MPT:128 YB:320")
_add(I32, "PI:8 XI:8 INTC:16 TMPI:48")
ALIAS = {}
for _buf, _text in (("SM", "XL:0 ACOL:8 AV1:32 AV2:40 LV:48 VM:64 PV:80 U8:88 SX:96 FB:136 FT:168 FO:200 SQ:216 S4:220 S8:222 LF:224"),
                    ("CT", "TBL:0 WT:144 MASK:272 SEGH:400 MT:784 RST:912 EM:1040"),
                    ("KW", "OH:0 MK:32 SK:96 DK:192"),
                    ("TMPF", "FNAT:0 FBL:16 FH:24 FRG:28 FLV:36 FKP:40"),
                    ("LW", "OUT:0 SEL:16 AL:32 L:40")):
    for _item in _text.split(" "):
        ALIAS[_item.split(":")[0]] = (_buf, int(_item.split(":")[1]))
LISTS = {"nat": 0, "bl": 16, "ac": 24, "rg": 28, "fo": 36, "ow": 40, "hh": 42, "se": 44, "sl": 46, "pp": 48, "gx": 52}
_add(U16, "LST:54 LW:44")
SEMAPHORES = (["qg", "qv", "qs", "qt", "snt"] + [s + str(t) for s in ("sc", "dl", "ls", "hs") for t in range(R)]
              + ["m%d" % i for i in range(48)])


def _blocks(o):
    b = o // 2
    lay = ["R" if q == b else "D" if q > b else "S" for q in range(4)]
    if b == 0:
        lay[3] = "S"
    if b == 3:
        lay[2] = "D"
    return lay


def _fetch(r):
    need, col = [], {}
    for k in range(8):
        o, q, kind = (k - r) % 8, k // 2, "D" if k >= r else "S"
        col[k] = OWN + (o - r) % 8
        if _blocks(o)[q] != kind:
            need.append((k, [x for x in range(4) if _blocks(o)[x] == kind]))
    ways = [[]]
    for k, src in need:
        ways = [x + [(64 * (k // 4), 64 - 64 * (k // 4), 64) if s == (k // 2 + 2) % 4 else (32 * (k // 2), 32 * s, 32)] for x in ways for s in src]
    way = min(ways, key=lambda x: len(set(x)))
    moves = sorted(set(way), key=lambda x: (-x[2], x))
    for (k, src), mv in zip(need, way):
        col[k] += 8 * moves.index(mv) - OWN
    return moves, col


def slot(s, d):
    return (s - d) % 8


def bits(e):
    return sum(1 << x for x in e)


def _far(s, cores, topo):
    return [o for o in range(len(cores)) if o != s and topo.chip(cores[s]) != topo.chip(cores[o])]


def _near(src, dst, away, topo):
    return [x for x in topo.engines(src, dst) if x not in away]


def _helpers(s, cores, topo):
    return [c for c in topo.cores_of(cores[s]) if topo.die(c) == topo.die(cores[s]) and c not in cores][:3]


def _order(s, cores, topo):
    fs = _far(s, cores, topo)
    first = max(o for o in range(len(cores)) if o not in fs)
    return [(first + j) % len(cores) for j in range(len(cores))]


def _share(kind, dests, engines):
    n = max(x for x in (1, 2, 4, 8, 16) if x * len(dests) <= len(engines))
    return [(kind, d, engines[n * i:n * i + n]) for i, d in enumerate(dests)]


def _waves(kind, dests, src, s, cores, topo):
    fs = [o for o in dests if o in _far(s, cores, topo)]
    away = topo.engines(src, cores[fs[0]])
    calls = []
    while fs:
        n = max(x for x in (1, 2, 4) if x <= len(fs))
        calls.append(_share(kind, fs[:n], away))
        fs = fs[n:]
    calls[0] += [(kind, o, _near(src, cores[o], away, topo)[:NEAR]) for o in dests if o not in _far(s, cores, topo)]
    return calls


def _hand(t, s, k, cores, topo):
    kind, a, b = HAND[t][k]
    return _waves(kind, [o for o in _order(s, cores, topo)[a:b] if o != s], _helpers(s, cores, topo)[k], s, cores, topo)


def _calls(t, s, cores, topo):
    order = _order(s, cores, topo)
    away = topo.engines(cores[s], cores[_far(s, cores, topo)[0]])
    close = _near(cores[s], _helpers(s, cores, topo)[0], away, topo)
    left = {x: [o for o in order if o != s and not any(kind == x and o in order[a:b] for kind, a, b in HAND[t])] for x in ("code", "scale")}
    return ([_share("hand", [0, 1], close), _share("hand", [2], close)]
            + _waves("scale", left["scale"], cores[s], s, cores, topo) + [_share("code", [o], close) for o in left["code"]])


def _sent(calls, kind, d):
    return sum(len(e) for call in calls for k, o, e in call if (k, o) == (kind, d))


def _to(core, topo):
    rid, pid = topo.addr(core)[:2]
    return DstId(rid=rid, pnc=pid)


def _cols(T, kind, name, a, n):
    return T["c_" + name][:, a:a + n].bitcast(dt.uint8) if kind == "code" else T["z_" + name][:, a:a + n]


def hand_on(g, core, s, cores, T, topo):
    k = _helpers(s, cores, topo).index(core)
    order, sent = _order(s, cores, topo), 0
    for t in range(R):
        g.wait_ge(T.sem["hs%d" % t], _sent(_calls(t, s, cores, topo), "hand", k))
        for call in _hand(t, s, k, cores, topo):
            g.remote_dma_fused([RemoteDMATransfer(dst_ids=[_to(cores[o], topo)], dma_engine_mask=bits(e), remote_sem=T.sem["dl%d" % t],
                                                  srcs=[_cols(T, kind, "HC%d" % t, 8 * (order.index(o) - HAND[t][k][1]), 8)],
                                                  dsts=[_cols(T, kind, "LA%d" % t, 8 + 8 * slot(s, o), 8)]) for kind, o, e in call], local_sem=T.sem.snt)
            sent += sum(len(e) for kind, o, e in call)
    g.wait_ge(T.sem.snt, sent)


def _before(calls):
    hist, sends, out = {}, [], []
    for j, (ways, reads, writes, what, late, after) in enumerate(calls):
        pre = {i: False for i in after}
        for regions, wr in ((reads, False), (writes, True)):
            for name, cols, p0, p1 in regions:
                for c, a, b, w2, i in hist.get(name, ()):
                    if c & cols and a < p1 and p0 < b and (wr or w2 or name == "ps"):
                        pre[i] = pre.get(i, True) and name == "ps" and wr == w2
        if what == "send" and sends:
            pre.setdefault(sends[-1], True)
        if what == "send":
            sends.append(j)
        for name, cols, p0, p1 in writes:
            hist[name] = [h for h in hist.get(name, ()) if not (h[0] & ~cols == 0 and p0 <= h[1] and h[2] <= p1)] + [(cols, p0, p1, True, j)]
        for name, cols, p0, p1 in reads:
            hist.setdefault(name, []).append((cols, p0, p1, False, j))
        out.append(pre)
    return out


def _plan(calls, ahead):
    pre, gap = _before(calls), PLAN["gap"]
    span = [max(min(c for f, c in x[0].values()), x[4]) for x in calls]
    chain = list(span)
    for j in range(len(calls) - 1, -1, -1):
        chain[j] += ahead.get(j, 0)
        for i, soft in pre[j].items():
            chain[i] = max(chain[i], span[i] + (0 if soft else gap) + chain[j])
    busy, start, done, on = {}, {}, {}, {}
    for j in sorted(range(len(calls)), key=lambda j: (-chain[j], j)):
        best = None
        for q, (f, c) in calls[j][0].items():
            t = max([0] + [done[i] + (0 if soft and on[i] == q else gap) for i, soft in pre[j].items()])
            sure = max([0] + [done[i] + gap + PLAN["sure"] for i in pre[j] if on[i] != q])
            for a, b in busy.get(q, ()):
                if max(t, sure) + c + PLAN["room"] <= a:
                    break
                t = max(t, b)
            if best is None or t + c < best[0]:
                best = (t + c, t, q, c)
        end, t, q, c = best
        busy[q] = sorted(busy.get(q, []) + [(t, end)])
        start[j], done[j], on[j] = t, t + max(c, calls[j][4]), q
    return [(j, on[j]) for j in sorted(start, key=lambda j: (start[j], j))]


def rank_program(g, core, T, topo):
    cores = [int(c) for c in T.cores]
    n_ranks = len(cores)
    me = T.rank_of(core)
    if me is None:
        for s in range(n_ranks):
            if core in _helpers(s, cores, topo):
                hand_on(g, core, s, cores, T, topo)
        return
    r = me
    calls, ahead = [], {}

    def w(name, c0, c1, step=1, p0=0, p1=128):
        if name in ALIAS:
            name, c0, c1 = ALIAS[name][0], c0 + ALIAS[name][1], c1 + ALIAS[name][1]
        t, n = T[name], len(range(c0, c1, step))
        if p0 == 0 and p1 == 128:
            a = t[:, c0:c1] if step == 1 else t[:, c0:c1:step]
        else:
            a = t[p0:p1, c0:c1] if step == 1 else t[p0:p1, c0:c1:step]
        if name == "ps":
            return (a, [(name, sum(1 << b for b in range(c0 // 512, (c1 + 511) // 512)), 0, 128)], n, False)
        cols = ((1 << (c1 - c0)) - 1) << c0 if step == 1 else sum(1 << c for c in range(c0, c1, step))
        return (a, [(name, cols, p0, p1)], n, SCRATCH[name][2] in (BF, U16))

    def ind(v, o):
        return (v[0].indirect(o[0]), v[1] + o[1], 16 * o[2], None)

    def lst(name, n, off=0):
        a = LISTS[name] + off
        return w("LST", a, a + n)

    def as_bytes(v):
        return (v[0].bitcast(dt.uint8),) + v[1:]

    def put(ways, reads, writes, what="compute", late=0, after=()):
        calls.append((ways, [x for v in reads for x in v[1]], [x for v in writes for x in v[1]], what, late, after))
        return len(calls) - 1

    def cycles(q, out, a, k=1):
        if a[3] is None:
            return 60 + 1.6 * a[2]
        return max(64, k * a[2] * (0.5 if q == "v" and k == 1 and out[3] and a[3] else 1))

    def S(x):
        return x[0] if isinstance(x, tuple) else x

    def deps(*xs):
        return [x for x in xs if isinstance(x, tuple)]

    def either(qs, out, a, on_v, on_s, more=()):
        ways = {"v": (on_v, cycles("v", out, a)), "s": (on_s, cycles("s", out, a))}
        put({q: ways[q] for q in qs}, [a] + list(more), [out])

    def cp(qs, out, a):
        either(qs, out, a, lambda: g.vector.tensor_copy(out[0], a[0]), lambda: g.scalar.activation(out[0], a[0], F.Copy))

    def lin(out, a, scale=1.0, bias=0.0, qs="sv"):
        either(qs, out, a, lambda: g.vector.tensor_scalar(out[0], a[0], S(scale), S(bias), A.mult, A.add),
               lambda: g.scalar.activation(out[0], a[0], F.Identity, bias=S(bias), scale=S(scale)), deps(scale, bias))

    def fill(name, a, b, c, step=1):
        out, one = w(name, a, b, step), w("ONE", 0, len(range(a, b, step)))
        ways = {"s": (lambda: g.scalar.activation(out[0], one[0], F.Identity, bias=c, scale=0.0), cycles("s", out, one)),
                "v": (lambda: g.vector.memset(out[0], c), cycles("v", out, one))}
        if step == 1 and PLAN["gfill"]:
            ways["g"] = (lambda: g.iota(out[0], [[0, b - a]], int(c), 0, allow_small_or_imprecise_dtypes=True), 150 + 2 * out[2])
        put(ways, [one], [out])

    def sign(out, a, z, total=None):
        if total is None:
            put({"s": (lambda: g.scalar.activation(out[0], a[0], F.Sign, bias=z[0], scale=-1.0), cycles("s", out, a))}, [a, z], [out])
        else:
            put({"s": (lambda: g.scalar.activation(out[0], a[0], F.Sign, bias=z[0], scale=-1.0, accum_out=total[0]), cycles("s", out, a) + 24)}, [a, z], [out, total])

    def tt(out, a, b, op):
        put({"v": (lambda: g.vector.tensor_tensor(out[0], a[0], b[0], op), cycles("v", out, a, 2))}, [a, b], [out])

    def ts(out, a, s1, op0, s2=None, op1=None):
        if op1 is None:
            put({"v": (lambda: g.vector.tensor_scalar(out[0], a[0], S(s1), None, op0), cycles("v", out, a))}, [a] + deps(s1), [out])
        else:
            put({"v": (lambda: g.vector.tensor_scalar(out[0], a[0], S(s1), S(s2), op0, op1), cycles("v", out, a))}, [a] + deps(s1, s2), [out])

    def tr(out, a):
        put({"v": (lambda: g.vector.transpose(out[0], a[0]), cycles("v", out, a))}, [a], [out])

    def scan(out, a, b):
        put({"v": (lambda: g.vector.tensor_tensor_scan(out[0], a[0], b[0], 0.0, A.mult, A.add), max(cycles("v", out, a), cycles("v", out, b)))}, [a, b], [out])

    def rsum(out, a):
        put({"v": (lambda: g.vector.tensor_reduce(out[0], a[0], AX.X, A.add), max(64, a[2]))}, [a], [out])

    def iota(out, pattern, base=0, ch=0, small=True):
        if small:
            put({"g": (lambda: g.iota(out[0], pattern, base, ch, allow_small_or_imprecise_dtypes=True), 150 + 2 * out[2])}, [], [out])
        else:
            put({"g": (lambda: g.iota(out[0], pattern, base, ch), 150 + 2 * out[2])}, [], [out])

    def quant(name, c0, src, n):
        c, z, a = w("c_" + name, c0, c0 + n), w("z_" + name, c0, c0 + n), w(src[0], src[1], src[1] + 4 * n)
        put({"v": (lambda: g.vector.quantize_mx(c[0], z[0], a[0]), 15 + 1.06 * n)}, [a], [c, z])

    def pick(dst, d0, n, src, width, off, a0=0):
        b, k = off
        o = w(b, k, k + n // 16)
        co, ci = w("c_" + dst, d0, d0 + n), w("c_" + src, a0, a0 + width)
        put({"v": (lambda: g.vector.tensor_copy(co[0].bitcast(dt.uint32), ci[0].bitcast(dt.uint32).indirect(o[0])), 60 + 1.6 * n)}, [ci, o], [co])
        cp("s", w("z_" + dst, d0, d0 + n), ind(w("z_" + src, a0, a0 + width), o))

    def mm(bank, n, lhs, l0, rhs, r0, start=True, stop=True):
        out = w("ps", 512 * bank, 512 * bank + n)
        a, az = w("c_" + lhs, l0, l0 + 128), w("z_" + lhs, l0, l0 + 128)
        b, bz = w("c_" + rhs, r0, r0 + n), w("z_" + rhs, r0, r0 + n)
        put({"t": (lambda: g.tensor.matmul_mx(out[0], a[0], az[0], b[0], bz[0], start, stop), 0.6 * (n + 16))}, [a, az, b, bz], [out])

    def bank(b, n, c0=0):
        return w("ps", 512 * b + c0, 512 * b + c0 + n)

    Q = {"g": g, "v": g.vector, "s": g.scalar, "t": g.tensor, "y": g.sync}

    def load(q, out, a, late, after=()):
        put({q: (lambda: Q[q].dma_start(out[0], a), 60)}, list(after), [out], "dma", PLAN[late])

    def store(q, a, src):
        put({q: (lambda: Q[q].dma_start(a, src[0]), 60)}, [src], [], "dma", PLAN["store"])

    others = [o for o in range(n_ranks) if o != me]
    afar = _far(me, cores, topo)
    away = topo.engines(core, cores[afar[0]])
    helpers, order = _helpers(me, cores, topo), _order(me, cores, topo)
    sent = [0]

    def fused(reads, transfers, cost=PLAN["send"]):
        sent[0] += sum(len(x[1]) for x in transfers)
        tf = [RemoteDMATransfer(dst_ids=[_to(c, topo) for c in ds], dma_engine_mask=bits(e), remote_sem=sem, srcs=[src], dsts=lands)
              for ds, e, sem, src, lands in transfers]
        return put({"g": (lambda: g.remote_dma_fused(tf, local_sem=T.sem.snt), cost)}, reads, [], "send")

    def arrive(views, sem, n, after, late):
        put({sem: (n, 0)}, [], views, "arrive", late - PLAN["gap"] - sum(calls[j][0]["g"][1] for j in after), after)

    def to_all(name, a, n, sem, late, first=False):
        src = w(name, a, a + n)
        land = {o: T[name][:, a + n * slot(me, o):a + n + n * slot(me, o)] for o in others}
        far = [([cores[o] for o in afar], away, T.sem[sem], src[0], [land[o] for o in afar])]
        near = [([cores[o]], _near(core, cores[o], away, topo)[:len(away) if first else 2], T.sem[sem], src[0], [land[o]]) for o in others if o not in afar]
        sends = [fused([src], call, cost) for call, cost in zip((far, near), PLAN["first"])] if first else [fused([src], far + near)]
        if first:
            ahead[sends[0]] = PLAN["ahead0"]
        arrive([w(name, a + n, a + 8 * n)], sem, sum(len(away) if s in afar or first else 2 for s in others), sends, late)

    def delta_count(t, s):
        cs = _calls(t, s, cores, topo) + [c for k in range(len(helpers)) for c in _hand(t, s, k, cores, topo)]
        return _sent(cs, "scale", me) + _sent(cs, "code", me)

    lay = _blocks(me)
    QB, DB = lay.index("R"), lay.index("D")
    HR = QB // 2
    moves, ccol = _fetch(r)

    load("s", w("PT", 128 * DB, 128 * DB + 128), T.pd[:, :], "small")
    load("y", w("UV", 16, 32), T.v[:, 0:16], "small")
    load("s", w("PT", 128 * QB, 128 * QB + 128), T.pr[:, :], "pr")
    load("y", w("XB", 0, 1024), T.x[:, :], "x")
    load("s", w("UV", 0, 16), T.u[:, 0:16], "x")
    load("s", w("z_W", 0, 512), T.ws[:, :], "x")
    load("y", as_bytes(w("c_W", 0, 512)), T.wc[:, :], "w")
    n_loads = len(calls)

    fnat, fh, frg, fbl, flv, fkp = w("FNAT", 0, 16), w("FH", 0, 4), w("FRG", 0, 8), w("FBL", 0, 8), w("FLV", 0, 4), w("FKP", 0, 32)
    eb, one = w("EB", 0, 520), w("ONE", 0, 520)
    put({"v": (lambda: g.vector.memset(one[0], 1.0), 260)}, [], [one])
    iota(w("PI", 3, 7), [[4 * me, 2], [64 * HR, 2]], 0, 1, small=False)
    for k in range(3):
        iota(w("PI", k, k + 1), [[0, 1]], 0, 8 >> k, small=False)
    iota(fh, [[1, 2], [0, 2]])
    iota(fnat, [[1, 2], [2, 4], [128, 2]])
    iota(frg, [[2, 4], [0, 2]], order[0])
    iota(w("XI", 0, 8), [[32, 4], [0, 2]], 32, 1, small=False)
    put({"g": (lambda: g.affine_select(eb[0], one[0], [[-1, 520]], A.is_equal, 0.0, 4, 4), 1240)}, [one], [eb])
    fill("UV", 32, 528, 0.0)

    def col(j):
        return w("FC", j, j + 1)
    P16, P31, QQ, B0, B1, B2, B3, P8, K2, RK, M, KK, Q1 = range(13)
    C8P, CA, CB, CQ, SHF, PC, PC3, VP, VD, OP, C1P, MK1, SU, Y2, Y3, PP, PD, P3, VPB, VDB, W0, W1, W2, W3, W4, SU2, Y4 = range(16, 43)
    for j, n, a, step, sh, an in ((P16, 1, 3, 1, 0, 15), (P31, 1, 3, 1, 0, 31), (QQ, 1, 3, 1, 5, 3), (B0, 4, 0, 1, 3, 1), (P8, 3, 1, 2, 2, 7),
                                  (M, 2, 1, 2, 2, 3), (Q1, 1, 4, 1, 6, 1)):
        o, i = w("INTC", j, j + n), w("PI", a, a + step * (n - 1) + 1, step)
        if sh:
            ts(o, i, sh, A.arith_shift_right, an, A.bitwise_and)
        else:
            ts(o, i, an, A.bitwise_and)
    cp("v", w("FC", P16, P16 + 1), w("INTC", P16, P16 + 1))
    cp("v", w("FC", P31, Q1 + 1), w("INTC", P31, Q1 + 1))

    for b in range(4):
        a, d = 128 * b, 128 * DB
        for o0, o1, i0 in {"R": [], "D": [(0, 128, 0)] if b != DB else [], "S": [(4, 128, 0), (0, 4, 124)]}[lay[b]]:
            cp("vs", w("PT", a + o0, a + o1), w("PT", d + i0, d + i0 + o1 - o0))
    quant("S", 128, ("UV", 16), 128)
    quant("PB0", OLD, ("PT", 0), 128)

    def scores(t):
        n = "N%d" % t
        mm(0, 128, "PB%d" % t, OLD, "S", 128)
        cp("sv", w(n, OWN, OWN + 1), w("ps", t, t + 1))
        to_all(n, OWN, 1, "sc%d" % t, PLAN["scores"] + (0 if t else PLAN["begin"]), t == 0)

    scores(0)
    iota(w("RST", 0, 64), [[1, 64]])
    iota(w("MT", 0, 128), [[0, 32], [2, 4]], -32)
    iota(fkp, [[8, 32]], -MID)
    iota(flv, [[256, 4]])
    iota(w("SQ", 0, 4), [[32 * (DB - QB), 2], [16, 2]], 32 * QB)
    iota(w("S4", 0, 2), [[4, 2]], me)
    iota(w("S8", 0, 2), [[8, 2]], PLC - 64)
    iota(w("MASK", 0, 64), [[16, 2], [0, 2], [1, 16]])
    iota(w("MASK", 64, 128), [[16, 2], [0, 2], [1, 16]], -1)
    iota(w("WT", 0, 128), [[32, 4], [0, 2], [2, 16]], -63)
    iota(w("EM", 0, 32), [[0, 2], [1, 2], [0, 8]])

    ti, xi = w("TMPI", 0, 10), w("XI", 0, 8)
    lin(col(C8P), col(P16), 8.0)
    lin(col(CQ), col(QQ), -2.0, 6.0)
    lin(col(CA), col(B2), float(r), col(B3))
    ts(lst("nat", 16), fnat, col(C8P), A.add)
    ts(w("TMPI", 0, 8), frg, col(CA), A.add, col(CQ), A.add)
    ts(w("TMPI", 8, 10), w("ONE", 0, 2), col(P8), A.mult, col(CQ), A.add)
    ts(ti, ti, 7, A.bitwise_and)
    cp("v", lst("rg", 10), ti)
    for q in range(4):
        for a, c0, c1 in ((0, OWN % 8 + slot(2 * q, me), OWN % 8 + slot(2 * q + 1, me)), (4, ccol[2 * q], ccol[2 * q + 1])):
            lin(w("FBL", a, a + 4, 1, 32 * q, 32 * q + 32), w("FH", 0, 4, 1, 32 * q, 32 * q + 32), float(c1 - c0), float(c0))
    cp("v", lst("bl", 12), w("FBL", 0, 12))
    for t in range(R):
        fill("N%d" % t, 0, OWN, 0.0)
    ts(w("RST", 0, 64), w("RST", 0, 64), col(P31), A.is_equal, -2.0, A.mult)
    lin(w("RST", 0, 64), w("RST", 0, 64), 1.0, 1.0)
    ts(xi, xi, 127, A.bitwise_and)
    cp("v", w("XL", 0, 8), xi)
    lin(w("XL", 1, 8, 2), w("XL", 1, 8, 2), 1.0, 128.0)
    fill("DMP", 0, 128, -1.0)
    cp("vs", w("RG", 0, 128), ind(w("XL", 0, 8), lst("rg", 8)))
    tr(w("MM", 0, 128), w("RG", 0, 128))
    cp("vs", w("DMP", 31, 128, 32), w("MM", 31, 128, 32))
    for h in range(2):
        lin(w("LV", 4 * h, 4 * h + 4), flv, 1.0, w("XL", 6 + h, 7 + h))
    fill("LV", 8, 16, 0.0)
    fill("AV1", 0, 16, 0.0)

    lin(col(W0), col(P31), 1.0, float(LAP))
    lin(col(W1), col(P31), 1.0, OLD + 32.0 * QB)
    lin(col(W2), col(P31), -1.0, 31.0 - OLD - 32.0 * QB)
    lin(col(PC), col(P31), 8.0, -MID - 0.5)
    lin(col(PC3), col(P31), 8.0, 7.25 - MID)
    lin(col(VPB), col(Q1), 32.0, col(W0))
    lin(col(OP), col(Q1), 32.0 * (DB - QB), col(W1))
    lin(col(C1P), col(Q1), 64.0 - 32.0 * (DB - QB), col(W2))
    lin(w("KX", 0, 32), fkp, 1.0, -0.5)
    ts(col(SHF), col(RK), float(8 - r), A.is_ge, col(Q1), A.mult)
    lin(col(W3), col(RK), 1.0, 248.0 - MID)
    lin(w("DK", 0, 1), col(SHF), 256.0, -8.0)
    fill("DK", 1, 31, -8.0)
    lin(w("DK", 31, 32), col(SHF), -8.0, col(W3))
    fill("DK", 32, 64, 0.0)
    fill("MK", 32, 64, 1.0)
    gu, gd = w("TMPI", 16, 18), w("TMPI", 20, 22)
    fill("LF", 0, 14, 0.0)

    def stage(name, n):
        a = LISTS[name] - LISTS["ow"]
        return w("LF", a, a + n)
    lin(col(VP), col(KK), 2.0)
    lin(col(CB), col(QQ), -2.0, 8.0 + me)
    lin(w("S4", 0, 2), w("S4", 0, 2), 1.0, col(KK))
    ts(gu, w("S4", 0, 2), col(Q1), A.mult, col(CB), A.add)
    ts(gu, gu, 7, A.bitwise_and)
    ts(gd, gu, 1, A.arith_shift_right)
    lin(w("S8", 0, 2), w("S8", 0, 2), 1.0, col(VP))
    tt(w("S8", 0, 2), w("S8", 0, 2), gu, A.add)
    ts(w("S4", 0, 2), gd, -2.0 - STEP, A.mult)
    tt(stage("gx", 2), w("S8", 0, 2), w("S4", 0, 2), A.add)
    lin(col(VD), col(K2), 8.0, col(M))
    lin(col(W4), col(Q1), 4.0, 8.0)
    lin(col(VDB), col(VD), 1.0, col(W4))
    lin(stage("pp", 4), w("SQ", 0, 4), 1.0, col(P16))
    lin(stage("ow", 1), col(P8), 1.0, 8.0 * order.index(me))
    lin(stage("hh", 1), col(B2), 1.0, 6.0)
    lin(stage("sl", 1), col(B1), 4.0, col(B0))
    c0, c1, c2, c3 = [{"R": 0.0, "D": 4.0, "S": 6.0}[x] for x in lay]
    lin(col(Y2), col(B1), c3 - c2 - c1 + c0, c2 - c0)
    lin(col(Y3), col(B2), col(Y2), col(B0))
    lin(col(Y4), col(B1), c1 - c0, c0)
    lin(stage("se", 1), col(Y3), 1.0, col(Y4))
    cp("v", lst("ow", 14), stage("ow", 14))
    pick("LA0", LAP, 64, "PB0", 128, ("LST", LISTS["pp"]), OLD)
    fill("TBL", 0, LAP, 1.0)
    fill("TBL", LAP, 144, 0.0)
    fill("SEGH", 0, 384, 1.0)
    fill("SEGH", 0, 256, 0.0, 64)
    fill("SEGH", 256, 384, 0.0, 32)
    fill("MASK", 64, 96, 31.0, 16)
    ts(w("MASK", 0, 128), w("MASK", 0, 128), col(P31), A.is_equal)
    ts(w("EM", 0, 32), w("EM", 0, 32), col(B0), A.is_equal)

    def with_u(v, bk):
        for h in range(2):
            mm(bk + h, 128, "XA", 256 * v + 128 * h, "S", 0)
        for t in range(v, R):
            cp("sv", w("AV%d" % t, v, 8, 4) if t else w("ACOL", 0, 2), w("ps", 512 * bk + t, 512 * bk + 1024, 512))

    def relu(b, bk):
        o, i = w("HT", b, 1024, 4), bank(bk, 256)
        either(PLAN["rq"] if bk < 4 else "s", o, i, lambda: g.vector.tensor_scalar(o[0], i[0], 0.0, 0.0625, A.max, A.mult),
               lambda: g.scalar.activation(o[0], i[0], F.Relu, scale=0.0625))

    def unpack(v, new):
        for b in range(4):
            mm(4 + b, 256, "E", (0 if new else 512) + 128 * b, "XA", 256 * (v + new), not new, bool(new))

    def version(v):
        bk = 4 if v else 0
        for b in range(4):
            mm(bk + b, 256, "W", 128 * b, "XA", 256 * v)
        if v == 0:
            with_u(0, 4)
            arow(0)
        for b in range(4):
            relu(b, bk + b)
        unpack(v, 0)
        for k in range(0, 256, 128):
            if v == 1:
                for j in range(4 * k, 4 * k + 512, 128):
                    ts(w("HT", j, j + 128), w("HT", j, j + 128), BIG, A.min)
            quant("XA", 256 * (v + 1) + k, ("HT", 4 * k), 128)
        unpack(v, 1)
        for b in range(4):
            cp("s" if v else PLAN["dq"], w("DT", b, 1024, 4), bank(4 + b, 256))
            ahead[len(calls) - 1] = PLAN["ahead%d" % v]
        for k in range(0, 256, 128):
            quant("DL", 256 * v + k, ("DT", 4 * k), 128)

    def arow(t):
        cp("vs", w("RA", 0, 64), ind(w("ACOL", 8 * t, 8 * t + 2), lst("ac", 4)))

    quant("X", 0, ("XB", 0), 256)
    quant("S", 0, ("UV", 0), 128)
    pick("XA", 0, 256, "X", 256, ("LST", LISTS["nat"]))
    lin(w("NB", 0, 520), eb, -1.0, qs=PLAN["nq"])
    for b in range(4):
        quant("E", 512 + 128 * b, ("NB", 4 - b), 128)
        quant("E", 128 * b, ("EB", 4 - b), 128)
    version(0)
    with_u(1, 0)
    version(1)
    version(2)
    load("y", w("UB", 0, 512), T.u[:, :], "late", [w("N0", OWN + 1, OWN + 8)])
    load("y", w("VB", 0, 512), T.v[:, :], "late", [w("N0", OWN + 1, OWN + 8)])
    quant("U", 0, ("UB", 0), 128)
    quant("V", 0, ("VB", 0), 128)

    def across(name, a, n, moves):
        for q, d, c in moves:
            k = 64 if d == 2 and (q ^ 1, d, c) in moves else 32
            if k == 32 or q % 2 == 0:
                f = 32 * ((q + d) % 4)
                cp("vs", w(name, c, c + n, 1, 32 * q, 32 * q + k), w(name, a, a + n, 1, f, f + k))

    def choose(t):
        n = "N%d" % t
        rb, rr, st = w("RB", 0, 64), w("RR", 0, 64), w("ST", 0, 64)
        tt(rb, ind(w(n, OWN - OWN % 8, OWN + 8), lst("bl", 4)), w("RA", 0, 64), A.subtract)
        for j, (to, frm, k) in enumerate(moves):
            cp("sv", w(n, 8 * j, 8 + 8 * j, 1, to, to + k), w(n, OWN, OWN + 8, 1, frm, frm + k))
        tt(rr, ind(w(n, 0, OWN + 8), lst("bl", 4, 4)), rb, A.add)
        tr(st, rr)
        for h in range(2):
            a, z = w("ST", 32 * h, 32 * h + 32), w("RR", 32 * h, 32 * h + 1)
            ts(w("EL", 64 * h, 64 * h + 32), a, z, A.is_equal, -1.0, A.mult)
            sign(w("EL", 64 * h + 32, 64 * h + 64), a, z)
        cx, sn, la = "CX%d" % t, "SN%d" % t, "LA%d" % t
        for h in range(2):
            scan(w(cx, PLC - 126 + h, PLC + 2, 2), w("RST", 0, 64), w("EL", 64 * h, 64 * h + 64))
        to_all(cx, PLC, 2, "ls%d" % t, PLAN["places"])
        across(cx, PLC, 2, [(q, d, PLC - 8 + 2 * d) for d in (1, 2, 3) for q in range(4)])
        rg, m, xr = w("RG", 0, 128), w("MM", 0, 128), w(cx, PLC - 6, PLC + 2)

        def transfer(kind, o, e):
            if kind == "hand":
                what, a, b = HAND[t][o]
                return ([helpers[o]], e, T.sem["hs%d" % t], _cols(T, what, sn, 8 * a, 8 * (b - a)), [_cols(T, what, "HC%d" % t, 0, 8 * (b - a))])
            return ([cores[o]], e, T.sem["dl%d" % t], _cols(T, kind, sn, 8 * order.index(o), 8), [_cols(T, kind, la, 8 + 8 * slot(me, o), 8)])

        def send():
            src = {"scale": w("z_" + sn, 0, 64), "code": w("c_" + sn, 0, 64)}
            return [fused([src[HAND[t][call[0][1]][0] if call[0][0] == "hand" else call[0][0]]], [transfer(*x) for x in call])
                    for call in _calls(t, me, cores, topo)]
        tt(rg, ind(xr, lst("rg", 8)), w("MT", 0, 128), A.not_equal)
        tr(m, rg)
        scan(w("SCN", 0, 128), m, w("DMP", 0, 128))
        cp("v", w("L", 0, 4), w("SCN", 31, 128, 32))
        pick(sn, 0, 64, "DL", 256 * (t + 1), ("L", 0))
        arrive([w("c_" + la, 16, 72), w("z_" + la, 16, 72)], "dl%d" % t, sum(delta_count(t, s) for s in others),
               send(), PLAN["deltas"] + (0 if t else PLAN["cold"]))
        pick(la, 0, 16, sn, 64, ("LST", LISTS["ow"]))

    def advance(t):
        xl, u = w("XL", 0, 8), t + 1
        ts(w("U8", 0, 8), w("CX%d" % t, PLC - 6, PLC + 2), -25.0, A.is_lt, 256.0, A.mult)
        tt(xl, xl, w("U8", 0, 8), A.add)
        if t < R - 1:
            tt(w("VM", 0, 16), ind(xl, lst("hh", 1)), w("LV", 0, 16), A.is_equal)
            tt(w("PV", 0, 8), w("VM", 0, 8), w("AV%d" % u, 0, 8), A.mult)
            rsum(w("ACOL", 8 * u, 8 * u + 1), w("PV", 0, 4))
            rsum(w("ACOL", 8 * u + 1, 8 * u + 2), w("PV", 4, 8))
            arow(u)
            cp("sv", w("MP", 0, 128), ind(xl, lst("rg", 8)))
            tr(w("MPT", 0, 128), w("MP", 0, 128))
            tt(w("DMP", 0, 127), w("MPT", 0, 127), w("MPT", 1, 128), A.subtract)
            cp("sv", w("DMP", 31, 128, 32), w("MPT", 31, 128, 32))
        else:
            tt(w("FB", 0, 32), ind(xl, lst("fo", 2)), w("EM", 0, 32), A.mult)
            tr(w("FT", 0, 32), w("FB", 0, 32))
            tt(w("FO", 0, 16), w("FT", 0, 32, 2), w("FT", 1, 32, 2), A.add)
            cp("v", w("OUT", 0, 16), w("FO", 0, 16))
            pick("FD", 0, 256, "XA", 1024, ("OUT", 0))
            mm(4, 256, "U", 0, "FD", 0)
            store("y", T.oc[:, 0:1024], as_bytes(w("c_FD", 0, 256)))
            for k in range(4):
                store("y", T.osc[4 * k:4 * k + 4, 0:256], w("z_FD", 0, 256, 1, 32 * k, 32 * k + 4))
            cp("sv", w("YB", 0, 256), w("ps", 2048, 2304))
            store("y", T.y[:, 0:256], w("YB", 0, 256))

    def patch(t):
        la, cx, pb, pn, last = "LA%d" % t, "CX%d" % t, "PB%d" % t, "PB%d" % (t + 1), t == R - 1
        across(cx, PLC, 16, [(q, d, PLC - STEP * d) for d in (1, 2, 3) for q in range(4) if q // 2 != HR or (q + d) % 4 == QB])
        tt(w("OH", 0, 32), ind(w(cx, 64, PLC + 16), lst("gx", 2)), w("MT", 0, 32), A.not_equal)
        tr(w("MK", 0, 32), w("OH", 0, 32))
        scan(w("SK", 0, 64), w("MK", 0, 64), w("DK", 0, 64))
        tr(w("KX", 32, 64), w("SK", 32, 64))
        pp, pd, p3 = col(PP), col(PD), col(P3)
        for j, (out, key) in enumerate(((pd, w("SK", 31, 32)), (pp, col(PC)), (p3, col(PC3)))):
            sign(w("GG", 64 * j, 64 * j + 64), w("KX", 0, 64), key, out)
        ts(w("HH", 128, 256), w("WT", 0, 128), pd, A.is_equal, col(VDB), A.mult)
        ts(w("HH", 0, 128), w("WT", 0, 128), pp, A.is_equal, col(VPB), A.mult)
        tr(w("HHT", 1, 256, 2), w("HH", 128, 256))
        tr(w("HHT", 0, 256, 2), w("HH", 0, 128))
        scan(w("SH", 0, 256), w("SEGH", 0, 256), w("HHT", 0, 256))
        for k in range(2):
            for h in range(2):
                cp("v", w("AL", 4 * k, 4 * k + 4, 1, 64 * h, 64 * h + 64), w("SH", 63, 256, 64, 64 * (k ^ HR), 64 * (k ^ HR) + 64))
        wide = 64 if last else 128
        ts(col(MK1), p3, pp, A.subtract, 1.0, A.is_gt)
        lin(col(SU), p3, 0.5, col(C1P))
        lin(col(SU2), col(SU), col(MK1), col(OP))
        lin(w("HH", 256, 256 + wide), w("MASK", 0, wide), col(SU2))
        tr(w("HHT", 256, 256 + wide), w("HH", 256, 256 + wide))
        scan(w("SH", 256, 256 + wide), w("SEGH", 256, 256 + wide), w("HHT", 256, 256 + wide))
        for k in range(2):
            for h in range(2):
                cp("sv", w("SX", 4 * k, 4 * k + wide // 32, 1, 64 * h, 64 * h + 64), w("SH", 287, 256 + wide, 32, 64 * (k ^ HR), 64 * (k ^ HR) + 64))
        cp("v", w("SEL", 0, 16), ind(w("SX", 0, 8), lst("sl" if last else "se", 1)))
        ms = w("MS", 0, 128)
        pick("AR", 0, 128, la, 144, ("AL", 0))
        for k in range(2):
            cp("sv", w("MS", 64 * k, 64 * k + 64), ind(w("TBL", 0, 144), w("AL", 4 * k, 4 * k + 4)))
        for b in range(4):
            mm(b, 128, "E", 128 * b, "AR", 0)
        for b in range(4):
            scan(w("NT", b, 512, 4), ms, bank(b, 128))
        quant(pb, 0, ("NT", 0), 128)
        if not last:
            pick(pn, OLD, 128, pb, 256, ("SEL", 0))
            scores(t + 1)
            if t == 0:
                with_u(2, 1)
            pick("LA%d" % (t + 1), LAP, 64, pn, 128, ("LST", LISTS["pp"]), OLD)
        else:
            pick("FD", 256, 64, pb, 256, ("SEL", 0))
            mm(0, 128, "V", 0, "FD", 192)
            store("y", T.oc[:, 1024:1280], as_bytes(w("c_FD", 256, 320)))
            for k in range(4):
                store("ys"[k % 2], T.osc[4 * k:4 * k + 4, 256:320], w("z_FD", 256, 320, 1, 32 * k, 32 * k + 4))
            cp("vs", w("YB", 256, 320), bank(0, 64, 64))
            store("s", T.y[:, 256:320], w("YB", 256, 320))

    for t in range(R):
        choose(t)
        advance(t)
        patch(t)

    csem = {"g": "qg", "v": "qv", "s": "qs", "t": "qt"}
    pre = _before(calls)
    total, known, ends, on = {"snt": sent[0]}, {q: {} for q in Q}, {}, {}
    ndma = 0
    plan = _plan(calls, ahead)
    for j, q in sorted(x for x in plan if x[0] < n_loads) + [x for x in plan if x[0] >= n_loads]:
        ways, reads, writes, what, late, after = calls[j]
        on[j] = q
        if what == "arrive":
            total[q] = ways[q][0]
            ends[j] = (q, total[q], {q: total[q]})
            continue
        need = {}
        for i, soft in pre[j].items():
            if i in ends and not (soft and on[i] == q):
                sem, n, clock = ends[i]
                if known[q].get(sem, 0) < n and need.get(sem, (0,))[0] < n:
                    need[sem] = (n, clock)
        for sem in sorted(need):
            if not any(s2 != sem and c2.get(sem, 0) >= need[sem][0] for s2, (n2, c2) in need.items()):
                Q[q].wait_ge(T.sem[sem], need[sem][0])
        for n, clock in need.values():
            for k, v in clock.items():
                known[q][k] = max(known[q].get(k, 0), v)
        if what == "send":
            ways[q][0]()
            continue
        if what == "dma":
            sem, inc = "m%d" % ndma, 16
            ndma += 1
        else:
            sem, inc = csem[q], 1
        total[sem] = total.get(sem, 0) + inc
        ways[q][0]().then_inc(T.sem[sem], inc)
        ends[j] = (sem, total[sem], dict(known[q], **{sem: total[sem]}))
    for sem in sorted(total):
        if known["g"].get(sem, 0) < total[sem]:
            g.wait_ge(T.sem[sem], total[sem])
